import numpy as np
import ml_dtypes


def mxq(x, axis, fmt="e4m3"):
    dtype, down = {"e4m3": (ml_dtypes.float8_e4m3fn, 7), "e5m2": (ml_dtypes.float8_e5m2, 14)}[fmt]
    v = np.moveaxis(np.asarray(x, np.float32).astype(ml_dtypes.bfloat16).astype(np.float64), axis, -1)
    blocks = v.reshape(v.shape[:-1] + (-1, 32))
    amax = np.abs(blocks).max(-1, keepdims=True)
    byte = np.maximum(np.where(amax > 0, np.frexp(amax)[1] - 1 + 127, 0) - down, 1)
    scale = np.exp2(byte - 127.0)
    codes = (blocks / scale).astype(np.float32).astype(dtype).astype(np.float64)
    return np.moveaxis((codes * scale).reshape(v.shape), -1, axis)


WIDE = False


def mx_kscale(k):
    if not WIDE:
        return np.ones(k)
    levels = np.array([10, -10, 5, -5, 0])
    if k % 512:
        return np.exp2(np.random.permutation(np.resize(levels, k // 32))).repeat(32)
    a = np.empty((k // 512, 16))
    for p in range(k // 512):
        a[p, :8] = np.random.permutation(np.resize(levels, 8))
        for g in range(8):
            far = levels[np.abs(levels - a[p, g]) >= 10]
            a[p, g + 8] = far[np.random.randint(len(far))]
    return np.exp2(a.ravel()).repeat(32)


def f64(x):
    return np.asarray(x).astype(np.float64)


def striped(idx):
    return np.tile(idx.reshape(-1, 16).T, (8, 1)).astype(np.uint16)


def unstriped(offs):
    return offs[:16].T.reshape(-1).astype(np.int64)


E2M1 = np.array([0.0, 0.5, 1.0, 1.5, 2.0, 3.0, 4.0, 6.0, -0.0, -0.5, -1.0, -1.5, -2.0, -3.0, -4.0, -6.0])


def pack_weight(w, fmt):
    k, n = w.shape
    w = f64(np.asarray(w, np.float32).astype(ml_dtypes.bfloat16)).reshape(k // 32, 32, n)
    amax = np.abs(w).max(1)
    if fmt == "e4m3":
        byte = np.frexp(amax)[1] - 1 + 127 - 7
    else:
        mant, ex = np.frexp(amax / 6.0)
        byte = np.where(mant > 0.5, ex, ex - 1) + 127
    byte = np.clip(np.where(amax > 0, byte, 1), 1, 254)
    scaled = (w * np.exp2(127.0 - byte)[:, None, :]).reshape(k, n).astype(np.float32)
    by_word = np.ascontiguousarray(scaled.reshape(k // 512, 128, 4, n).transpose(0, 1, 3, 2))
    if fmt == "e4m3":
        words = by_word.astype(ml_dtypes.float8_e4m3fn).view(np.uint8)
    else:
        c = by_word.astype(ml_dtypes.float4_e2m1fn).view(np.uint8) & 0xF
        words = (c[..., 0::2] | (c[..., 1::2] << 4)).reshape(k // 512, 128, 2 * n)
    return np.ascontiguousarray(words), np.ascontiguousarray(byte.astype(np.uint8).reshape(k // 512, 16, n))


def unpack_weight(words, scales, fmt):
    g, _, n = scales.shape
    words = np.ascontiguousarray(words).reshape(g, 128, n, -1)
    if fmt == "e4m3":
        vals = words.view(ml_dtypes.float8_e4m3fn).astype(np.float64)
    else:
        nib = np.empty((g, 128, n, 4), np.uint8)
        nib[..., 0::2] = words & 0xF
        nib[..., 1::2] = words >> 4
        vals = E2M1[nib]
    vals = vals * np.repeat(np.exp2(scales.astype(np.float64) - 127.0), 8, axis=1)[..., None]
    return vals.transpose(0, 1, 3, 2).reshape(g * 512, n)


def relu2(v):
    return np.maximum(v, 0.0) ** 2


K, T, E, C, F, D, H = 512, 1024, 4, 256, 8, 128, 512
N = 512


def by_expert(wq, xq, E, C):
    return np.concatenate([wq[e].T @ xq[:, e * C:(e + 1) * C] for e in range(E)], axis=1)


def setup_inputs():
    n = np.random.standard_normal
    s = mx_kscale(K)
    u = mx_kscale(H)
    slot_token = np.random.permutation(T)[:E * C]
    slots2 = np.random.permutation(T)[:F * D]
    x = pack_weight(n((K, T)) * s[:, None], "e4m3")
    w = [pack_weight(m, "e2m1") for m in n((E, K, N)) / np.sqrt(K) / s[None, :, None]]
    wa = [pack_weight(m, "e4m3") for m in n((F, K, H)) / np.sqrt(K) / s[None, :, None] * u]
    wb = [pack_weight(m, "e4m3") for m in n((F, H, N)) / np.sqrt(H) / u[None, :, None] ** 2]
    return {
        "x_words": x[0],
        "x_scales": x[1],
        "w_words": np.stack([m[0] for m in w]),
        "w_scales": np.stack([m[1] for m in w]),
        "wa_words": np.stack([m[0] for m in wa]),
        "wa_scales": np.stack([m[1] for m in wa]),
        "wb_words": np.stack([m[0] for m in wb]),
        "wb_scales": np.stack([m[1] for m in wb]),
        "gate": np.tile(np.random.uniform(0.2, 1.0, E * C), (128, 1)).astype(np.float32),
        "gate2": (np.tile(np.random.uniform(0.2, 1.0, F * D), (128, 1))).astype(np.float32),
        "offs": striped(slot_token),
        "offs2": striped(slots2),
    }


def reference(x_words, x_scales, w_words, w_scales, wa_words, wa_scales, wb_words, wb_scales, gate, gate2, offs, offs2):
    w = np.stack([unpack_weight(w_words[e], w_scales[e], "e2m1") for e in range(E)])
    wa = np.stack([unpack_weight(wa_words[e], wa_scales[e], "e4m3") for e in range(F)])
    wb = np.stack([unpack_weight(wb_words[e], wb_scales[e], "e4m3") for e in range(F)])
    idx, idx2 = unstriped(offs), unstriped(offs2)
    x = unpack_weight(x_words, x_scales, "e4m3")
    y = by_expert(w, x[:, idx], E, C)
    h = relu2(by_expert(wa, x[:, idx2], F, D))
    z = by_expert(wb, mxq(h, 0, "e4m3"), F, D)
    out = np.zeros((N, T))
    out[:, idx] = f64(gate[:1]) * y
    out[:, idx2] += f64(gate2[:1]) * z
    return out

@@ -1,0 +1,206 @@
+from contextlib import ExitStack
+
+import concourse.mybir as mybir
+from concourse.masks import make_identity
+
+K, T, E, C, F, D, H, N = 512, 1024, 4, 256, 8, 128, 512, 512
+FLOPS = 2 * K * N * E * C + 2 * K * H * F * D + 2 * H * N * F * D
+
+F32 = mybir.dt.float32
+BF16 = mybir.dt.bfloat16
+I32 = mybir.dt.int32
+U32 = mybir.dt.uint32
+U16 = mybir.dt.uint16
+U8 = mybir.dt.uint8
+FP8X4 = mybir.dt.float8_e4m3fn_x4
+FP4X4 = mybir.dt.float4_e2m1fn_x4
+ACT = mybir.ActivationFunctionType
+ALU = mybir.AluOpType
+
+P = 128
+BANK = 512
+TILES = N // P
+WINDOW = 1408
+
+
+def tile_moe_mlr_relu2_kernel(
+    tc, x_words, x_scales, w_words, w_scales, wa_words, wa_scales, wb_words, wb_scales, gate, gate2, offs, offs2, out
+):
+    nc = tc.nc
+    with ExitStack() as ctx:
+        keep = ctx.enter_context(tc.tile_pool(name="keep", bufs=1))
+        ring = ctx.enter_context(tc.tile_pool(name="ring", bufs=3))
+        mm = ctx.enter_context(tc.psum_pool(name="mm", bufs=4))
+        tr = ctx.enter_context(tc.psum_pool(name="tr", bufs=4))
+
+        list1 = keep.tile([P, T // 16], U16, name="list1")
+        list2 = keep.tile([P, T // 16], U16, name="list2")
+        xw = keep.tile([P, T], I32, name="xw", align_bytes=64)
+        xs = keep.tile([P, T], U8, name="xs", align_bytes=64)
+        ww = keep.tile([P, E, 2 * N], U8, name="ww", align_bytes=64)
+        ws = keep.tile([P, E, N], U8, name="ws", align_bytes=64)
+        aw = [keep.tile([P, 2, H], I32, name="aw%d" % i, align_bytes=64) for i in range(F // 2)]
+        bw = [keep.tile([P, 4, N], I32, name="bw%d" % i, align_bytes=64) for i in range(F // 4)]
+        a_s = keep.tile([P, F, H], U8, name="a_s", align_bytes=64)
+        b_s = keep.tile([P, F, N], U8, name="b_s", align_bytes=64)
+        g1 = keep.tile([P, T], F32, name="g1")
+        g2rows = keep.tile([P, P], F32, name="g2rows")
+        g2 = keep.tile([P, F], F32, name="g2")
+        ident = keep.tile([P, P], F32, name="ident")
+
+        def flat32(t):
+            return t[:].rearrange("p e n -> p (e n)").bitcast(I32)
+
+        def load_planes(queue, plane, scales):
+            for q in range(4):
+                queue.dma_start(
+                    out=plane[32 * q : 32 * q + 4, :, :].bitcast(I32),
+                    in_=scales[:, 0, 4 * q : 4 * q + 4, :].rearrange("e r n -> r e n").bitcast(I32),
+                )
+
+        def load_words(tile, words, f0, f1):
+            nc.sync.dma_start(out=tile[:], in_=words[f0:f1, 0].rearrange("f p n d -> p f (n d)").bitcast(I32))
+
+        nc.vector.memset(xs[:].bitcast(I32), 0)
+        nc.vector.memset(flat32(ws), 0)
+        nc.vector.memset(flat32(a_s), 0)
+        nc.vector.memset(flat32(b_s), 0)
+
+        nc.sync.dma_start(list1[:], offs)
+        for q in range(4):
+            nc.sync.dma_start(
+                out=xs[32 * q : 32 * q + 4, :].bitcast(I32), in_=x_scales[0, 4 * q : 4 * q + 4, :].bitcast(I32)
+            )
+        nc.sync.dma_start(out=xw[:], in_=x_words[0].rearrange("p t d -> p (t d)").bitcast(I32))
+        nc.sync.dma_start(list2[:], offs2)
+        load_planes(nc.sync, ws, w_scales)
+        nc.sync.dma_start(out=ww[:].bitcast(I32), in_=w_words[:, 0].rearrange("e p b -> p e b").bitcast(I32))
+        load_planes(nc.sync, a_s, wa_scales)
+        for i in range(F // 2):
+            load_words(aw[i], wa_words, 2 * i, 2 * i + 2)
+            if i == 0:
+                nc.sync.dma_start(out=g1[:], in_=gate)
+        nc.sync.dma_start(out=g2rows[:], in_=gate2[0 : P // F, :].rearrange("r (f s) -> (r f) s", f=F))
+        load_planes(nc.sync, b_s, wb_scales)
+        for i in range(F // 4):
+            load_words(bw[i], wb_words, 4 * i, 4 * i + 4)
+
+        make_identity(nc, ident[:])
+
+        def gather(name, offsets, half):
+            words = keep.tile([P, BANK], U32, name="gw_%s%d" % (name, half), align_bytes=64)
+            scales = keep.tile([P, BANK], U8, name="gs_%s%d" % (name, half), align_bytes=64)
+            piece = offsets[:, 32 * half : 32 * half + 32]
+            nc.vector.tensor_copy(scales[:], xs[:].indirect(piece))
+            nc.vector.tensor_copy(words[:], xw[:].bitcast(U32).indirect(piece))
+            return words, scales
+
+        xe = [gather("e", list1, half) for half in range(2)]
+        xa = [gather("a", list2, half) for half in range(2)]
+
+        ys = [keep.tile([P, T], F32, name="ys%d" % j) for j in range(TILES)]
+        for j in range(TILES):
+            for half in range(2):
+                acc = mm.tile([P, BANK], F32, name="acc")
+                words, scales = xe[half]
+                for u in range(2):
+                    e = 2 * half + u
+                    cols = slice(u * C, (u + 1) * C)
+                    nc.tensor.matmul_mx(
+                        out=acc[:, cols],
+                        lhsT=ww[:, e, 2 * P * j : 2 * P * (j + 1)].bitcast(FP4X4),
+                        lhsT_scale=ws[:, e, P * j : P * (j + 1)],
+                        rhs=words[:, cols].bitcast(FP8X4),
+                        rhs_scale=scales[:, cols],
+                        start=True,
+                        stop=True,
+                    )
+                nc.scalar.copy(out=ys[j][:, BANK * half : BANK * (half + 1)], in_=acc[:])
+
+        hb = [keep.tile([P, BANK, 4], BF16, name="hb%d" % half, align_bytes=64) for half in range(2)]
+        for f in range(F):
+            half, u = divmod(f, 4)
+            words, scales = xa[half]
+            cols = slice(u * D, (u + 1) * D)
+            acc = mm.tile([P, BANK], F32, name="acc")
+            nc.tensor.matmul_mx(
+                out=acc[:],
+                lhsT=words[:, cols].bitcast(FP8X4),
+                lhsT_scale=scales[:, cols],
+                rhs=aw[f // 2][:, f % 2, :].bitcast(FP8X4),
+                rhs_scale=a_s[:, f, :],
+                start=True,
+                stop=True,
+            )
+            pos = ring.tile([P, 4, P], F32, name="pos")
+            nc.scalar.activation(out=pos[:], in_=acc[:].rearrange("p (m t) -> p t m", t=4), func=ACT.Relu)
+            turned = tr.tile([P, 4, P], F32, name="turned")
+            for t in range(4):
+                nc.tensor.transpose(turned[:, t, :], pos[:, t, :], ident[:])
+            nc.scalar.activation(
+                out=hb[half][:, cols, :], in_=turned[:].rearrange("p t s -> p s t"), func=ACT.Square
+            )
+
+        oy = [keep.tile([P, WINDOW], F32, name="oy%d" % j) for j in range(TILES)]
+        oz = [keep.tile([P, WINDOW], F32, name="oz%d" % j) for j in range(TILES)]
+        hw = [keep.tile([P, BANK], U32, name="hw%d" % half, align_bytes=64) for half in range(2)]
+        hs = [keep.tile([P, BANK], U8, name="hs%d" % half, align_bytes=64) for half in range(2)]
+        for j in range(TILES):
+            nc.vector.tensor_tensor(oy[j][:].indirect(list1[:]), ys[j][:], g1[:], ALU.mult)
+            if j in (1, 2):
+                half = j - 1
+                nc.vector.quantize_mx(
+                    out=hw[half][:].bitcast(FP8X4), scales=hs[half][:], in_=hb[half][:].rearrange("p s t -> p (s t)")
+                )
+
+        g2turned = tr.tile([P, 4, P], F32, name="turned")
+        nc.tensor.transpose(g2turned[:, 0, :], g2rows[:], ident[:])
+        nc.scalar.copy(out=g2[:], in_=g2turned[:, 0, 0:F])
+
+        zs = keep.tile([P, TILES, T], F32, name="zs")
+        for f in range(F):
+            half, u = divmod(f, 4)
+            cols = slice(u * D, (u + 1) * D)
+            acc = mm.tile([P, BANK], F32, name="acc")
+            nc.tensor.matmul_mx(
+                out=acc[:],
+                lhsT=hw[half][:, cols].bitcast(FP8X4),
+                lhsT_scale=hs[half][:, cols],
+                rhs=bw[half][:, u, :].bitcast(FP8X4),
+                rhs_scale=b_s[:, f, :],
+                start=True,
+                stop=True,
+            )
+            gated = ring.tile([P, TILES, P], F32, name="gated")
+            nc.scalar.activation(
+                out=gated[:].rearrange("p j n -> p (j n)"), in_=acc[:], func=ACT.Copy, scale=g2[:, f : f + 1]
+            )
+            turned = tr.tile([P, 4, P], F32, name="turned")
+            for j in range(TILES):
+                nc.tensor.transpose(turned[:, j, :], gated[:, j, :], ident[:])
+            nc.scalar.copy(out=zs[:, :, D * f : D * (f + 1)], in_=turned[:])
+
+        for j in range(TILES):
+            rows = slice(P * j, P * (j + 1))
+            nc.vector.tensor_copy(oz[j][:].indirect(list2[:]), zs[:, j, :])
+            if j < TILES - 1:
+                for half in range(2):
+                    total = tr.tile([P, 4, P], F32, name="turned")
+                    for b in range(4):
+                        cols = slice(BANK * half + P * b, BANK * half + P * (b + 1))
+                        nc.tensor.matmul(total[:, b, :], oy[j][:, cols], ident[:], start=True, stop=False, is_transpose=True)
+                        nc.tensor.matmul(total[:, b, :], oz[j][:, cols], ident[:], start=False, stop=True, is_transpose=True)
+                    by_token = ring.tile([P, 4, P], F32, name="by_token")
+                    nc.scalar.copy(out=by_token[:], in_=total[:])
+                    back = tr.tile([P, 4, P], F32, name="turned")
+                    for b in range(4):
+                        nc.tensor.transpose(back[:, b, :], by_token[:, b, :], ident[:])
+                    res = ring.tile([P, BANK], F32, name="res")
+                    nc.scalar.copy(out=res[:], in_=back[:].rearrange("p b t -> p (b t)"))
+                    nc.scalar.dma_start(out=out[rows, BANK * half : BANK * (half + 1)], in_=res[:])
+            else:
+                for quarter in range(4):
+                    cols = slice(256 * quarter, 256 * (quarter + 1))
+                    last = keep.tile([P, 256], F32, name="last%d" % quarter)
+                    nc.vector.tensor_tensor(last[:], oy[j][:, cols], oz[j][:, cols], ALU.add)
+                    nc.sync.dma_start(out=out[rows, cols], in_=last[:])

@@ -41,11 +41,10 @@ def tile_moe_mlr_relu2_kernel(
         ws = keep.tile([P, E, N], U8, name="ws", align_bytes=64)
         aw = [keep.tile([P, 2, H], I32, name="aw%d" % i, align_bytes=64) for i in range(F // 2)]
         bw = [keep.tile([P, 4, N], I32, name="bw%d" % i, align_bytes=64) for i in range(F // 4)]
-        a_s = keep.tile([P, F, H], U8, name="a_s", align_bytes=64)
-        b_s = keep.tile([P, F, N], U8, name="b_s", align_bytes=64)
+        a_s = keep.tile([P, 2, H], U8, name="a_s", align_bytes=64)
+        b_s = keep.tile([P, 2, N], U8, name="b_s", align_bytes=64)
         g1 = keep.tile([P, T], F32, name="g1")
-        g2rows = keep.tile([P, P], F32, name="g2rows")
-        g2 = keep.tile([P, F], F32, name="g2")
+        g2 = keep.tile([P, T], F32, name="g2")
         ident = keep.tile([P, P], F32, name="ident")
 
         def flat32(t):
@@ -57,6 +56,14 @@ def tile_moe_mlr_relu2_kernel(
                     out=plane[32 * q : 32 * q + 4, :, :].bitcast(I32),
                     in_=scales[:, 0, 4 * q : 4 * q + 4, :].rearrange("e r n -> r e n").bitcast(I32),
                 )
+
+        def load_packed_planes(plane, scales):
+            for half in range(2):
+                for q in range(4):
+                    nc.sync.dma_start(
+                        out=plane[32 * q : 32 * q + 16, half, :].bitcast(I32),
+                        in_=scales[4 * half : 4 * half + 4, 0, 4 * q : 4 * q + 4, :].bitcast(I32),
+                    )
 
         def load_words(tile, words, f0, f1):
             nc.sync.dma_start(out=tile[:], in_=words[f0:f1, 0].rearrange("f p n d -> p f (n d)").bitcast(I32))
@@ -75,15 +82,15 @@ def tile_moe_mlr_relu2_kernel(
         nc.sync.dma_start(list2[:], offs2)
         load_planes(nc.sync, ws, w_scales)
         nc.sync.dma_start(out=ww[:].bitcast(I32), in_=w_words[:, 0].rearrange("e p b -> p e b").bitcast(I32))
-        load_planes(nc.sync, a_s, wa_scales)
+        load_packed_planes(a_s, wa_scales)
         for i in range(F // 2):
             load_words(aw[i], wa_words, 2 * i, 2 * i + 2)
             if i == 0:
                 nc.sync.dma_start(out=g1[:], in_=gate)
-        nc.sync.dma_start(out=g2rows[:], in_=gate2[0 : P // F, :].rearrange("r (f s) -> (r f) s", f=F))
-        load_planes(nc.sync, b_s, wb_scales)
+        load_packed_planes(b_s, wb_scales)
         for i in range(F // 4):
             load_words(bw[i], wb_words, 4 * i, 4 * i + 4)
+        nc.sync.dma_start(out=g2[:], in_=gate2)
 
         make_identity(nc, ident[:])
 
@@ -98,8 +105,9 @@ def tile_moe_mlr_relu2_kernel(
         xe = [gather("e", list1, half) for half in range(2)]
         xa = [gather("a", list2, half) for half in range(2)]
 
-        ys = [keep.tile([P, T], F32, name="ys%d" % j) for j in range(TILES)]
-        for j in range(TILES):
+        ys = [keep.tile([P, T], F32, name="ys%d" % j, tag="ys%d" % j, align_bytes=64) for j in range(TILES)]
+
+        def experts(j):
             for half in range(2):
                 acc = mm.tile([P, BANK], F32, name="acc")
                 words, scales = xe[half]
@@ -117,8 +125,9 @@ def tile_moe_mlr_relu2_kernel(
                     )
                 nc.scalar.copy(out=ys[j][:, BANK * half : BANK * (half + 1)], in_=acc[:])
 
-        hb = [keep.tile([P, BANK, 4], BF16, name="hb%d" % half, align_bytes=64) for half in range(2)]
-        for f in range(F):
+        hb = keep.tile([P, T, 4], BF16, name="hb", tag="hb_then_oy", align_bytes=64)
+
+        def first_layer(f):
             half, u = divmod(f, 4)
             words, scales = xa[half]
             cols = slice(u * D, (u + 1) * D)
@@ -128,7 +137,7 @@ def tile_moe_mlr_relu2_kernel(
                 lhsT=words[:, cols].bitcast(FP8X4),
                 lhsT_scale=scales[:, cols],
                 rhs=aw[f // 2][:, f % 2, :].bitcast(FP8X4),
-                rhs_scale=a_s[:, f, :],
+                rhs_scale=a_s[4 * u :, half, :],
                 start=True,
                 stop=True,
             )
@@ -138,69 +147,76 @@ def tile_moe_mlr_relu2_kernel(
             for t in range(4):
                 nc.tensor.transpose(turned[:, t, :], pos[:, t, :], ident[:])
             nc.scalar.activation(
-                out=hb[half][:, cols, :], in_=turned[:].rearrange("p t s -> p s t"), func=ACT.Square
+                out=hb[:, D * f : D * (f + 1), :], in_=turned[:].rearrange("p t s -> p s t"), func=ACT.Square
             )
 
-        oy = [keep.tile([P, WINDOW], F32, name="oy%d" % j) for j in range(TILES)]
-        oz = [keep.tile([P, WINDOW], F32, name="oz%d" % j) for j in range(TILES)]
-        hw = [keep.tile([P, BANK], U32, name="hw%d" % half, align_bytes=64) for half in range(2)]
-        hs = [keep.tile([P, BANK], U8, name="hs%d" % half, align_bytes=64) for half in range(2)]
-        for j in range(TILES):
-            nc.vector.tensor_tensor(oy[j][:].indirect(list1[:]), ys[j][:], g1[:], ALU.mult)
-            if j in (1, 2):
-                half = j - 1
-                nc.vector.quantize_mx(
-                    out=hw[half][:].bitcast(FP8X4), scales=hs[half][:], in_=hb[half][:].rearrange("p s t -> p (s t)")
-                )
+        experts(0)
+        for f in range(F // 2):
+            first_layer(f)
+        experts(1)
+        for f in range(F // 2, F):
+            first_layer(f)
+        experts(2)
 
-        g2turned = tr.tile([P, 4, P], F32, name="turned")
-        nc.tensor.transpose(g2turned[:, 0, :], g2rows[:], ident[:])
-        nc.scalar.copy(out=g2[:], in_=g2turned[:, 0, 0:F])
+        hw = keep.tile([P, T], U32, name="hw", align_bytes=64)
+        hs = keep.tile([P, T], U8, name="hs", align_bytes=64)
 
-        zs = keep.tile([P, TILES, T], F32, name="zs")
-        for f in range(F):
-            half, u = divmod(f, 4)
-            cols = slice(u * D, (u + 1) * D)
-            acc = mm.tile([P, BANK], F32, name="acc")
-            nc.tensor.matmul_mx(
-                out=acc[:],
-                lhsT=hw[half][:, cols].bitcast(FP8X4),
-                lhsT_scale=hs[half][:, cols],
-                rhs=bw[half][:, u, :].bitcast(FP8X4),
-                rhs_scale=b_s[:, f, :],
-                start=True,
-                stop=True,
-            )
-            gated = ring.tile([P, TILES, P], F32, name="gated")
-            nc.scalar.activation(
-                out=gated[:].rearrange("p j n -> p (j n)"), in_=acc[:], func=ACT.Copy, scale=g2[:, f : f + 1]
-            )
-            turned = tr.tile([P, 4, P], F32, name="turned")
-            for j in range(TILES):
-                nc.tensor.transpose(turned[:, j, :], gated[:, j, :], ident[:])
-            nc.scalar.copy(out=zs[:, :, D * f : D * (f + 1)], in_=turned[:])
+        def second_layer(j, zs):
+            for half in range(2):
+                acc = mm.tile([P, BANK], F32, name="acc")
+                for u in range(4):
+                    f = 4 * half + u
+                    nc.tensor.matmul_mx(
+                        out=acc[:, u * D : (u + 1) * D],
+                        lhsT=bw[half][:, u, P * j : P * (j + 1)].bitcast(FP8X4),
+                        lhsT_scale=b_s[4 * u :, half, P * j : P * (j + 1)],
+                        rhs=hw[:, D * f : D * (f + 1)].bitcast(FP8X4),
+                        rhs_scale=hs[:, D * f : D * (f + 1)],
+                        start=True,
+                        stop=True,
+                    )
+                nc.scalar.copy(out=zs[:, BANK * half : BANK * (half + 1)], in_=acc[:])
 
-        for j in range(TILES):
+        def scatter(name, tag, offsets, values, weights):
+            window = keep.tile([P, WINDOW], F32, name=name, tag=tag, align_bytes=64)
+            nc.vector.tensor_tensor(window[:].indirect(offsets[:]), values[:], weights[:], ALU.mult)
+            return window
+
+        def add_on_tensor(j, oy, oz):
             rows = slice(P * j, P * (j + 1))
-            nc.vector.tensor_copy(oz[j][:].indirect(list2[:]), zs[:, j, :])
-            if j < TILES - 1:
-                for half in range(2):
-                    total = tr.tile([P, 4, P], F32, name="turned")
-                    for b in range(4):
-                        cols = slice(BANK * half + P * b, BANK * half + P * (b + 1))
-                        nc.tensor.matmul(total[:, b, :], oy[j][:, cols], ident[:], start=True, stop=False, is_transpose=True)
-                        nc.tensor.matmul(total[:, b, :], oz[j][:, cols], ident[:], start=False, stop=True, is_transpose=True)
-                    by_token = ring.tile([P, 4, P], F32, name="by_token")
-                    nc.scalar.copy(out=by_token[:], in_=total[:])
-                    back = tr.tile([P, 4, P], F32, name="turned")
-                    for b in range(4):
-                        nc.tensor.transpose(back[:, b, :], by_token[:, b, :], ident[:])
-                    res = ring.tile([P, BANK], F32, name="res")
-                    nc.scalar.copy(out=res[:], in_=back[:].rearrange("p b t -> p (b t)"))
-                    nc.scalar.dma_start(out=out[rows, BANK * half : BANK * (half + 1)], in_=res[:])
-            else:
-                for quarter in range(4):
-                    cols = slice(256 * quarter, 256 * (quarter + 1))
-                    last = keep.tile([P, 256], F32, name="last%d" % quarter)
-                    nc.vector.tensor_tensor(last[:], oy[j][:, cols], oz[j][:, cols], ALU.add)
-                    nc.sync.dma_start(out=out[rows, cols], in_=last[:])
+            by_token = []
+            for half in range(2):
+                total = tr.tile([P, 4, P], F32, name="turned")
+                for b in range(4):
+                    cols = slice(BANK * half + P * b, BANK * half + P * (b + 1))
+                    nc.tensor.matmul(total[:, b, :], oy[:, cols], ident[:], start=True, stop=False, is_transpose=True)
+                    nc.tensor.matmul(total[:, b, :], oz[:, cols], ident[:], start=False, stop=True, is_transpose=True)
+                by_token.append(ring.tile([P, 4, P], F32, name="by_token"))
+                nc.scalar.copy(out=by_token[half][:], in_=total[:])
+            for half in range(2):
+                back = tr.tile([P, 4, P], F32, name="turned")
+                for b in range(4):
+                    nc.tensor.transpose(back[:, b, :], by_token[half][:, b, :], ident[:])
+                res = ring.tile([P, BANK], F32, name="res")
+                nc.scalar.copy(out=res[:], in_=back[:].rearrange("p b t -> p (b t)"))
+                nc.scalar.dma_start(out=out[rows, BANK * half : BANK * (half + 1)], in_=res[:])
+
+        oy = [scatter("oy%d" % j, "oy%d" % j, list1, ys[j], g1) for j in range(2)]
+        nc.vector.quantize_mx(out=hw[:].bitcast(FP8X4), scales=hs[:], in_=hb[:].rearrange("p s t -> p (s t)"))
+        oy.append(scatter("oy2", "hb_then_oy", list1, ys[2], g1))
+        zs = [keep.tile([P, T], F32, name="zs%d" % j, tag="zs%d" % j, align_bytes=64) for j in range(TILES)]
+        for j in range(TILES):
+            second_layer(j, zs[j])
+        experts(3)
+        for j in range(TILES - 1):
+            oz = scatter("oz%d" % j, "oz%d" % j, list2, zs[j], g2)
+            add_on_tensor(j, oy[j], oz)
+        j = TILES - 1
+        oy_last = scatter("oy3", "zs2", list1, ys[j], g1)
+        oz_last = scatter("oz3", "oz3", list2, zs[j], g2)
+        rows = slice(P * j, P * (j + 1))
+        for quarter in range(4):
+            cols = slice(256 * quarter, 256 * (quarter + 1))
+            last = keep.tile([P, 256], F32, name="last%d" % quarter)
+            nc.vector.tensor_tensor(last[:], oy_last[:, cols], oz_last[:, cols], ALU.add)
+            nc.sync.dma_start(out=out[rows, cols], in_=last[:])

@@ -68,7 +68,7 @@ def tile_moe_mlr_relu2_kernel(
         def load_words(tile, words, f0, f1):
             nc.sync.dma_start(out=tile[:], in_=words[f0:f1, 0].rearrange("f p n d -> p f (n d)").bitcast(I32))
 
-        nc.vector.memset(xs[:].bitcast(I32), 0)
+        nc.gpsimd.memset(xs[:].bitcast(I32), 0)
         nc.vector.memset(flat32(ws), 0)
         nc.vector.memset(flat32(a_s), 0)
         nc.vector.memset(flat32(b_s), 0)
@@ -78,7 +78,7 @@ def tile_moe_mlr_relu2_kernel(
             nc.sync.dma_start(
                 out=xs[32 * q : 32 * q + 4, :].bitcast(I32), in_=x_scales[0, 4 * q : 4 * q + 4, :].bitcast(I32)
             )
-        nc.sync.dma_start(out=xw[:], in_=x_words[0].rearrange("p t d -> p (t d)").bitcast(I32))
+        nc.scalar.dma_start(out=xw[:], in_=x_words[0].rearrange("p t d -> p (t d)").bitcast(I32))
         nc.sync.dma_start(list2[:], offs2)
         load_planes(nc.sync, ws, w_scales)
         nc.sync.dma_start(out=ww[:].bitcast(I32), in_=w_words[:, 0].rearrange("e p b -> p e b").bitcast(I32))
@@ -105,9 +105,10 @@ def tile_moe_mlr_relu2_kernel(
         xe = [gather("e", list1, half) for half in range(2)]
         xa = [gather("a", list2, half) for half in range(2)]
 
-        ys = [keep.tile([P, T], F32, name="ys%d" % j, tag="ys%d" % j, align_bytes=64) for j in range(TILES)]
+        ys = []
 
         def experts(j):
+            ys.append(keep.tile([P, T], F32, name="ys%d" % j, tag="ys%d" % j))
             for half in range(2):
                 acc = mm.tile([P, BANK], F32, name="acc")
                 words, scales = xe[half]
@@ -125,7 +126,7 @@ def tile_moe_mlr_relu2_kernel(
                     )
                 nc.scalar.copy(out=ys[j][:, BANK * half : BANK * (half + 1)], in_=acc[:])
 
-        hb = keep.tile([P, T, 4], BF16, name="hb", tag="hb_then_oy", align_bytes=64)
+        hb = keep.tile([P, T, 4], BF16, name="hb", align_bytes=64)
 
         def first_layer(f):
             half, u = divmod(f, 4)
@@ -141,7 +142,10 @@ def tile_moe_mlr_relu2_kernel(
                 start=True,
                 stop=True,
             )
-            pos = ring.tile([P, 4, P], F32, name="pos")
+            if f < F - 1:
+                pos = ring.tile([P, 4, P], F32, name="pos")
+            else:
+                pos = keep.tile([P, 4, P], F32, name="pos_last", tag="ys2")
             nc.scalar.activation(out=pos[:], in_=acc[:].rearrange("p (m t) -> p t m", t=4), func=ACT.Relu)
             turned = tr.tile([P, 4, P], F32, name="turned")
             for t in range(4):
@@ -193,17 +197,17 @@ def tile_moe_mlr_relu2_kernel(
                     nc.tensor.matmul(total[:, b, :], oz[:, cols], ident[:], start=False, stop=True, is_transpose=True)
                 by_token.append(ring.tile([P, 4, P], F32, name="by_token"))
                 nc.scalar.copy(out=by_token[half][:], in_=total[:])
+            res = ring.tile([P, T], F32, name="res")
             for half in range(2):
                 back = tr.tile([P, 4, P], F32, name="turned")
                 for b in range(4):
                     nc.tensor.transpose(back[:, b, :], by_token[half][:, b, :], ident[:])
-                res = ring.tile([P, BANK], F32, name="res")
-                nc.scalar.copy(out=res[:], in_=back[:].rearrange("p b t -> p (b t)"))
-                nc.scalar.dma_start(out=out[rows, BANK * half : BANK * (half + 1)], in_=res[:])
+                nc.scalar.copy(out=res[:, BANK * half : BANK * (half + 1)], in_=back[:].rearrange("p b t -> p (b t)"))
+            nc.scalar.dma_start(out=out[rows, :], in_=res[:])
 
         oy = [scatter("oy%d" % j, "oy%d" % j, list1, ys[j], g1) for j in range(2)]
         nc.vector.quantize_mx(out=hw[:].bitcast(FP8X4), scales=hs[:], in_=hb[:].rearrange("p s t -> p (s t)"))
-        oy.append(scatter("oy2", "hb_then_oy", list1, ys[2], g1))
+        oy.append(scatter("oy2", "oy2", list1, ys[2], g1))
         zs = [keep.tile([P, T], F32, name="zs%d" % j, tag="zs%d" % j, align_bytes=64) for j in range(TILES)]
         for j in range(TILES):
             second_layer(j, zs[j])

@@ -68,7 +68,7 @@ def tile_moe_mlr_relu2_kernel(
         def load_words(tile, words, f0, f1):
             nc.sync.dma_start(out=tile[:], in_=words[f0:f1, 0].rearrange("f p n d -> p f (n d)").bitcast(I32))
 
-        nc.gpsimd.memset(xs[:].bitcast(I32), 0)
+        nc.vector.memset(xs[:].bitcast(I32), 0)
         nc.vector.memset(flat32(ws), 0)
         nc.vector.memset(flat32(a_s), 0)
         nc.vector.memset(flat32(b_s), 0)
@@ -78,7 +78,7 @@ def tile_moe_mlr_relu2_kernel(
             nc.sync.dma_start(
                 out=xs[32 * q : 32 * q + 4, :].bitcast(I32), in_=x_scales[0, 4 * q : 4 * q + 4, :].bitcast(I32)
             )
-        nc.scalar.dma_start(out=xw[:], in_=x_words[0].rearrange("p t d -> p (t d)").bitcast(I32))
+        nc.sync.dma_start(out=xw[:], in_=x_words[0].rearrange("p t d -> p (t d)").bitcast(I32))
         nc.sync.dma_start(list2[:], offs2)
         load_planes(nc.sync, ws, w_scales)
         nc.sync.dma_start(out=ww[:].bitcast(I32), in_=w_words[:, 0].rearrange("e p b -> p e b").bitcast(I32))
@@ -94,16 +94,19 @@ def tile_moe_mlr_relu2_kernel(
 
         make_identity(nc, ident[:])
 
-        def gather(name, offsets, half):
-            words = keep.tile([P, BANK], U32, name="gw_%s%d" % (name, half), align_bytes=64)
-            scales = keep.tile([P, BANK], U8, name="gs_%s%d" % (name, half), align_bytes=64)
-            piece = offsets[:, 32 * half : 32 * half + 32]
-            nc.vector.tensor_copy(scales[:], xs[:].indirect(piece))
-            nc.vector.tensor_copy(words[:], xw[:].bitcast(U32).indirect(piece))
-            return words, scales
+        def gather(name, window, dtype, offsets, half):
+            picked = keep.tile([P, BANK], dtype, name="%s%d" % (name, half), align_bytes=64)
+            nc.vector.tensor_copy(picked[:], window.indirect(offsets[:, 32 * half : 32 * half + 32]))
+            return picked
 
-        xe = [gather("e", list1, half) for half in range(2)]
-        xa = [gather("a", list2, half) for half in range(2)]
+        x_scale_window, x_word_window = xs[:], xw[:].bitcast(U32)
+        e_scales = [gather("gs_e", x_scale_window, U8, list1, half) for half in range(2)]
+        e_words = [gather("gw_e", x_word_window, U32, list1, half) for half in range(2)]
+        xe = list(zip(e_words, e_scales))
+        xa = []
+        for half in range(2):
+            scales = gather("gs_a", x_scale_window, U8, list2, half)
+            xa.append((gather("gw_a", x_word_window, U32, list2, half), scales))
 
         ys = []
 

@@ -35,8 +35,8 @@ def tile_moe_mlr_relu2_kernel(
 
         list1 = keep.tile([P, T // 16], U16, name="list1")
         list2 = keep.tile([P, T // 16], U16, name="list2")
-        xw = keep.tile([P, T], I32, name="xw", align_bytes=64)
-        xs = keep.tile([P, T], U8, name="xs", align_bytes=64)
+        xw = keep.tile([P, WINDOW], I32, name="xw", align_bytes=64)
+        xs = keep.tile([P, WINDOW], U8, name="xs", align_bytes=64)
         ww = keep.tile([P, E, 2 * N], U8, name="ww", align_bytes=64)
         ws = keep.tile([P, E, N], U8, name="ws", align_bytes=64)
         aw = [keep.tile([P, 2, H], I32, name="aw%d" % i, align_bytes=64) for i in range(F // 2)]
@@ -68,7 +68,6 @@ def tile_moe_mlr_relu2_kernel(
         def load_words(tile, words, f0, f1):
             nc.sync.dma_start(out=tile[:], in_=words[f0:f1, 0].rearrange("f p n d -> p f (n d)").bitcast(I32))
 
-        nc.vector.memset(xs[:].bitcast(I32), 0)
         nc.vector.memset(flat32(ws), 0)
         nc.vector.memset(flat32(a_s), 0)
         nc.vector.memset(flat32(b_s), 0)
@@ -76,17 +75,17 @@ def tile_moe_mlr_relu2_kernel(
         nc.sync.dma_start(list1[:], offs)
         for q in range(4):
             nc.sync.dma_start(
-                out=xs[32 * q : 32 * q + 4, :].bitcast(I32), in_=x_scales[0, 4 * q : 4 * q + 4, :].bitcast(I32)
+                out=xs[32 * q : 32 * q + 32, :T].bitcast(I32),
+                in_=x_scales[0, 4 * q : 4 * q + 4, :].bitcast(I32).unsqueeze(0).broadcast_to([8, 4, T // 4]),
             )
-        nc.sync.dma_start(out=xw[:], in_=x_words[0].rearrange("p t d -> p (t d)").bitcast(I32))
+        nc.sync.dma_start(out=xw[:, :T], in_=x_words[0].rearrange("p t d -> p (t d)").bitcast(I32))
         nc.sync.dma_start(list2[:], offs2)
-        load_planes(nc.sync, ws, w_scales)
         nc.sync.dma_start(out=ww[:].bitcast(I32), in_=w_words[:, 0].rearrange("e p b -> p e b").bitcast(I32))
+        load_planes(nc.sync, ws, w_scales)
+        nc.sync.dma_start(out=g1[:], in_=gate)
         load_packed_planes(a_s, wa_scales)
         for i in range(F // 2):
             load_words(aw[i], wa_words, 2 * i, 2 * i + 2)
-            if i == 0:
-                nc.sync.dma_start(out=g1[:], in_=gate)
         load_packed_planes(b_s, wb_scales)
         for i in range(F // 4):
             load_words(bw[i], wb_words, 4 * i, 4 * i + 4)
@@ -94,19 +93,16 @@ def tile_moe_mlr_relu2_kernel(
 
         make_identity(nc, ident[:])
 
-        def gather(name, window, dtype, offsets, half):
-            picked = keep.tile([P, BANK], dtype, name="%s%d" % (name, half), align_bytes=64)
-            nc.vector.tensor_copy(picked[:], window.indirect(offsets[:, 32 * half : 32 * half + 32]))
+        def gather(name, window, dtype, offsets):
+            picked = keep.tile([P, T], dtype, name=name, align_bytes=64)
+            nc.vector.tensor_copy(picked[:], window.indirect(offsets[:]))
             return picked
 
         x_scale_window, x_word_window = xs[:], xw[:].bitcast(U32)
-        e_scales = [gather("gs_e", x_scale_window, U8, list1, half) for half in range(2)]
-        e_words = [gather("gw_e", x_word_window, U32, list1, half) for half in range(2)]
-        xe = list(zip(e_words, e_scales))
-        xa = []
-        for half in range(2):
-            scales = gather("gs_a", x_scale_window, U8, list2, half)
-            xa.append((gather("gw_a", x_word_window, U32, list2, half), scales))
+        e_scales = gather("e_scales", x_scale_window, U8, list1)
+        e_words = gather("e_words", x_word_window, U32, list1)
+        a_scales = gather("a_scales", x_scale_window, U8, list2)
+        a_words = gather("a_words", x_word_window, U32, list2)
 
         ys = []
 
@@ -114,16 +110,15 @@ def tile_moe_mlr_relu2_kernel(
             ys.append(keep.tile([P, T], F32, name="ys%d" % j, tag="ys%d" % j))
             for half in range(2):
                 acc = mm.tile([P, BANK], F32, name="acc")
-                words, scales = xe[half]
                 for u in range(2):
                     e = 2 * half + u
-                    cols = slice(u * C, (u + 1) * C)
+                    cols = slice(e * C, (e + 1) * C)
                     nc.tensor.matmul_mx(
-                        out=acc[:, cols],
+                        out=acc[:, u * C : (u + 1) * C],
                         lhsT=ww[:, e, 2 * P * j : 2 * P * (j + 1)].bitcast(FP4X4),
                         lhsT_scale=ws[:, e, P * j : P * (j + 1)],
-                        rhs=words[:, cols].bitcast(FP8X4),
-                        rhs_scale=scales[:, cols],
+                        rhs=e_words[:, cols].bitcast(FP8X4),
+                        rhs_scale=e_scales[:, cols],
                         start=True,
                         stop=True,
                     )
@@ -133,13 +128,12 @@ def tile_moe_mlr_relu2_kernel(
 
         def first_layer(f):
             half, u = divmod(f, 4)
-            words, scales = xa[half]
-            cols = slice(u * D, (u + 1) * D)
+            cols = slice(f * D, (f + 1) * D)
             acc = mm.tile([P, BANK], F32, name="acc")
             nc.tensor.matmul_mx(
                 out=acc[:],
-                lhsT=words[:, cols].bitcast(FP8X4),
-                lhsT_scale=scales[:, cols],
+                lhsT=a_words[:, cols].bitcast(FP8X4),
+                lhsT_scale=a_scales[:, cols],
                 rhs=aw[f // 2][:, f % 2, :].bitcast(FP8X4),
                 rhs_scale=a_s[4 * u :, half, :],
                 start=True,
@@ -148,7 +142,7 @@ def tile_moe_mlr_relu2_kernel(
             if f < F - 1:
                 pos = ring.tile([P, 4, P], F32, name="pos")
             else:
-                pos = keep.tile([P, 4, P], F32, name="pos_last", tag="ys2")
+                pos = keep.tile([P, 4, P], F32, name="pos_last", tag="ys3")
             nc.scalar.activation(out=pos[:], in_=acc[:].rearrange("p (m t) -> p t m", t=4), func=ACT.Relu)
             turned = tr.tile([P, 4, P], F32, name="turned")
             for t in range(4):
@@ -157,13 +151,11 @@ def tile_moe_mlr_relu2_kernel(
                 out=hb[:, D * f : D * (f + 1), :], in_=turned[:].rearrange("p t s -> p s t"), func=ACT.Square
             )
 
-        experts(0)
-        for f in range(F // 2):
+        for j in range(TILES - 1):
+            experts(j)
+        for f in range(F):
             first_layer(f)
-        experts(1)
-        for f in range(F // 2, F):
-            first_layer(f)
-        experts(2)
+        experts(TILES - 1)
 
         hw = keep.tile([P, T], U32, name="hw", align_bytes=64)
         hs = keep.tile([P, T], U8, name="hs", align_bytes=64)
@@ -208,18 +200,16 @@ def tile_moe_mlr_relu2_kernel(
                 nc.scalar.copy(out=res[:, BANK * half : BANK * (half + 1)], in_=back[:].rearrange("p b t -> p (b t)"))
             nc.scalar.dma_start(out=out[rows, :], in_=res[:])
 
-        oy = [scatter("oy%d" % j, "oy%d" % j, list1, ys[j], g1) for j in range(2)]
+        oy = [scatter("oy%d" % j, "oy%d" % j, list1, ys[j], g1) for j in range(TILES - 1)]
         nc.vector.quantize_mx(out=hw[:].bitcast(FP8X4), scales=hs[:], in_=hb[:].rearrange("p s t -> p (s t)"))
-        oy.append(scatter("oy2", "oy2", list1, ys[2], g1))
+        oy_last = scatter("oy3", "oy3", list1, ys[TILES - 1], g1)
         zs = [keep.tile([P, T], F32, name="zs%d" % j, tag="zs%d" % j, align_bytes=64) for j in range(TILES)]
         for j in range(TILES):
             second_layer(j, zs[j])
-        experts(3)
         for j in range(TILES - 1):
             oz = scatter("oz%d" % j, "oz%d" % j, list2, zs[j], g2)
             add_on_tensor(j, oy[j], oz)
         j = TILES - 1
-        oy_last = scatter("oy3", "zs2", list1, ys[j], g1)
         oz_last = scatter("oz3", "oz3", list2, zs[j], g2)
         rows = slice(P * j, P * (j + 1))
         for quarter in range(4):

@@ -74,12 +74,12 @@ def tile_moe_mlr_relu2_kernel(
 
         nc.sync.dma_start(list1[:], offs)
         for q in range(4):
-            nc.sync.dma_start(
+            (nc.sync, nc.scalar)[q // 2].dma_start(
                 out=xs[32 * q : 32 * q + 32, :T].bitcast(I32),
                 in_=x_scales[0, 4 * q : 4 * q + 4, :].bitcast(I32).unsqueeze(0).broadcast_to([8, 4, T // 4]),
             )
-        nc.sync.dma_start(out=xw[:, :T], in_=x_words[0].rearrange("p t d -> p (t d)").bitcast(I32))
         nc.sync.dma_start(list2[:], offs2)
+        nc.sync.dma_start(out=xw[:, :T], in_=x_words[0].rearrange("p t d -> p (t d)").bitcast(I32))
         nc.sync.dma_start(out=ww[:].bitcast(I32), in_=w_words[:, 0].rearrange("e p b -> p e b").bitcast(I32))
         load_planes(nc.sync, ws, w_scales)
         nc.sync.dma_start(out=g1[:], in_=gate)
@@ -94,15 +94,17 @@ def tile_moe_mlr_relu2_kernel(
         make_identity(nc, ident[:])
 
         def gather(name, window, dtype, offsets):
-            picked = keep.tile([P, T], dtype, name=name, align_bytes=64)
-            nc.vector.tensor_copy(picked[:], window.indirect(offsets[:]))
+            picked = keep.tile([P, 16 * offsets.shape[1]], dtype, name=name, align_bytes=64)
+            nc.vector.tensor_copy(picked[:], window.indirect(offsets))
             return picked
 
         x_scale_window, x_word_window = xs[:], xw[:].bitcast(U32)
-        e_scales = gather("e_scales", x_scale_window, U8, list1)
-        e_words = gather("e_words", x_word_window, U32, list1)
-        a_scales = gather("a_scales", x_scale_window, U8, list2)
-        a_words = gather("a_words", x_word_window, U32, list2)
+        e_scales = gather("e_scales", x_scale_window, U8, list1[:])
+        a_scales = gather("a_scales", x_scale_window, U8, list2[:])
+        e_words = [
+            gather("e_words%d" % half, x_word_window, U32, list1[:, 32 * half : 32 * half + 32]) for half in range(2)
+        ]
+        a_words = gather("a_words", x_word_window, U32, list2[:])
 
         ys = []
 
@@ -117,7 +119,7 @@ def tile_moe_mlr_relu2_kernel(
                         out=acc[:, u * C : (u + 1) * C],
                         lhsT=ww[:, e, 2 * P * j : 2 * P * (j + 1)].bitcast(FP4X4),
                         lhsT_scale=ws[:, e, P * j : P * (j + 1)],
-                        rhs=e_words[:, cols].bitcast(FP8X4),
+                        rhs=e_words[half][:, u * C : (u + 1) * C].bitcast(FP8X4),
                         rhs_scale=e_scales[:, cols],
                         start=True,
                         stop=True,

@@ -78,8 +78,8 @@ def tile_moe_mlr_relu2_kernel(
                 out=xs[32 * q : 32 * q + 32, :T].bitcast(I32),
                 in_=x_scales[0, 4 * q : 4 * q + 4, :].bitcast(I32).unsqueeze(0).broadcast_to([8, 4, T // 4]),
             )
-        nc.sync.dma_start(list2[:], offs2)
         nc.sync.dma_start(out=xw[:, :T], in_=x_words[0].rearrange("p t d -> p (t d)").bitcast(I32))
+        nc.sync.dma_start(list2[:], offs2)
         nc.sync.dma_start(out=ww[:].bitcast(I32), in_=w_words[:, 0].rearrange("e p b -> p e b").bitcast(I32))
         load_planes(nc.sync, ws, w_scales)
         nc.sync.dma_start(out=g1[:], in_=gate)
@@ -100,11 +100,17 @@ def tile_moe_mlr_relu2_kernel(
 
         x_scale_window, x_word_window = xs[:], xw[:].bitcast(U32)
         e_scales = gather("e_scales", x_scale_window, U8, list1[:])
-        a_scales = gather("a_scales", x_scale_window, U8, list2[:])
         e_words = [
             gather("e_words%d" % half, x_word_window, U32, list1[:, 32 * half : 32 * half + 32]) for half in range(2)
         ]
+        a_scales = gather("a_scales", x_scale_window, U8, list2[:])
         a_words = gather("a_words", x_word_window, U32, list2[:])
+
+        def gated(values, acc, weights, half):
+            cols = slice(BANK * half, BANK * (half + 1))
+            sums = ring.tile([P, BANK], F32, name="sums")
+            nc.scalar.copy(out=sums[:], in_=acc[:])
+            nc.gpsimd.tensor_tensor(values[:, cols], sums[:], weights[:, cols], ALU.mult)
 
         ys = []
 
@@ -124,7 +130,7 @@ def tile_moe_mlr_relu2_kernel(
                         start=True,
                         stop=True,
                     )
-                nc.scalar.copy(out=ys[j][:, BANK * half : BANK * (half + 1)], in_=acc[:])
+                gated(ys[j], acc, g1, half)
 
         hb = keep.tile([P, T, 4], BF16, name="hb", align_bytes=64)
 
@@ -176,11 +182,11 @@ def tile_moe_mlr_relu2_kernel(
                         start=True,
                         stop=True,
                     )
-                nc.scalar.copy(out=zs[:, BANK * half : BANK * (half + 1)], in_=acc[:])
+                gated(zs, acc, g2, half)
 
-        def scatter(name, tag, offsets, values, weights):
+        def scatter(name, tag, offsets, values):
             window = keep.tile([P, WINDOW], F32, name=name, tag=tag, align_bytes=64)
-            nc.vector.tensor_tensor(window[:].indirect(offsets[:]), values[:], weights[:], ALU.mult)
+            nc.vector.tensor_copy(window[:].indirect(offsets[:]), values[:])
             return window
 
         def add_on_tensor(j, oy, oz):
@@ -202,17 +208,17 @@ def tile_moe_mlr_relu2_kernel(
                 nc.scalar.copy(out=res[:, BANK * half : BANK * (half + 1)], in_=back[:].rearrange("p b t -> p (b t)"))
             nc.scalar.dma_start(out=out[rows, :], in_=res[:])
 
-        oy = [scatter("oy%d" % j, "oy%d" % j, list1, ys[j], g1) for j in range(TILES - 1)]
+        oy = [scatter("oy%d" % j, "oy%d" % j, list1, ys[j]) for j in range(TILES - 1)]
         nc.vector.quantize_mx(out=hw[:].bitcast(FP8X4), scales=hs[:], in_=hb[:].rearrange("p s t -> p (s t)"))
-        oy_last = scatter("oy3", "oy3", list1, ys[TILES - 1], g1)
+        oy_last = scatter("oy3", "oy3", list1, ys[TILES - 1])
         zs = [keep.tile([P, T], F32, name="zs%d" % j, tag="zs%d" % j, align_bytes=64) for j in range(TILES)]
         for j in range(TILES):
             second_layer(j, zs[j])
         for j in range(TILES - 1):
-            oz = scatter("oz%d" % j, "oz%d" % j, list2, zs[j], g2)
+            oz = scatter("oz%d" % j, "oz%d" % j, list2, zs[j])
             add_on_tensor(j, oy[j], oz)
         j = TILES - 1
-        oz_last = scatter("oz3", "oz3", list2, zs[j], g2)
+        oz_last = scatter("oz3", "oz3", list2, zs[j])
         rows = slice(P * j, P * (j + 1))
         for quarter in range(4):
             cols = slice(256 * quarter, 256 * (quarter + 1))

@@ -68,6 +68,7 @@ def tile_moe_mlr_relu2_kernel(
         def load_words(tile, words, f0, f1):
             nc.sync.dma_start(out=tile[:], in_=words[f0:f1, 0].rearrange("f p n d -> p f (n d)").bitcast(I32))
 
+        nc.vector.memset(xs[:, :T].bitcast(I32), 0)
         nc.vector.memset(flat32(ws), 0)
         nc.vector.memset(flat32(a_s), 0)
         nc.vector.memset(flat32(b_s), 0)
@@ -75,8 +76,8 @@ def tile_moe_mlr_relu2_kernel(
         nc.sync.dma_start(list1[:], offs)
         for q in range(4):
             (nc.sync, nc.scalar)[q // 2].dma_start(
-                out=xs[32 * q : 32 * q + 32, :T].bitcast(I32),
-                in_=x_scales[0, 4 * q : 4 * q + 4, :].bitcast(I32).unsqueeze(0).broadcast_to([8, 4, T // 4]),
+                out=xs[32 * q : 32 * q + 4, :T].bitcast(I32),
+                in_=x_scales[0, 4 * q : 4 * q + 4, :].bitcast(I32),
             )
         nc.sync.dma_start(out=xw[:, :T], in_=x_words[0].rearrange("p t d -> p (t d)").bitcast(I32))
         nc.sync.dma_start(list2[:], offs2)

@@ -20,7 +20,12 @@ ALU = mybir.AluOpType
 P = 128
 BANK = 512
 TILES = N // P
+LAST = TILES - 1
+QUADS = 4
+PACKED = 4
+LIST_COLS = T // 16
 WINDOW = 1408
+PIECE = 256
 
 
 def tile_moe_mlr_relu2_kernel(
@@ -33,63 +38,56 @@ def tile_moe_mlr_relu2_kernel(
         mm = ctx.enter_context(tc.psum_pool(name="mm", bufs=4))
         tr = ctx.enter_context(tc.psum_pool(name="tr", bufs=4))
 
-        list1 = keep.tile([P, T // 16], U16, name="list1")
-        list2 = keep.tile([P, T // 16], U16, name="list2")
+        list1 = keep.tile([P, LIST_COLS], U16, name="list1")
+        list2 = keep.tile([P, LIST_COLS], U16, name="list2")
         xw = keep.tile([P, WINDOW], I32, name="xw", align_bytes=64)
         xs = keep.tile([P, WINDOW], U8, name="xs", align_bytes=64)
         ww = keep.tile([P, E, 2 * N], U8, name="ww", align_bytes=64)
         ws = keep.tile([P, E, N], U8, name="ws", align_bytes=64)
         aw = [keep.tile([P, 2, H], I32, name="aw%d" % i, align_bytes=64) for i in range(F // 2)]
-        bw = [keep.tile([P, 4, N], I32, name="bw%d" % i, align_bytes=64) for i in range(F // 4)]
-        a_s = keep.tile([P, 2, H], U8, name="a_s", align_bytes=64)
-        b_s = keep.tile([P, 2, N], U8, name="b_s", align_bytes=64)
+        bw = [keep.tile([P, PACKED, N], I32, name="bw%d" % i, align_bytes=64) for i in range(F // PACKED)]
+        a_s = keep.tile([P, F // PACKED, H], U8, name="a_s", align_bytes=64)
+        b_s = keep.tile([P, F // PACKED, N], U8, name="b_s", align_bytes=64)
         g1 = keep.tile([P, T], F32, name="g1")
         g2 = keep.tile([P, T], F32, name="g2")
         ident = keep.tile([P, P], F32, name="ident")
 
-        def flat32(t):
-            return t[:].rearrange("p e n -> p (e n)").bitcast(I32)
+        nc.vector.memset(xs[:, :T].bitcast(I32), 0)
+        for scale_tile in (ws, a_s, b_s):
+            nc.vector.memset(scale_tile[:].rearrange("p e n -> p (e n)").bitcast(I32), 0)
 
-        def load_planes(queue, plane, scales):
-            for q in range(4):
-                queue.dma_start(
-                    out=plane[32 * q : 32 * q + 4, :, :].bitcast(I32),
-                    in_=scales[:, 0, 4 * q : 4 * q + 4, :].rearrange("e r n -> r e n").bitcast(I32),
-                )
-
-        def load_packed_planes(plane, scales):
-            for half in range(2):
-                for q in range(4):
+        def load_packed_scales(scale_tile, scales):
+            for group in range(F // PACKED):
+                for q in range(QUADS):
                     nc.sync.dma_start(
-                        out=plane[32 * q : 32 * q + 16, half, :].bitcast(I32),
-                        in_=scales[4 * half : 4 * half + 4, 0, 4 * q : 4 * q + 4, :].bitcast(I32),
+                        out=scale_tile[32 * q : 32 * q + 4 * PACKED, group, :].bitcast(I32),
+                        in_=scales[PACKED * group : PACKED * (group + 1), 0, 4 * q : 4 * q + 4, :].bitcast(I32),
                     )
 
-        def load_words(tile, words, f0, f1):
-            nc.sync.dma_start(out=tile[:], in_=words[f0:f1, 0].rearrange("f p n d -> p f (n d)").bitcast(I32))
-
-        nc.vector.memset(xs[:, :T].bitcast(I32), 0)
-        nc.vector.memset(flat32(ws), 0)
-        nc.vector.memset(flat32(a_s), 0)
-        nc.vector.memset(flat32(b_s), 0)
+        def load_words(word_tiles, words):
+            per_tile = F // len(word_tiles)
+            for i, word_tile in enumerate(word_tiles):
+                matrices = words[per_tile * i : per_tile * (i + 1), 0]
+                nc.sync.dma_start(out=word_tile[:], in_=matrices.rearrange("f p n d -> p f (n d)").bitcast(I32))
 
         nc.sync.dma_start(list1[:], offs)
-        for q in range(4):
-            (nc.sync, nc.scalar)[q // 2].dma_start(
-                out=xs[32 * q : 32 * q + 4, :T].bitcast(I32),
-                in_=x_scales[0, 4 * q : 4 * q + 4, :].bitcast(I32),
+        for q in range(QUADS):
+            nc.sync.dma_start(
+                out=xs[32 * q : 32 * q + 4, :T].bitcast(I32), in_=x_scales[0, 4 * q : 4 * q + 4, :].bitcast(I32)
             )
         nc.sync.dma_start(out=xw[:, :T], in_=x_words[0].rearrange("p t d -> p (t d)").bitcast(I32))
         nc.sync.dma_start(list2[:], offs2)
         nc.sync.dma_start(out=ww[:].bitcast(I32), in_=w_words[:, 0].rearrange("e p b -> p e b").bitcast(I32))
-        load_planes(nc.sync, ws, w_scales)
+        for q in range(QUADS):
+            nc.sync.dma_start(
+                out=ws[32 * q : 32 * q + 4, :, :].bitcast(I32),
+                in_=w_scales[:, 0, 4 * q : 4 * q + 4, :].rearrange("e r n -> r e n").bitcast(I32),
+            )
         nc.sync.dma_start(out=g1[:], in_=gate)
-        load_packed_planes(a_s, wa_scales)
-        for i in range(F // 2):
-            load_words(aw[i], wa_words, 2 * i, 2 * i + 2)
-        load_packed_planes(b_s, wb_scales)
-        for i in range(F // 4):
-            load_words(bw[i], wb_words, 4 * i, 4 * i + 4)
+        load_packed_scales(a_s, wa_scales)
+        load_words(aw, wa_words)
+        load_packed_scales(b_s, wb_scales)
+        load_words(bw, wb_words)
         nc.sync.dma_start(out=g2[:], in_=gate2)
 
         make_identity(nc, ident[:])
@@ -100,9 +98,11 @@ def tile_moe_mlr_relu2_kernel(
             return picked
 
         x_scale_window, x_word_window = xs[:], xw[:].bitcast(U32)
+        half_cols = LIST_COLS // 2
         e_scales = gather("e_scales", x_scale_window, U8, list1[:])
         e_words = [
-            gather("e_words%d" % half, x_word_window, U32, list1[:, 32 * half : 32 * half + 32]) for half in range(2)
+            gather("e_words%d" % half, x_word_window, U32, list1[:, half_cols * half : half_cols * (half + 1)])
+            for half in range(2)
         ]
         a_scales = gather("a_scales", x_scale_window, U8, list2[:])
         a_words = gather("a_words", x_word_window, U32, list2[:])
@@ -113,58 +113,53 @@ def tile_moe_mlr_relu2_kernel(
             nc.scalar.copy(out=sums[:], in_=acc[:])
             nc.gpsimd.tensor_tensor(values[:, cols], sums[:], weights[:, cols], ALU.mult)
 
-        ys = []
-
         def experts(j):
-            ys.append(keep.tile([P, T], F32, name="ys%d" % j, tag="ys%d" % j))
+            ys = keep.tile([P, T], F32, name="ys%d" % j, tag="ys%d" % j)
             for half in range(2):
                 acc = mm.tile([P, BANK], F32, name="acc")
-                for u in range(2):
-                    e = 2 * half + u
-                    cols = slice(e * C, (e + 1) * C)
+                for u in range(BANK // C):
+                    e = BANK // C * half + u
                     nc.tensor.matmul_mx(
                         out=acc[:, u * C : (u + 1) * C],
                         lhsT=ww[:, e, 2 * P * j : 2 * P * (j + 1)].bitcast(FP4X4),
                         lhsT_scale=ws[:, e, P * j : P * (j + 1)],
                         rhs=e_words[half][:, u * C : (u + 1) * C].bitcast(FP8X4),
-                        rhs_scale=e_scales[:, cols],
+                        rhs_scale=e_scales[:, e * C : (e + 1) * C],
                         start=True,
                         stop=True,
                     )
-                gated(ys[j], acc, g1, half)
+                gated(ys, acc, g1, half)
+            return ys
 
         hb = keep.tile([P, T, 4], BF16, name="hb", align_bytes=64)
 
         def first_layer(f):
-            half, u = divmod(f, 4)
-            cols = slice(f * D, (f + 1) * D)
+            group, u = divmod(f, PACKED)
+            slots = slice(f * D, (f + 1) * D)
             acc = mm.tile([P, BANK], F32, name="acc")
             nc.tensor.matmul_mx(
                 out=acc[:],
-                lhsT=a_words[:, cols].bitcast(FP8X4),
-                lhsT_scale=a_scales[:, cols],
+                lhsT=a_words[:, slots].bitcast(FP8X4),
+                lhsT_scale=a_scales[:, slots],
                 rhs=aw[f // 2][:, f % 2, :].bitcast(FP8X4),
-                rhs_scale=a_s[4 * u :, half, :],
+                rhs_scale=a_s[4 * u :, group, :],
                 start=True,
                 stop=True,
             )
             if f < F - 1:
                 pos = ring.tile([P, 4, P], F32, name="pos")
             else:
-                pos = keep.tile([P, 4, P], F32, name="pos_last", tag="ys3")
+                pos = keep.tile([P, 4, P], F32, name="pos_last", tag="ys%d" % LAST)
             nc.scalar.activation(out=pos[:], in_=acc[:].rearrange("p (m t) -> p t m", t=4), func=ACT.Relu)
             turned = tr.tile([P, 4, P], F32, name="turned")
             for t in range(4):
                 nc.tensor.transpose(turned[:, t, :], pos[:, t, :], ident[:])
-            nc.scalar.activation(
-                out=hb[:, D * f : D * (f + 1), :], in_=turned[:].rearrange("p t s -> p s t"), func=ACT.Square
-            )
+            nc.scalar.activation(out=hb[:, slots, :], in_=turned[:].rearrange("p t s -> p s t"), func=ACT.Square)
 
-        for j in range(TILES - 1):
-            experts(j)
+        ys = [experts(j) for j in range(LAST)]
         for f in range(F):
             first_layer(f)
-        experts(TILES - 1)
+        ys.append(experts(LAST))
 
         hw = keep.tile([P, T], U32, name="hw", align_bytes=64)
         hs = keep.tile([P, T], U8, name="hs", align_bytes=64)
@@ -172,8 +167,8 @@ def tile_moe_mlr_relu2_kernel(
         def second_layer(j, zs):
             for half in range(2):
                 acc = mm.tile([P, BANK], F32, name="acc")
-                for u in range(4):
-                    f = 4 * half + u
+                for u in range(PACKED):
+                    f = PACKED * half + u
                     nc.tensor.matmul_mx(
                         out=acc[:, u * D : (u + 1) * D],
                         lhsT=bw[half][:, u, P * j : P * (j + 1)].bitcast(FP8X4),
@@ -185,20 +180,21 @@ def tile_moe_mlr_relu2_kernel(
                     )
                 gated(zs, acc, g2, half)
 
-        def scatter(name, tag, offsets, values):
-            window = keep.tile([P, WINDOW], F32, name=name, tag=tag, align_bytes=64)
+        def scatter(name, offsets, values):
+            window = keep.tile([P, WINDOW], F32, name=name, align_bytes=64)
             nc.vector.tensor_copy(window[:].indirect(offsets[:]), values[:])
             return window
 
-        def add_on_tensor(j, oy, oz):
-            rows = slice(P * j, P * (j + 1))
+        def add_on_tensor(j, oy_tile, oz_tile):
             by_token = []
             for half in range(2):
                 total = tr.tile([P, 4, P], F32, name="turned")
                 for b in range(4):
                     cols = slice(BANK * half + P * b, BANK * half + P * (b + 1))
-                    nc.tensor.matmul(total[:, b, :], oy[:, cols], ident[:], start=True, stop=False, is_transpose=True)
-                    nc.tensor.matmul(total[:, b, :], oz[:, cols], ident[:], start=False, stop=True, is_transpose=True)
+                    for addend, first in ((oy_tile, True), (oz_tile, False)):
+                        nc.tensor.matmul(
+                            total[:, b, :], addend[:, cols], ident[:], start=first, stop=not first, is_transpose=True
+                        )
                 by_token.append(ring.tile([P, 4, P], F32, name="by_token"))
                 nc.scalar.copy(out=by_token[half][:], in_=total[:])
             res = ring.tile([P, T], F32, name="res")
@@ -207,22 +203,20 @@ def tile_moe_mlr_relu2_kernel(
                 for b in range(4):
                     nc.tensor.transpose(back[:, b, :], by_token[half][:, b, :], ident[:])
                 nc.scalar.copy(out=res[:, BANK * half : BANK * (half + 1)], in_=back[:].rearrange("p b t -> p (b t)"))
-            nc.scalar.dma_start(out=out[rows, :], in_=res[:])
+            nc.scalar.dma_start(out=out[P * j : P * (j + 1), :], in_=res[:])
 
-        oy = [scatter("oy%d" % j, "oy%d" % j, list1, ys[j]) for j in range(TILES - 1)]
+        oy = [scatter("oy%d" % j, list1, ys[j]) for j in range(LAST)]
         nc.vector.quantize_mx(out=hw[:].bitcast(FP8X4), scales=hs[:], in_=hb[:].rearrange("p s t -> p (s t)"))
-        oy_last = scatter("oy3", "oy3", list1, ys[TILES - 1])
-        zs = [keep.tile([P, T], F32, name="zs%d" % j, tag="zs%d" % j, align_bytes=64) for j in range(TILES)]
+        oy.append(scatter("oy%d" % LAST, list1, ys[LAST]))
+        zs = [keep.tile([P, T], F32, name="zs%d" % j, align_bytes=64) for j in range(TILES)]
         for j in range(TILES):
             second_layer(j, zs[j])
-        for j in range(TILES - 1):
-            oz = scatter("oz%d" % j, "oz%d" % j, list2, zs[j])
-            add_on_tensor(j, oy[j], oz)
-        j = TILES - 1
-        oz_last = scatter("oz3", "oz3", list2, zs[j])
-        rows = slice(P * j, P * (j + 1))
-        for quarter in range(4):
-            cols = slice(256 * quarter, 256 * (quarter + 1))
-            last = keep.tile([P, 256], F32, name="last%d" % quarter)
-            nc.vector.tensor_tensor(last[:], oy_last[:, cols], oz_last[:, cols], ALU.add)
-            nc.sync.dma_start(out=out[rows, cols], in_=last[:])
+        for j in range(LAST):
+            add_on_tensor(j, oy[j], scatter("oz%d" % j, list2, zs[j]))
+
+        oz_last = scatter("oz%d" % LAST, list2, zs[LAST])
+        for c in range(0, T, PIECE):
+            cols = slice(c, c + PIECE)
+            piece = keep.tile([P, PIECE], F32, name="piece%d" % c)
+            nc.vector.tensor_tensor(piece[:], oy[LAST][:, cols], oz_last[:, cols], ALU.add)
+            nc.sync.dma_start(out=out[P * LAST : P * TILES, cols], in_=piece[:])

@@ -42,6 +42,8 @@ def tile_moe_mlr_relu2_kernel(
         list2 = keep.tile([P, LIST_COLS], U16, name="list2")
         xw = keep.tile([P, WINDOW], I32, name="xw", align_bytes=64)
         xs = keep.tile([P, WINDOW], U8, name="xs", align_bytes=64)
+        xs_spread = keep.tile([P, WINDOW], U8, name="xs_spread", align_bytes=64)
+        a_scales = keep.tile([P, T], U8, name="a_scales", align_bytes=64)
         ww = keep.tile([P, E, 2 * N], U8, name="ww", align_bytes=64)
         ws = keep.tile([P, E, N], U8, name="ws", align_bytes=64)
         aw = [keep.tile([P, 2, H], I32, name="aw%d" % i, align_bytes=64) for i in range(F // 2)]
@@ -53,8 +55,14 @@ def tile_moe_mlr_relu2_kernel(
         ident = keep.tile([P, P], F32, name="ident")
 
         nc.vector.memset(xs[:, :T].bitcast(I32), 0)
+        nc.vector.memset(a_scales[:].bitcast(I32), 0)
         for scale_tile in (ws, a_s, b_s):
             nc.vector.memset(scale_tile[:].rearrange("p e n -> p (e n)").bitcast(I32), 0)
+
+        def gather(name, window, dtype, offsets):
+            picked = keep.tile([P, 16 * offsets.shape[1]], dtype, name=name, align_bytes=64)
+            nc.vector.tensor_copy(picked[:], window.indirect(offsets))
+            return picked
 
         def load_packed_scales(scale_tile, scales):
             for group in range(F // PACKED):
@@ -70,13 +78,17 @@ def tile_moe_mlr_relu2_kernel(
                 matrices = words[per_tile * i : per_tile * (i + 1), 0]
                 nc.sync.dma_start(out=word_tile[:], in_=matrices.rearrange("f p n d -> p f (n d)").bitcast(I32))
 
+        nc.sync.dma_start(list2[:], offs2)
+        nc.sync.dma_start(
+            out=xs_spread[:, :T].bitcast(I32),
+            in_=x_scales[0].bitcast(I32).unsqueeze(1).broadcast_to([4 * QUADS, P // (4 * QUADS), T // 4]),
+        )
         nc.sync.dma_start(list1[:], offs)
         for q in range(QUADS):
             nc.sync.dma_start(
                 out=xs[32 * q : 32 * q + 4, :T].bitcast(I32), in_=x_scales[0, 4 * q : 4 * q + 4, :].bitcast(I32)
             )
         nc.sync.dma_start(out=xw[:, :T], in_=x_words[0].rearrange("p t d -> p (t d)").bitcast(I32))
-        nc.sync.dma_start(list2[:], offs2)
         nc.sync.dma_start(out=ww[:].bitcast(I32), in_=w_words[:, 0].rearrange("e p b -> p e b").bitcast(I32))
         for q in range(QUADS):
             nc.sync.dma_start(
@@ -85,17 +97,18 @@ def tile_moe_mlr_relu2_kernel(
             )
         nc.sync.dma_start(out=g1[:], in_=gate)
         load_packed_scales(a_s, wa_scales)
+        a_spread = gather("a_spread", xs_spread[:], U8, list2[:])
+        for q in range(QUADS):
+            nc.sync.dma_start(
+                out=a_scales[32 * q : 32 * q + 4, :].bitcast(I32),
+                in_=a_spread[32 * q : 32 * (q + 1) : 8, :].bitcast(I32),
+            )
         load_words(aw, wa_words)
         load_packed_scales(b_s, wb_scales)
         load_words(bw, wb_words)
         nc.sync.dma_start(out=g2[:], in_=gate2)
 
         make_identity(nc, ident[:])
-
-        def gather(name, window, dtype, offsets):
-            picked = keep.tile([P, 16 * offsets.shape[1]], dtype, name=name, align_bytes=64)
-            nc.vector.tensor_copy(picked[:], window.indirect(offsets))
-            return picked
 
         x_scale_window, x_word_window = xs[:], xw[:].bitcast(U32)
         half_cols = LIST_COLS // 2
@@ -104,14 +117,11 @@ def tile_moe_mlr_relu2_kernel(
             gather("e_words%d" % half, x_word_window, U32, list1[:, half_cols * half : half_cols * (half + 1)])
             for half in range(2)
         ]
-        a_scales = gather("a_scales", x_scale_window, U8, list2[:])
         a_words = gather("a_words", x_word_window, U32, list2[:])
 
         def gated(values, acc, weights, half):
             cols = slice(BANK * half, BANK * (half + 1))
-            sums = ring.tile([P, BANK], F32, name="sums")
-            nc.scalar.copy(out=sums[:], in_=acc[:])
-            nc.gpsimd.tensor_tensor(values[:, cols], sums[:], weights[:, cols], ALU.mult)
+            nc.scalar.copy(out=values[:, cols], in_=acc[:])
 
         def experts(j):
             ys = keep.tile([P, T], F32, name="ys%d" % j, tag="ys%d" % j)
@@ -180,9 +190,9 @@ def tile_moe_mlr_relu2_kernel(
                     )
                 gated(zs, acc, g2, half)
 
-        def scatter(name, offsets, values):
+        def scatter(name, offsets, values, weights):
             window = keep.tile([P, WINDOW], F32, name=name, align_bytes=64)
-            nc.vector.tensor_copy(window[:].indirect(offsets[:]), values[:])
+            nc.vector.tensor_tensor(window[:].indirect(offsets[:]), values[:], weights[:], ALU.mult)
             return window
 
         def add_on_tensor(j, oy_tile, oz_tile):
@@ -205,16 +215,16 @@ def tile_moe_mlr_relu2_kernel(
                 nc.scalar.copy(out=res[:, BANK * half : BANK * (half + 1)], in_=back[:].rearrange("p b t -> p (b t)"))
             nc.scalar.dma_start(out=out[P * j : P * (j + 1), :], in_=res[:])
 
-        oy = [scatter("oy%d" % j, list1, ys[j]) for j in range(LAST)]
+        oy = [scatter("oy%d" % j, list1, ys[j], g1) for j in range(LAST)]
         nc.vector.quantize_mx(out=hw[:].bitcast(FP8X4), scales=hs[:], in_=hb[:].rearrange("p s t -> p (s t)"))
-        oy.append(scatter("oy%d" % LAST, list1, ys[LAST]))
+        oy.append(scatter("oy%d" % LAST, list1, ys[LAST], g1))
         zs = [keep.tile([P, T], F32, name="zs%d" % j, align_bytes=64) for j in range(TILES)]
         for j in range(TILES):
             second_layer(j, zs[j])
         for j in range(LAST):
-            add_on_tensor(j, oy[j], scatter("oz%d" % j, list2, zs[j]))
+            add_on_tensor(j, oy[j], scatter("oz%d" % j, list2, zs[j], g2))
 
-        oz_last = scatter("oz%d" % LAST, list2, zs[LAST])
+        oz_last = scatter("oz%d" % LAST, list2, zs[LAST], g2)
         for c in range(0, T, PIECE):
             cols = slice(c, c + PIECE)
             piece = keep.tile([P, PIECE], F32, name="piece%d" % c)

@@ -54,10 +54,10 @@ def tile_moe_mlr_relu2_kernel(
         g2 = keep.tile([P, T], F32, name="g2")
         ident = keep.tile([P, P], F32, name="ident")
 
-        nc.vector.memset(xs[:, :T].bitcast(I32), 0)
-        nc.vector.memset(a_scales[:].bitcast(I32), 0)
+        nc.gpsimd.memset(xs[:, :T].bitcast(I32), 0)
         for scale_tile in (ws, a_s, b_s):
-            nc.vector.memset(scale_tile[:].rearrange("p e n -> p (e n)").bitcast(I32), 0)
+            nc.gpsimd.memset(scale_tile[:].rearrange("p e n -> p (e n)").bitcast(I32), 0)
+        nc.gpsimd.memset(a_scales[:].bitcast(I32), 0)
 
         def gather(name, window, dtype, offsets):
             picked = keep.tile([P, 16 * offsets.shape[1]], dtype, name=name, align_bytes=64)
@@ -78,11 +78,11 @@ def tile_moe_mlr_relu2_kernel(
                 matrices = words[per_tile * i : per_tile * (i + 1), 0]
                 nc.sync.dma_start(out=word_tile[:], in_=matrices.rearrange("f p n d -> p f (n d)").bitcast(I32))
 
-        nc.sync.dma_start(list2[:], offs2)
         nc.sync.dma_start(
             out=xs_spread[:, :T].bitcast(I32),
             in_=x_scales[0].bitcast(I32).unsqueeze(1).broadcast_to([4 * QUADS, P // (4 * QUADS), T // 4]),
         )
+        nc.sync.dma_start(list2[:], offs2)
         nc.sync.dma_start(list1[:], offs)
         for q in range(QUADS):
             nc.sync.dma_start(

@@ -54,6 +54,8 @@ def tile_moe_mlr_relu2_kernel(
         g2 = keep.tile([P, T], F32, name="g2")
         ident = keep.tile([P, P], F32, name="ident")
 
+        nc.vector.memset(xs_spread[:, 480 : T + 4].bitcast(I32), 0)
+        nc.gpsimd.memset(xs_spread[:, :480].bitcast(I32), 0)
         nc.gpsimd.memset(xs[:, :T].bitcast(I32), 0)
         for scale_tile in (ws, a_s, b_s):
             nc.gpsimd.memset(scale_tile[:].rearrange("p e n -> p (e n)").bitcast(I32), 0)
@@ -78,11 +80,11 @@ def tile_moe_mlr_relu2_kernel(
                 matrices = words[per_tile * i : per_tile * (i + 1), 0]
                 nc.sync.dma_start(out=word_tile[:], in_=matrices.rearrange("f p n d -> p f (n d)").bitcast(I32))
 
-        nc.sync.dma_start(
-            out=xs_spread[:, :T].bitcast(I32),
-            in_=x_scales[0].bitcast(I32).unsqueeze(1).broadcast_to([4 * QUADS, P // (4 * QUADS), T // 4]),
-        )
         nc.sync.dma_start(list2[:], offs2)
+        nc.sync.dma_start(
+            out=xs_spread[0:P:8, :T].bitcast(I32),
+            in_=x_scales[0].bitcast(I32),
+        )
         nc.sync.dma_start(list1[:], offs)
         for q in range(QUADS):
             nc.sync.dma_start(

@@ -43,7 +43,7 @@ def tile_moe_mlr_relu2_kernel(
         xw = keep.tile([P, WINDOW], I32, name="xw", align_bytes=64)
         xs = keep.tile([P, WINDOW], U8, name="xs", align_bytes=64)
         xs_spread = keep.tile([P, WINDOW], U8, name="xs_spread", align_bytes=64)
-        a_scales = keep.tile([P, T], U8, name="a_scales", align_bytes=64)
+        e_scales = keep.tile([P, T], U8, name="e_scales", align_bytes=64)
         ww = keep.tile([P, E, 2 * N], U8, name="ww", align_bytes=64)
         ws = keep.tile([P, E, N], U8, name="ws", align_bytes=64)
         aw = [keep.tile([P, 2, H], I32, name="aw%d" % i, align_bytes=64) for i in range(F // 2)]
@@ -54,12 +54,12 @@ def tile_moe_mlr_relu2_kernel(
         g2 = keep.tile([P, T], F32, name="g2")
         ident = keep.tile([P, P], F32, name="ident")
 
-        nc.vector.memset(xs_spread[:, 480 : T + 4].bitcast(I32), 0)
-        nc.gpsimd.memset(xs_spread[:, :480].bitcast(I32), 0)
+        nc.gpsimd.memset(xs_spread[:112, :T].bitcast(I32), 0)
+        nc.gpsimd.memset(ws[:].rearrange("p e n -> p (e n)").bitcast(I32), 0)
         nc.gpsimd.memset(xs[:, :T].bitcast(I32), 0)
-        for scale_tile in (ws, a_s, b_s):
+        nc.gpsimd.memset(e_scales[:].bitcast(I32), 0)
+        for scale_tile in (a_s, b_s):
             nc.gpsimd.memset(scale_tile[:].rearrange("p e n -> p (e n)").bitcast(I32), 0)
-        nc.gpsimd.memset(a_scales[:].bitcast(I32), 0)
 
         def gather(name, window, dtype, offsets):
             picked = keep.tile([P, 16 * offsets.shape[1]], dtype, name=name, align_bytes=64)
@@ -80,31 +80,28 @@ def tile_moe_mlr_relu2_kernel(
                 matrices = words[per_tile * i : per_tile * (i + 1), 0]
                 nc.sync.dma_start(out=word_tile[:], in_=matrices.rearrange("f p n d -> p f (n d)").bitcast(I32))
 
-        nc.sync.dma_start(list2[:], offs2)
-        nc.sync.dma_start(
-            out=xs_spread[0:P:8, :T].bitcast(I32),
-            in_=x_scales[0].bitcast(I32),
-        )
         nc.sync.dma_start(list1[:], offs)
-        for q in range(QUADS):
-            nc.sync.dma_start(
-                out=xs[32 * q : 32 * q + 4, :T].bitcast(I32), in_=x_scales[0, 4 * q : 4 * q + 4, :].bitcast(I32)
-            )
+        nc.sync.dma_start(out=xs_spread[112:, :T].bitcast(I32), in_=x_scales[0].bitcast(I32))
         nc.sync.dma_start(out=xw[:, :T], in_=x_words[0].rearrange("p t d -> p (t d)").bitcast(I32))
+        nc.sync.dma_start(list2[:], offs2)
         nc.sync.dma_start(out=ww[:].bitcast(I32), in_=w_words[:, 0].rearrange("e p b -> p e b").bitcast(I32))
         for q in range(QUADS):
             nc.sync.dma_start(
                 out=ws[32 * q : 32 * q + 4, :, :].bitcast(I32),
                 in_=w_scales[:, 0, 4 * q : 4 * q + 4, :].rearrange("e r n -> r e n").bitcast(I32),
             )
-        nc.sync.dma_start(out=g1[:], in_=gate)
-        load_packed_scales(a_s, wa_scales)
-        a_spread = gather("a_spread", xs_spread[:], U8, list2[:])
         for q in range(QUADS):
             nc.sync.dma_start(
-                out=a_scales[32 * q : 32 * q + 4, :].bitcast(I32),
-                in_=a_spread[32 * q : 32 * (q + 1) : 8, :].bitcast(I32),
+                out=xs[32 * q : 32 * q + 4, :T].bitcast(I32), in_=x_scales[0, 4 * q : 4 * q + 4, :].bitcast(I32)
             )
+        nc.sync.dma_start(out=g1[:], in_=gate)
+        e_rows = gather("e_rows", xs_spread[:], U8, list1[:])
+        for q in range(QUADS):
+            nc.sync.dma_start(
+                out=e_scales[32 * q : 32 * q + 4, :].bitcast(I32),
+                in_=e_rows[112 + 4 * q : 112 + 4 * (q + 1), :].bitcast(I32),
+            )
+        load_packed_scales(a_s, wa_scales)
         load_words(aw, wa_words)
         load_packed_scales(b_s, wb_scales)
         load_words(bw, wb_words)
@@ -114,11 +111,8 @@ def tile_moe_mlr_relu2_kernel(
 
         x_scale_window, x_word_window = xs[:], xw[:].bitcast(U32)
         half_cols = LIST_COLS // 2
-        e_scales = gather("e_scales", x_scale_window, U8, list1[:])
-        e_words = [
-            gather("e_words%d" % half, x_word_window, U32, list1[:, half_cols * half : half_cols * (half + 1)])
-            for half in range(2)
-        ]
+        e_words = gather("e_words", x_word_window, U32, list1[:])
+        a_scales = gather("a_scales", x_scale_window, U8, list2[:])
         a_words = gather("a_words", x_word_window, U32, list2[:])
 
         def gated(values, acc, weights, half):
@@ -135,7 +129,7 @@ def tile_moe_mlr_relu2_kernel(
                         out=acc[:, u * C : (u + 1) * C],
                         lhsT=ww[:, e, 2 * P * j : 2 * P * (j + 1)].bitcast(FP4X4),
                         lhsT_scale=ws[:, e, P * j : P * (j + 1)],
-                        rhs=e_words[half][:, u * C : (u + 1) * C].bitcast(FP8X4),
+                        rhs=e_words[:, e * C : (e + 1) * C].bitcast(FP8X4),
                         rhs_scale=e_scales[:, e * C : (e + 1) * C],
                         start=True,
                         stop=True,

@@ -23,6 +23,7 @@ TILES = N // P
 LAST = TILES - 1
 QUADS = 4
 PACKED = 4
+STACK = P - 4 * QUADS
 LIST_COLS = T // 16
 WINDOW = 1408
 PIECE = 256
@@ -42,7 +43,7 @@ def tile_moe_mlr_relu2_kernel(
         list2 = keep.tile([P, LIST_COLS], U16, name="list2")
         xw = keep.tile([P, WINDOW], I32, name="xw", align_bytes=64)
         xs = keep.tile([P, WINDOW], U8, name="xs", align_bytes=64)
-        xs_spread = keep.tile([P, WINDOW], U8, name="xs_spread", align_bytes=64)
+        xs_stacked = keep.tile([P, WINDOW], U8, name="xs_stacked", align_bytes=64)
         e_scales = keep.tile([P, T], U8, name="e_scales", align_bytes=64)
         ww = keep.tile([P, E, 2 * N], U8, name="ww", align_bytes=64)
         ws = keep.tile([P, E, N], U8, name="ws", align_bytes=64)
@@ -54,7 +55,7 @@ def tile_moe_mlr_relu2_kernel(
         g2 = keep.tile([P, T], F32, name="g2")
         ident = keep.tile([P, P], F32, name="ident")
 
-        nc.gpsimd.memset(xs_spread[:112, :T].bitcast(I32), 0)
+        nc.vector.memset(xs_stacked[:STACK, :T].bitcast(I32), 0)
         nc.gpsimd.memset(ws[:].rearrange("p e n -> p (e n)").bitcast(I32), 0)
         nc.gpsimd.memset(xs[:, :T].bitcast(I32), 0)
         nc.gpsimd.memset(e_scales[:].bitcast(I32), 0)
@@ -81,7 +82,7 @@ def tile_moe_mlr_relu2_kernel(
                 nc.sync.dma_start(out=word_tile[:], in_=matrices.rearrange("f p n d -> p f (n d)").bitcast(I32))
 
         nc.sync.dma_start(list1[:], offs)
-        nc.sync.dma_start(out=xs_spread[112:, :T].bitcast(I32), in_=x_scales[0].bitcast(I32))
+        nc.scalar.dma_start(out=xs_stacked[STACK:, :T].bitcast(I32), in_=x_scales[0].bitcast(I32))
         nc.sync.dma_start(out=xw[:, :T], in_=x_words[0].rearrange("p t d -> p (t d)").bitcast(I32))
         nc.sync.dma_start(list2[:], offs2)
         nc.sync.dma_start(out=ww[:].bitcast(I32), in_=w_words[:, 0].rearrange("e p b -> p e b").bitcast(I32))
@@ -94,13 +95,13 @@ def tile_moe_mlr_relu2_kernel(
             nc.sync.dma_start(
                 out=xs[32 * q : 32 * q + 4, :T].bitcast(I32), in_=x_scales[0, 4 * q : 4 * q + 4, :].bitcast(I32)
             )
-        nc.sync.dma_start(out=g1[:], in_=gate)
-        e_rows = gather("e_rows", xs_spread[:], U8, list1[:])
+        e_stacked = gather("e_stacked", xs_stacked[:], U8, list1[:])
         for q in range(QUADS):
             nc.sync.dma_start(
                 out=e_scales[32 * q : 32 * q + 4, :].bitcast(I32),
-                in_=e_rows[112 + 4 * q : 112 + 4 * (q + 1), :].bitcast(I32),
+                in_=e_stacked[STACK + 4 * q : STACK + 4 * (q + 1), :].bitcast(I32),
             )
+        nc.sync.dma_start(out=g1[:], in_=gate)
         load_packed_scales(a_s, wa_scales)
         load_words(aw, wa_words)
         load_packed_scales(b_s, wb_scales)
@@ -109,15 +110,10 @@ def tile_moe_mlr_relu2_kernel(
 
         make_identity(nc, ident[:])
 
-        x_scale_window, x_word_window = xs[:], xw[:].bitcast(U32)
-        half_cols = LIST_COLS // 2
+        x_word_window = xw[:].bitcast(U32)
         e_words = gather("e_words", x_word_window, U32, list1[:])
-        a_scales = gather("a_scales", x_scale_window, U8, list2[:])
+        a_scales = gather("a_scales", xs[:], U8, list2[:])
         a_words = gather("a_words", x_word_window, U32, list2[:])
-
-        def gated(values, acc, weights, half):
-            cols = slice(BANK * half, BANK * (half + 1))
-            nc.scalar.copy(out=values[:, cols], in_=acc[:])
 
         def experts(j):
             ys = keep.tile([P, T], F32, name="ys%d" % j, tag="ys%d" % j)
@@ -134,7 +130,7 @@ def tile_moe_mlr_relu2_kernel(
                         start=True,
                         stop=True,
                     )
-                gated(ys, acc, g1, half)
+                nc.scalar.copy(out=ys[:, BANK * half : BANK * (half + 1)], in_=acc[:])
             return ys
 
         hb = keep.tile([P, T, 4], BF16, name="hb", align_bytes=64)
@@ -184,7 +180,7 @@ def tile_moe_mlr_relu2_kernel(
                         start=True,
                         stop=True,
                     )
-                gated(zs, acc, g2, half)
+                nc.scalar.copy(out=zs[:, BANK * half : BANK * (half + 1)], in_=acc[:])
 
         def scatter(name, offsets, values, weights):
             window = keep.tile([P, WINDOW], F32, name=name, align_bytes=64)

@@ -55,9 +55,9 @@ def tile_moe_mlr_relu2_kernel(
         g2 = keep.tile([P, T], F32, name="g2")
         ident = keep.tile([P, P], F32, name="ident")
 
-        nc.vector.memset(xs_stacked[:STACK, :T].bitcast(I32), 0)
-        nc.gpsimd.memset(ws[:].rearrange("p e n -> p (e n)").bitcast(I32), 0)
         nc.gpsimd.memset(xs[:, :T].bitcast(I32), 0)
+        nc.gpsimd.memset(xs_stacked[:STACK, :T].bitcast(I32), 0)
+        nc.gpsimd.memset(ws[:].rearrange("p e n -> p (e n)").bitcast(I32), 0)
         nc.gpsimd.memset(e_scales[:].bitcast(I32), 0)
         for scale_tile in (a_s, b_s):
             nc.gpsimd.memset(scale_tile[:].rearrange("p e n -> p (e n)").bitcast(I32), 0)
@@ -82,7 +82,11 @@ def tile_moe_mlr_relu2_kernel(
                 nc.sync.dma_start(out=word_tile[:], in_=matrices.rearrange("f p n d -> p f (n d)").bitcast(I32))
 
         nc.sync.dma_start(list1[:], offs)
-        nc.scalar.dma_start(out=xs_stacked[STACK:, :T].bitcast(I32), in_=x_scales[0].bitcast(I32))
+        nc.sync.dma_start(out=xs_stacked[STACK:, :T].bitcast(I32), in_=x_scales[0].bitcast(I32))
+        for q in range(QUADS):
+            nc.sync.dma_start(
+                out=xs[32 * q : 32 * q + 4, :T].bitcast(I32), in_=x_scales[0, 4 * q : 4 * q + 4, :].bitcast(I32)
+            )
         nc.sync.dma_start(out=xw[:, :T], in_=x_words[0].rearrange("p t d -> p (t d)").bitcast(I32))
         nc.sync.dma_start(list2[:], offs2)
         nc.sync.dma_start(out=ww[:].bitcast(I32), in_=w_words[:, 0].rearrange("e p b -> p e b").bitcast(I32))
@@ -90,10 +94,6 @@ def tile_moe_mlr_relu2_kernel(
             nc.sync.dma_start(
                 out=ws[32 * q : 32 * q + 4, :, :].bitcast(I32),
                 in_=w_scales[:, 0, 4 * q : 4 * q + 4, :].rearrange("e r n -> r e n").bitcast(I32),
-            )
-        for q in range(QUADS):
-            nc.sync.dma_start(
-                out=xs[32 * q : 32 * q + 4, :T].bitcast(I32), in_=x_scales[0, 4 * q : 4 * q + 4, :].bitcast(I32)
             )
         e_stacked = gather("e_stacked", xs_stacked[:], U8, list1[:])
         for q in range(QUADS):

@@ -42,9 +42,9 @@ def tile_moe_mlr_relu2_kernel(
         list1 = keep.tile([P, LIST_COLS], U16, name="list1")
         list2 = keep.tile([P, LIST_COLS], U16, name="list2")
         xw = keep.tile([P, WINDOW], I32, name="xw", align_bytes=64)
-        xs = keep.tile([P, WINDOW], U8, name="xs", align_bytes=64)
         xs_stacked = keep.tile([P, WINDOW], U8, name="xs_stacked", align_bytes=64)
         e_scales = keep.tile([P, T], U8, name="e_scales", align_bytes=64)
+        a_scales = keep.tile([P, T], U8, name="a_scales", align_bytes=64)
         ww = keep.tile([P, E, 2 * N], U8, name="ww", align_bytes=64)
         ws = keep.tile([P, E, N], U8, name="ws", align_bytes=64)
         aw = [keep.tile([P, 2, H], I32, name="aw%d" % i, align_bytes=64) for i in range(F // 2)]
@@ -55,10 +55,10 @@ def tile_moe_mlr_relu2_kernel(
         g2 = keep.tile([P, T], F32, name="g2")
         ident = keep.tile([P, P], F32, name="ident")
 
-        nc.gpsimd.memset(xs[:, :T].bitcast(I32), 0)
         nc.gpsimd.memset(xs_stacked[:STACK, :T].bitcast(I32), 0)
         nc.gpsimd.memset(ws[:].rearrange("p e n -> p (e n)").bitcast(I32), 0)
         nc.gpsimd.memset(e_scales[:].bitcast(I32), 0)
+        nc.gpsimd.memset(a_scales[:].bitcast(I32), 0)
         for scale_tile in (a_s, b_s):
             nc.gpsimd.memset(scale_tile[:].rearrange("p e n -> p (e n)").bitcast(I32), 0)
 
@@ -66,6 +66,13 @@ def tile_moe_mlr_relu2_kernel(
             picked = keep.tile([P, 16 * offsets.shape[1]], dtype, name=name, align_bytes=64)
             nc.vector.tensor_copy(picked[:], window.indirect(offsets))
             return picked
+
+        def unstack(scale_tile, stacked):
+            for q in range(QUADS):
+                nc.sync.dma_start(
+                    out=scale_tile[32 * q : 32 * q + 4, :].bitcast(I32),
+                    in_=stacked[STACK + 4 * q : STACK + 4 * (q + 1), :].bitcast(I32),
+                )
 
         def load_packed_scales(scale_tile, scales):
             for group in range(F // PACKED):
@@ -83,10 +90,6 @@ def tile_moe_mlr_relu2_kernel(
 
         nc.sync.dma_start(list1[:], offs)
         nc.sync.dma_start(out=xs_stacked[STACK:, :T].bitcast(I32), in_=x_scales[0].bitcast(I32))
-        for q in range(QUADS):
-            nc.sync.dma_start(
-                out=xs[32 * q : 32 * q + 4, :T].bitcast(I32), in_=x_scales[0, 4 * q : 4 * q + 4, :].bitcast(I32)
-            )
         nc.sync.dma_start(out=xw[:, :T], in_=x_words[0].rearrange("p t d -> p (t d)").bitcast(I32))
         nc.sync.dma_start(list2[:], offs2)
         nc.sync.dma_start(out=ww[:].bitcast(I32), in_=w_words[:, 0].rearrange("e p b -> p e b").bitcast(I32))
@@ -96,24 +99,20 @@ def tile_moe_mlr_relu2_kernel(
                 in_=w_scales[:, 0, 4 * q : 4 * q + 4, :].rearrange("e r n -> r e n").bitcast(I32),
             )
         e_stacked = gather("e_stacked", xs_stacked[:], U8, list1[:])
-        for q in range(QUADS):
-            nc.sync.dma_start(
-                out=e_scales[32 * q : 32 * q + 4, :].bitcast(I32),
-                in_=e_stacked[STACK + 4 * q : STACK + 4 * (q + 1), :].bitcast(I32),
-            )
+        unstack(e_scales, e_stacked)
         nc.sync.dma_start(out=g1[:], in_=gate)
         load_packed_scales(a_s, wa_scales)
         load_words(aw, wa_words)
-        load_packed_scales(b_s, wb_scales)
-        load_words(bw, wb_words)
-        nc.sync.dma_start(out=g2[:], in_=gate2)
 
         make_identity(nc, ident[:])
 
         x_word_window = xw[:].bitcast(U32)
         e_words = gather("e_words", x_word_window, U32, list1[:])
-        a_scales = gather("a_scales", xs[:], U8, list2[:])
+        unstack(a_scales, gather("a_stacked", xs_stacked[:], U8, list2[:]))
         a_words = gather("a_words", x_word_window, U32, list2[:])
+        load_packed_scales(b_s, wb_scales)
+        load_words(bw, wb_words)
+        nc.sync.dma_start(out=g2[:], in_=gate2)
 
         def experts(j):
             ys = keep.tile([P, T], F32, name="ys%d" % j, tag="ys%d" % j)

@@ -27,6 +27,7 @@ STACK = P - 4 * QUADS
 LIST_COLS = T // 16
 WINDOW = 1408
 PIECE = 256
+ALIGN = 256
 
 
 def tile_moe_mlr_relu2_kernel(
@@ -39,20 +40,20 @@ def tile_moe_mlr_relu2_kernel(
         mm = ctx.enter_context(tc.psum_pool(name="mm", bufs=4))
         tr = ctx.enter_context(tc.psum_pool(name="tr", bufs=4))
 
-        list1 = keep.tile([P, LIST_COLS], U16, name="list1")
-        list2 = keep.tile([P, LIST_COLS], U16, name="list2")
-        xw = keep.tile([P, WINDOW], I32, name="xw", align_bytes=64)
-        xs_stacked = keep.tile([P, WINDOW], U8, name="xs_stacked", align_bytes=64)
-        e_scales = keep.tile([P, T], U8, name="e_scales", align_bytes=64)
-        a_scales = keep.tile([P, T], U8, name="a_scales", align_bytes=64)
-        ww = keep.tile([P, E, 2 * N], U8, name="ww", align_bytes=64)
-        ws = keep.tile([P, E, N], U8, name="ws", align_bytes=64)
-        aw = [keep.tile([P, 2, H], I32, name="aw%d" % i, align_bytes=64) for i in range(F // 2)]
-        bw = [keep.tile([P, PACKED, N], I32, name="bw%d" % i, align_bytes=64) for i in range(F // PACKED)]
-        a_s = keep.tile([P, F // PACKED, H], U8, name="a_s", align_bytes=64)
-        b_s = keep.tile([P, F // PACKED, N], U8, name="b_s", align_bytes=64)
-        g1 = keep.tile([P, T], F32, name="g1")
-        g2 = keep.tile([P, T], F32, name="g2")
+        list1 = keep.tile([P, LIST_COLS], U16, name="list1", align_bytes=ALIGN)
+        list2 = keep.tile([P, LIST_COLS], U16, name="list2", align_bytes=ALIGN)
+        xw = keep.tile([P, WINDOW], I32, name="xw", align_bytes=ALIGN)
+        xs_stacked = keep.tile([P, WINDOW], U8, name="xs_stacked", align_bytes=ALIGN)
+        e_scales = keep.tile([P, T], U8, name="e_scales", align_bytes=ALIGN)
+        a_scales = keep.tile([P, T], U8, name="a_scales", align_bytes=ALIGN)
+        ww = keep.tile([P, E, 2 * N], U8, name="ww", align_bytes=ALIGN)
+        ws = keep.tile([P, E, N], U8, name="ws", align_bytes=ALIGN)
+        aw = [keep.tile([P, 2, H], I32, name="aw%d" % i, align_bytes=ALIGN) for i in range(F // 2)]
+        bw = [keep.tile([P, PACKED, N], I32, name="bw%d" % i, align_bytes=ALIGN) for i in range(F // PACKED)]
+        a_s = keep.tile([P, F // PACKED, H], U8, name="a_s", align_bytes=ALIGN)
+        b_s = keep.tile([P, F // PACKED, N], U8, name="b_s", align_bytes=ALIGN)
+        g1 = keep.tile([P, T], F32, name="g1", align_bytes=ALIGN)
+        g2 = keep.tile([P, T], F32, name="g2", align_bytes=ALIGN)
         ident = keep.tile([P, P], F32, name="ident")
 
         nc.gpsimd.memset(xs_stacked[:STACK, :T].bitcast(I32), 0)
@@ -63,7 +64,7 @@ def tile_moe_mlr_relu2_kernel(
             nc.gpsimd.memset(scale_tile[:].rearrange("p e n -> p (e n)").bitcast(I32), 0)
 
         def gather(name, window, dtype, offsets):
-            picked = keep.tile([P, 16 * offsets.shape[1]], dtype, name=name, align_bytes=64)
+            picked = keep.tile([P, 16 * offsets.shape[1]], dtype, name=name, align_bytes=ALIGN)
             nc.vector.tensor_copy(picked[:], window.indirect(offsets))
             return picked
 
@@ -132,7 +133,7 @@ def tile_moe_mlr_relu2_kernel(
                 nc.scalar.copy(out=ys[:, BANK * half : BANK * (half + 1)], in_=acc[:])
             return ys
 
-        hb = keep.tile([P, T, 4], BF16, name="hb", align_bytes=64)
+        hb = keep.tile([P, T, 4], BF16, name="hb", align_bytes=ALIGN)
 
         def first_layer(f):
             group, u = divmod(f, PACKED)
@@ -162,8 +163,8 @@ def tile_moe_mlr_relu2_kernel(
             first_layer(f)
         ys.append(experts(LAST))
 
-        hw = keep.tile([P, T], U32, name="hw", align_bytes=64)
-        hs = keep.tile([P, T], U8, name="hs", align_bytes=64)
+        hw = keep.tile([P, T], U32, name="hw", align_bytes=ALIGN)
+        hs = keep.tile([P, T], U8, name="hs", align_bytes=ALIGN)
 
         def second_layer(j, zs):
             for half in range(2):
@@ -182,7 +183,7 @@ def tile_moe_mlr_relu2_kernel(
                 nc.scalar.copy(out=zs[:, BANK * half : BANK * (half + 1)], in_=acc[:])
 
         def scatter(name, offsets, values, weights):
-            window = keep.tile([P, WINDOW], F32, name=name, align_bytes=64)
+            window = keep.tile([P, WINDOW], F32, name=name, align_bytes=ALIGN)
             nc.vector.tensor_tensor(window[:].indirect(offsets[:]), values[:], weights[:], ALU.mult)
             return window
 
@@ -198,7 +199,7 @@ def tile_moe_mlr_relu2_kernel(
                         )
                 by_token.append(ring.tile([P, 4, P], F32, name="by_token"))
                 nc.scalar.copy(out=by_token[half][:], in_=total[:])
-            res = ring.tile([P, T], F32, name="res")
+            res = ring.tile([P, T], F32, name="res", align_bytes=ALIGN)
             for half in range(2):
                 back = tr.tile([P, 4, P], F32, name="turned")
                 for b in range(4):
@@ -209,7 +210,7 @@ def tile_moe_mlr_relu2_kernel(
         oy = [scatter("oy%d" % j, list1, ys[j], g1) for j in range(LAST)]
         nc.vector.quantize_mx(out=hw[:].bitcast(FP8X4), scales=hs[:], in_=hb[:].rearrange("p s t -> p (s t)"))
         oy.append(scatter("oy%d" % LAST, list1, ys[LAST], g1))
-        zs = [keep.tile([P, T], F32, name="zs%d" % j, align_bytes=64) for j in range(TILES)]
+        zs = [keep.tile([P, T], F32, name="zs%d" % j, align_bytes=ALIGN) for j in range(TILES)]
         for j in range(TILES):
             second_layer(j, zs[j])
         for j in range(LAST):
@@ -218,6 +219,6 @@ def tile_moe_mlr_relu2_kernel(
         oz_last = scatter("oz%d" % LAST, list2, zs[LAST], g2)
         for c in range(0, T, PIECE):
             cols = slice(c, c + PIECE)
-            piece = keep.tile([P, PIECE], F32, name="piece%d" % c)
+            piece = keep.tile([P, PIECE], F32, name="piece%d" % c, align_bytes=ALIGN)
             nc.vector.tensor_tensor(piece[:], oy[LAST][:, cols], oz_last[:, cols], ALU.add)
             nc.sync.dma_start(out=out[P * LAST : P * TILES, cols], in_=piece[:])

@@ -49,7 +49,7 @@ def tile_moe_mlr_relu2_kernel(
         ww = keep.tile([P, E, 2 * N], U8, name="ww", align_bytes=ALIGN)
         ws = keep.tile([P, E, N], U8, name="ws", align_bytes=ALIGN)
         aw = [keep.tile([P, 2, H], I32, name="aw%d" % i, align_bytes=ALIGN) for i in range(F // 2)]
-        bw = [keep.tile([P, PACKED, N], I32, name="bw%d" % i, align_bytes=ALIGN) for i in range(F // PACKED)]
+        bw = [keep.tile([P, 2, N], I32, name="bw%d" % i, align_bytes=ALIGN) for i in range(F // 2)]
         a_s = keep.tile([P, F // PACKED, H], U8, name="a_s", align_bytes=ALIGN)
         b_s = keep.tile([P, F // PACKED, N], U8, name="b_s", align_bytes=ALIGN)
         g1 = keep.tile([P, T], F32, name="g1", align_bytes=ALIGN)
@@ -173,7 +173,7 @@ def tile_moe_mlr_relu2_kernel(
                     f = PACKED * half + u
                     nc.tensor.matmul_mx(
                         out=acc[:, u * D : (u + 1) * D],
-                        lhsT=bw[half][:, u, P * j : P * (j + 1)].bitcast(FP8X4),
+                        lhsT=bw[f // 2][:, f % 2, P * j : P * (j + 1)].bitcast(FP8X4),
                         lhsT_scale=b_s[4 * u :, half, P * j : P * (j + 1)],
                         rhs=hw[:, D * f : D * (f + 1)].bitcast(FP8X4),
                         rhs_scale=hs[:, D * f : D * (f + 1)],

@@ -89,8 +89,8 @@ def tile_moe_mlr_relu2_kernel(
                 matrices = words[per_tile * i : per_tile * (i + 1), 0]
                 nc.sync.dma_start(out=word_tile[:], in_=matrices.rearrange("f p n d -> p f (n d)").bitcast(I32))
 
-        nc.sync.dma_start(list1[:], offs)
         nc.sync.dma_start(out=xs_stacked[STACK:, :T].bitcast(I32), in_=x_scales[0].bitcast(I32))
+        nc.sync.dma_start(list1[:], offs)
         nc.sync.dma_start(out=xw[:, :T], in_=x_words[0].rearrange("p t d -> p (t d)").bitcast(I32))
         nc.sync.dma_start(list2[:], offs2)
         nc.sync.dma_start(out=ww[:].bitcast(I32), in_=w_words[:, 0].rearrange("e p b -> p e b").bitcast(I32))

@@ -19,6 +19,8 @@ ALU = mybir.AluOpType
 
 P = 128
 BANK = 512
+BLOCKS = T // P
+PER_BANK = BANK // P
 TILES = N // P
 LAST = TILES - 1
 QUADS = 4
@@ -49,16 +51,17 @@ def tile_moe_mlr_relu2_kernel(
         ww = keep.tile([P, E, 2 * N], U8, name="ww", align_bytes=ALIGN)
         ws = keep.tile([P, E, N], U8, name="ws", align_bytes=ALIGN)
         aw = [keep.tile([P, 2, H], I32, name="aw%d" % i, align_bytes=ALIGN) for i in range(F // 2)]
-        bw = [keep.tile([P, 2, N], I32, name="bw%d" % i, align_bytes=ALIGN) for i in range(F // 2)]
+        bw = keep.tile([P, F, N], I32, name="bw", align_bytes=ALIGN)
         a_s = keep.tile([P, F // PACKED, H], U8, name="a_s", align_bytes=ALIGN)
         b_s = keep.tile([P, F // PACKED, N], U8, name="b_s", align_bytes=ALIGN)
-        g1 = keep.tile([P, T], F32, name="g1", align_bytes=ALIGN)
-        g2 = keep.tile([P, T], F32, name="g2", align_bytes=ALIGN)
-        ident = keep.tile([P, P], F32, name="ident")
+        gate_rows = keep.tile([P, P], F32, name="gate_rows", align_bytes=ALIGN)
+        gate_cols = keep.tile([P, 2 * BLOCKS], F32, name="gate_cols", align_bytes=ALIGN)
+        ident = keep.tile([P, P], F32, name="ident", align_bytes=ALIGN)
 
         nc.gpsimd.memset(xs_stacked[:STACK, :T].bitcast(I32), 0)
         nc.gpsimd.memset(ws[:].rearrange("p e n -> p (e n)").bitcast(I32), 0)
         nc.gpsimd.memset(e_scales[:].bitcast(I32), 0)
+        nc.gpsimd.memset(gate_rows[:STACK, :], 0.0)
         nc.gpsimd.memset(a_scales[:].bitcast(I32), 0)
         for scale_tile in (a_s, b_s):
             nc.gpsimd.memset(scale_tile[:].rearrange("p e n -> p (e n)").bitcast(I32), 0)
@@ -99,38 +102,62 @@ def tile_moe_mlr_relu2_kernel(
                 out=ws[32 * q : 32 * q + 4, :, :].bitcast(I32),
                 in_=w_scales[:, 0, 4 * q : 4 * q + 4, :].rearrange("e r n -> r e n").bitcast(I32),
             )
+        for i, weights in enumerate((gate, gate2)):
+            first = STACK + BLOCKS * i
+            nc.sync.dma_start(out=gate_rows[first : first + BLOCKS, :], in_=weights[0].rearrange("(b s) -> b s", s=P))
         e_stacked = gather("e_stacked", xs_stacked[:], U8, list1[:])
         unstack(e_scales, e_stacked)
-        nc.sync.dma_start(out=g1[:], in_=gate)
         load_packed_scales(a_s, wa_scales)
         load_words(aw, wa_words)
 
         make_identity(nc, ident[:])
+        gates_turned = tr.tile([P, PER_BANK, P], F32, name="turned")
+        nc.tensor.transpose(gates_turned[:, 0, :], gate_rows[:], ident[:])
+        nc.scalar.copy(out=gate_cols[:], in_=gates_turned[:, 0, STACK:])
 
         x_word_window = xw[:].bitcast(U32)
         e_words = gather("e_words", x_word_window, U32, list1[:])
         unstack(a_scales, gather("a_stacked", xs_stacked[:], U8, list2[:]))
         a_words = gather("a_words", x_word_window, U32, list2[:])
         load_packed_scales(b_s, wb_scales)
-        load_words(bw, wb_words)
-        nc.sync.dma_start(out=g2[:], in_=gate2)
+        load_words([bw], wb_words)
 
-        def experts(j):
-            ys = keep.tile([P, T], F32, name="ys%d" % j, tag="ys%d" % j)
+        def gated_tile(result, words, scales, weights, first_gate):
+            gated = []
             for half in range(2):
-                acc = mm.tile([P, BANK], F32, name="acc")
-                for u in range(BANK // C):
-                    e = BANK // C * half + u
+                acc = mm.tile([P, PER_BANK, P], F32, name="acc")
+                for u in range(PER_BANK):
+                    b = PER_BANK * half + u
+                    rhs, rhs_scale = weights(b)
                     nc.tensor.matmul_mx(
-                        out=acc[:, u * C : (u + 1) * C],
-                        lhsT=ww[:, e, 2 * P * j : 2 * P * (j + 1)].bitcast(FP4X4),
-                        lhsT_scale=ws[:, e, P * j : P * (j + 1)],
-                        rhs=e_words[:, e * C : (e + 1) * C].bitcast(FP8X4),
-                        rhs_scale=e_scales[:, e * C : (e + 1) * C],
+                        out=acc[:, u, :],
+                        lhsT=words[:, P * b : P * (b + 1)].bitcast(FP8X4),
+                        lhsT_scale=scales[:, P * b : P * (b + 1)],
+                        rhs=rhs,
+                        rhs_scale=rhs_scale,
                         start=True,
                         stop=True,
                     )
-                nc.scalar.copy(out=ys[:, BANK * half : BANK * (half + 1)], in_=acc[:])
+                gated.append(ring.tile([P, PER_BANK, P], F32, name="by_slot", align_bytes=ALIGN))
+                for u in range(PER_BANK):
+                    g = first_gate + PER_BANK * half + u
+                    nc.scalar.activation(
+                        out=gated[half][:, u, :], in_=acc[:, u, :], func=ACT.Copy, scale=gate_cols[:, g : g + 1]
+                    )
+            for half in range(2):
+                turned = tr.tile([P, PER_BANK, P], F32, name="turned")
+                for u in range(PER_BANK):
+                    nc.tensor.transpose(turned[:, u, :], gated[half][:, u, :], ident[:])
+                nc.scalar.copy(out=result[:, BANK * half : BANK * (half + 1)], in_=turned[:].rearrange("p b s -> p (b s)"))
+
+        def experts(j):
+            ys = keep.tile([P, T], F32, name="ys%d" % j, tag="ys%d" % j, align_bytes=ALIGN)
+
+            def weights(b):
+                e = P * b // C
+                return ww[:, e, 2 * P * j : 2 * P * (j + 1)].bitcast(FP4X4), ws[:, e, P * j : P * (j + 1)]
+
+            gated_tile(ys, e_words, e_scales, weights, 0)
             return ys
 
         hb = keep.tile([P, T, 4], BF16, name="hb", align_bytes=ALIGN)
@@ -149,9 +176,9 @@ def tile_moe_mlr_relu2_kernel(
                 stop=True,
             )
             if f < F - 1:
-                pos = ring.tile([P, 4, P], F32, name="pos")
+                pos = ring.tile([P, 4, P], F32, name="by_slot", align_bytes=ALIGN)
             else:
-                pos = keep.tile([P, 4, P], F32, name="pos_last", tag="ys%d" % LAST)
+                pos = keep.tile([P, 4, P], F32, name="pos_last", tag="ys%d" % LAST, align_bytes=ALIGN)
             nc.scalar.activation(out=pos[:], in_=acc[:].rearrange("p (m t) -> p t m", t=4), func=ACT.Relu)
             turned = tr.tile([P, 4, P], F32, name="turned")
             for t in range(4):
@@ -166,57 +193,32 @@ def tile_moe_mlr_relu2_kernel(
         hw = keep.tile([P, T], U32, name="hw", align_bytes=ALIGN)
         hs = keep.tile([P, T], U8, name="hs", align_bytes=ALIGN)
 
-        def second_layer(j, zs):
-            for half in range(2):
-                acc = mm.tile([P, BANK], F32, name="acc")
-                for u in range(PACKED):
-                    f = PACKED * half + u
-                    nc.tensor.matmul_mx(
-                        out=acc[:, u * D : (u + 1) * D],
-                        lhsT=bw[f // 2][:, f % 2, P * j : P * (j + 1)].bitcast(FP8X4),
-                        lhsT_scale=b_s[4 * u :, half, P * j : P * (j + 1)],
-                        rhs=hw[:, D * f : D * (f + 1)].bitcast(FP8X4),
-                        rhs_scale=hs[:, D * f : D * (f + 1)],
-                        start=True,
-                        stop=True,
-                    )
-                nc.scalar.copy(out=zs[:, BANK * half : BANK * (half + 1)], in_=acc[:])
+        def second_layer(j):
+            zs = keep.tile([P, T], F32, name="zs%d" % j, align_bytes=ALIGN)
 
-        def scatter(name, offsets, values, weights):
+            def weights(f):
+                group, u = divmod(f, PACKED)
+                return bw[:, f, P * j : P * (j + 1)].bitcast(FP8X4), b_s[4 * u :, group, P * j : P * (j + 1)]
+
+            gated_tile(zs, hw, hs, weights, BLOCKS)
+            return zs
+
+        def scatter(name, offsets, values):
             window = keep.tile([P, WINDOW], F32, name=name, align_bytes=ALIGN)
-            nc.vector.tensor_tensor(window[:].indirect(offsets[:]), values[:], weights[:], ALU.mult)
+            nc.vector.tensor_copy(window[:].indirect(offsets[:]), values[:])
             return window
 
-        def add_on_tensor(j, oy_tile, oz_tile):
-            by_token = []
-            for half in range(2):
-                total = tr.tile([P, 4, P], F32, name="turned")
-                for b in range(4):
-                    cols = slice(BANK * half + P * b, BANK * half + P * (b + 1))
-                    for addend, first in ((oy_tile, True), (oz_tile, False)):
-                        nc.tensor.matmul(
-                            total[:, b, :], addend[:, cols], ident[:], start=first, stop=not first, is_transpose=True
-                        )
-                by_token.append(ring.tile([P, 4, P], F32, name="by_token"))
-                nc.scalar.copy(out=by_token[half][:], in_=total[:])
-            res = ring.tile([P, T], F32, name="res", align_bytes=ALIGN)
-            for half in range(2):
-                back = tr.tile([P, 4, P], F32, name="turned")
-                for b in range(4):
-                    nc.tensor.transpose(back[:, b, :], by_token[half][:, b, :], ident[:])
-                nc.scalar.copy(out=res[:, BANK * half : BANK * (half + 1)], in_=back[:].rearrange("p b t -> p (b t)"))
-            nc.scalar.dma_start(out=out[P * j : P * (j + 1), :], in_=res[:])
-
-        oy = [scatter("oy%d" % j, list1, ys[j], g1) for j in range(LAST)]
+        oy = [scatter("oy%d" % j, list1, ys[j]) for j in range(LAST)]
         nc.vector.quantize_mx(out=hw[:].bitcast(FP8X4), scales=hs[:], in_=hb[:].rearrange("p s t -> p (s t)"))
-        oy.append(scatter("oy%d" % LAST, list1, ys[LAST], g1))
-        zs = [keep.tile([P, T], F32, name="zs%d" % j, align_bytes=ALIGN) for j in range(TILES)]
-        for j in range(TILES):
-            second_layer(j, zs[j])
+        oy.append(scatter("oy%d" % LAST, list1, ys[LAST]))
+        zs = [second_layer(j) for j in range(TILES)]
         for j in range(LAST):
-            add_on_tensor(j, oy[j], scatter("oz%d" % j, list2, zs[j], g2))
+            oz = scatter("oz%d" % j, list2, zs[j])
+            res = keep.tile([P, T], F32, name="res%d" % j, align_bytes=ALIGN)
+            nc.gpsimd.tensor_tensor(res[:], oy[j][:, :T], oz[:, :T], ALU.add)
+            nc.sync.dma_start(out=out[P * j : P * (j + 1), :], in_=res[:])
 
-        oz_last = scatter("oz%d" % LAST, list2, zs[LAST], g2)
+        oz_last = scatter("oz%d" % LAST, list2, zs[LAST])
         for c in range(0, T, PIECE):
             cols = slice(c, c + PIECE)
             piece = keep.tile([P, PIECE], F32, name="piece%d" % c, align_bytes=ALIGN)

@@ -19,8 +19,6 @@ ALU = mybir.AluOpType
 
 P = 128
 BANK = 512
-BLOCKS = T // P
-PER_BANK = BANK // P
 TILES = N // P
 LAST = TILES - 1
 QUADS = 4
@@ -28,6 +26,8 @@ PACKED = 4
 STACK = P - 4 * QUADS
 LIST_COLS = T // 16
 WINDOW = 1408
+EARLY = 2 * D
+ACT_PIECE = 384
 PIECE = 256
 ALIGN = 256
 
@@ -42,32 +42,42 @@ def tile_moe_mlr_relu2_kernel(
         mm = ctx.enter_context(tc.psum_pool(name="mm", bufs=4))
         tr = ctx.enter_context(tc.psum_pool(name="tr", bufs=4))
 
-        list1 = keep.tile([P, LIST_COLS], U16, name="list1", align_bytes=ALIGN)
-        list2 = keep.tile([P, LIST_COLS], U16, name="list2", align_bytes=ALIGN)
-        xw = keep.tile([P, WINDOW], I32, name="xw", align_bytes=ALIGN)
-        xs_stacked = keep.tile([P, WINDOW], U8, name="xs_stacked", align_bytes=ALIGN)
-        e_scales = keep.tile([P, T], U8, name="e_scales", align_bytes=ALIGN)
-        a_scales = keep.tile([P, T], U8, name="a_scales", align_bytes=ALIGN)
-        ww = keep.tile([P, E, 2 * N], U8, name="ww", align_bytes=ALIGN)
-        ws = keep.tile([P, E, N], U8, name="ws", align_bytes=ALIGN)
-        aw = [keep.tile([P, 2, H], I32, name="aw%d" % i, align_bytes=ALIGN) for i in range(F // 2)]
-        bw = keep.tile([P, F, N], I32, name="bw", align_bytes=ALIGN)
-        a_s = keep.tile([P, F // PACKED, H], U8, name="a_s", align_bytes=ALIGN)
-        b_s = keep.tile([P, F // PACKED, N], U8, name="b_s", align_bytes=ALIGN)
-        gate_rows = keep.tile([P, P], F32, name="gate_rows", align_bytes=ALIGN)
-        gate_cols = keep.tile([P, 2 * BLOCKS], F32, name="gate_cols", align_bytes=ALIGN)
-        ident = keep.tile([P, P], F32, name="ident", align_bytes=ALIGN)
+        def kept(name, shape, dtype, tag=None):
+            return keep.tile(shape, dtype, name=name, tag=tag or name, align_bytes=ALIGN)
+
+        list1 = kept("list1", [P, LIST_COLS], U16)
+        list2 = kept("list2", [P, LIST_COLS], U16)
+        xw = kept("xw", [P, WINDOW], I32)
+        xs_stacked = kept("xs_stacked", [P, WINDOW], U8)
+        a_parts = ((0, EARLY), (EARLY, T))
+        a_scales = [kept("a_scales%d" % i, [P, b - a], U8) for i, (a, b) in enumerate(a_parts)]
+        e_scales = kept("e_scales", [P, T], U8)
+        ww = kept("ww", [P, E, 2 * N], U8)
+        ws = kept("ws", [P, E, N], U8)
+        aw = [kept("aw%d" % i, [P, 2, H], I32) for i in range(F // 2)]
+        bw = kept("bw", [P, F, N], I32)
+        a_s = [kept("a_s%d" % g, [P, H], U8) for g in range(F // PACKED)]
+        b_s = [kept("b_s%d" % g, [P, N], U8) for g in range(F // PACKED)]
+        g1 = kept("g1", [P, T], F32)
+        g2 = kept("g2", [P, T], F32)
+        ident = kept("ident", [P, P], F32)
 
         nc.gpsimd.memset(xs_stacked[:STACK, :T].bitcast(I32), 0)
-        nc.gpsimd.memset(ws[:].rearrange("p e n -> p (e n)").bitcast(I32), 0)
+        nc.gpsimd.memset(a_s[0][:].bitcast(I32), 0)
+        nc.gpsimd.memset(a_scales[0][:].bitcast(I32), 0)
+        make_identity(nc, ident[:])
+        nc.gpsimd.memset(a_scales[1][:].bitcast(I32), 0)
+        nc.gpsimd.memset(a_s[1][:].bitcast(I32), 0)
         nc.gpsimd.memset(e_scales[:].bitcast(I32), 0)
-        nc.gpsimd.memset(gate_rows[:STACK, :], 0.0)
-        nc.gpsimd.memset(a_scales[:].bitcast(I32), 0)
-        for scale_tile in (a_s, b_s):
-            nc.gpsimd.memset(scale_tile[:].rearrange("p e n -> p (e n)").bitcast(I32), 0)
+        nc.gpsimd.memset(ws[:].rearrange("p e n -> p (e n)").bitcast(I32), 0)
+        for scale_tile in b_s:
+            nc.gpsimd.memset(scale_tile[:].bitcast(I32), 0)
+
+        def entries(offsets, first, end):
+            return offsets[:, first // 16 : end // 16]
 
         def gather(name, window, dtype, offsets):
-            picked = keep.tile([P, 16 * offsets.shape[1]], dtype, name=name, align_bytes=ALIGN)
+            picked = kept(name, [P, 16 * offsets.shape[1]], dtype)
             nc.vector.tensor_copy(picked[:], window.indirect(offsets))
             return picked
 
@@ -78,149 +88,160 @@ def tile_moe_mlr_relu2_kernel(
                     in_=stacked[STACK + 4 * q : STACK + 4 * (q + 1), :].bitcast(I32),
                 )
 
-        def load_packed_scales(scale_tile, scales):
-            for group in range(F // PACKED):
-                for q in range(QUADS):
-                    nc.sync.dma_start(
-                        out=scale_tile[32 * q : 32 * q + 4 * PACKED, group, :].bitcast(I32),
-                        in_=scales[PACKED * group : PACKED * (group + 1), 0, 4 * q : 4 * q + 4, :].bitcast(I32),
-                    )
+        def load_packed_scales(scale_tile, scales, group):
+            for q in range(QUADS):
+                nc.sync.dma_start(
+                    out=scale_tile[32 * q : 32 * q + 4 * PACKED, :].bitcast(I32),
+                    in_=scales[PACKED * group : PACKED * (group + 1), 0, 4 * q : 4 * q + 4, :].bitcast(I32),
+                )
 
-        def load_words(word_tiles, words):
-            per_tile = F // len(word_tiles)
-            for i, word_tile in enumerate(word_tiles):
-                matrices = words[per_tile * i : per_tile * (i + 1), 0]
-                nc.sync.dma_start(out=word_tile[:], in_=matrices.rearrange("f p n d -> p f (n d)").bitcast(I32))
+        def load_words(word_tile, words, first):
+            matrices = words[first : first + word_tile.shape[1], 0]
+            nc.sync.dma_start(out=word_tile[:], in_=matrices.rearrange("f p n d -> p f (n d)").bitcast(I32))
 
+        x_word_window = xw[:].bitcast(U32)
         nc.sync.dma_start(out=xs_stacked[STACK:, :T].bitcast(I32), in_=x_scales[0].bitcast(I32))
-        nc.sync.dma_start(list1[:], offs)
-        nc.sync.dma_start(out=xw[:, :T], in_=x_words[0].rearrange("p t d -> p (t d)").bitcast(I32))
         nc.sync.dma_start(list2[:], offs2)
+        nc.sync.dma_start(out=xw[:, :T], in_=x_words[0].rearrange("p t d -> p (t d)").bitcast(I32))
+        load_words(aw[0], wa_words, 0)
+        load_packed_scales(a_s[0], wa_scales, 0)
+        nc.sync.dma_start(list1[:], offs)
+        a_words = []
+        for i, (a, b) in enumerate(a_parts):
+            unstack(a_scales[i], gather("a_stacked%d" % i, xs_stacked[:], U8, entries(list2, a, b)))
+            a_words.append(gather("a_words%d" % i, x_word_window, U32, entries(list2, a, b)))
+            load_words(aw[i + 1], wa_words, 2 * (i + 1))
+        load_packed_scales(a_s[1], wa_scales, 1)
+        load_words(aw[3], wa_words, 6)
+        unstack(e_scales, gather("e_stacked", xs_stacked[:], U8, list1[:]))
+        e_words = gather("e_words", x_word_window, U32, list1[:])
         nc.sync.dma_start(out=ww[:].bitcast(I32), in_=w_words[:, 0].rearrange("e p b -> p e b").bitcast(I32))
         for q in range(QUADS):
             nc.sync.dma_start(
                 out=ws[32 * q : 32 * q + 4, :, :].bitcast(I32),
                 in_=w_scales[:, 0, 4 * q : 4 * q + 4, :].rearrange("e r n -> r e n").bitcast(I32),
             )
-        for i, weights in enumerate((gate, gate2)):
-            first = STACK + BLOCKS * i
-            nc.sync.dma_start(out=gate_rows[first : first + BLOCKS, :], in_=weights[0].rearrange("(b s) -> b s", s=P))
-        e_stacked = gather("e_stacked", xs_stacked[:], U8, list1[:])
-        unstack(e_scales, e_stacked)
-        load_packed_scales(a_s, wa_scales)
-        load_words(aw, wa_words)
+        nc.sync.dma_start(out=g1[:], in_=gate)
+        for group in range(F // PACKED):
+            load_packed_scales(b_s[group], wb_scales, group)
+        load_words(bw, wb_words, 0)
+        nc.sync.dma_start(out=g2[:], in_=gate2)
 
-        make_identity(nc, ident[:])
-        gates_turned = tr.tile([P, PER_BANK, P], F32, name="turned")
-        nc.tensor.transpose(gates_turned[:, 0, :], gate_rows[:], ident[:])
-        nc.scalar.copy(out=gate_cols[:], in_=gates_turned[:, 0, STACK:])
-
-        x_word_window = xw[:].bitcast(U32)
-        e_words = gather("e_words", x_word_window, U32, list1[:])
-        unstack(a_scales, gather("a_stacked", xs_stacked[:], U8, list2[:]))
-        a_words = gather("a_words", x_word_window, U32, list2[:])
-        load_packed_scales(b_s, wb_scales)
-        load_words([bw], wb_words)
-
-        def gated_tile(result, words, scales, weights, first_gate):
-            gated = []
-            for half in range(2):
-                acc = mm.tile([P, PER_BANK, P], F32, name="acc")
-                for u in range(PER_BANK):
-                    b = PER_BANK * half + u
-                    rhs, rhs_scale = weights(b)
-                    nc.tensor.matmul_mx(
-                        out=acc[:, u, :],
-                        lhsT=words[:, P * b : P * (b + 1)].bitcast(FP8X4),
-                        lhsT_scale=scales[:, P * b : P * (b + 1)],
-                        rhs=rhs,
-                        rhs_scale=rhs_scale,
-                        start=True,
-                        stop=True,
-                    )
-                gated.append(ring.tile([P, PER_BANK, P], F32, name="by_slot", align_bytes=ALIGN))
-                for u in range(PER_BANK):
-                    g = first_gate + PER_BANK * half + u
-                    nc.scalar.activation(
-                        out=gated[half][:, u, :], in_=acc[:, u, :], func=ACT.Copy, scale=gate_cols[:, g : g + 1]
-                    )
-            for half in range(2):
-                turned = tr.tile([P, PER_BANK, P], F32, name="turned")
-                for u in range(PER_BANK):
-                    nc.tensor.transpose(turned[:, u, :], gated[half][:, u, :], ident[:])
-                nc.scalar.copy(out=result[:, BANK * half : BANK * (half + 1)], in_=turned[:].rearrange("p b s -> p (b s)"))
-
-        def experts(j):
-            ys = keep.tile([P, T], F32, name="ys%d" % j, tag="ys%d" % j, align_bytes=ALIGN)
-
-            def weights(b):
-                e = P * b // C
-                return ww[:, e, 2 * P * j : 2 * P * (j + 1)].bitcast(FP4X4), ws[:, e, P * j : P * (j + 1)]
-
-            gated_tile(ys, e_words, e_scales, weights, 0)
-            return ys
-
-        hb = keep.tile([P, T, 4], BF16, name="hb", align_bytes=ALIGN)
+        hb = [kept("hb%d" % half, [P, BANK, 4], BF16) for half in range(2)]
+        hw = [kept("hw%d" % half, [P, BANK], U32) for half in range(2)]
+        hs = [kept("hs%d" % half, [P, BANK], U8) for half in range(2)]
 
         def first_layer(f):
             group, u = divmod(f, PACKED)
-            slots = slice(f * D, (f + 1) * D)
+            part = 0 if f * D < EARLY else 1
+            first = f * D - a_parts[part][0]
             acc = mm.tile([P, BANK], F32, name="acc")
             nc.tensor.matmul_mx(
                 out=acc[:],
-                lhsT=a_words[:, slots].bitcast(FP8X4),
-                lhsT_scale=a_scales[:, slots],
+                lhsT=a_words[part][:, first : first + D].bitcast(FP8X4),
+                lhsT_scale=a_scales[part][:, first : first + D],
                 rhs=aw[f // 2][:, f % 2, :].bitcast(FP8X4),
-                rhs_scale=a_s[4 * u :, group, :],
+                rhs_scale=a_s[group][4 * u :, :],
                 start=True,
                 stop=True,
             )
-            if f < F - 1:
-                pos = ring.tile([P, 4, P], F32, name="by_slot", align_bytes=ALIGN)
-            else:
-                pos = keep.tile([P, 4, P], F32, name="pos_last", tag="ys%d" % LAST, align_bytes=ALIGN)
+            pos = ring.tile([P, 4, P], F32, name="pos", align_bytes=ALIGN)
             nc.scalar.activation(out=pos[:], in_=acc[:].rearrange("p (m t) -> p t m", t=4), func=ACT.Relu)
             turned = tr.tile([P, 4, P], F32, name="turned")
             for t in range(4):
                 nc.tensor.transpose(turned[:, t, :], pos[:, t, :], ident[:])
-            nc.scalar.activation(out=hb[:, slots, :], in_=turned[:].rearrange("p t s -> p s t"), func=ACT.Square)
+            nc.scalar.activation(
+                out=hb[group][:, u * D : (u + 1) * D, :], in_=turned[:].rearrange("p t s -> p s t"), func=ACT.Square
+            )
 
-        ys = [experts(j) for j in range(LAST)]
-        for f in range(F):
-            first_layer(f)
-        ys.append(experts(LAST))
+        def quantize(half):
+            nc.vector.quantize_mx(
+                out=hw[half][:].bitcast(FP8X4), scales=hs[half][:], in_=hb[half][:].rearrange("p s t -> p (s t)")
+            )
 
-        hw = keep.tile([P, T], U32, name="hw", align_bytes=ALIGN)
-        hs = keep.tile([P, T], U8, name="hs", align_bytes=ALIGN)
+        ys = [kept("ys%d" % j, [P, T], F32) for j in range(TILES)]
+        zs = [kept("zs%d" % j, [P, T], F32) for j in range(TILES)]
 
-        def second_layer(j):
-            zs = keep.tile([P, T], F32, name="zs%d" % j, align_bytes=ALIGN)
+        def gated(result, acc, weights, half):
+            cols = slice(BANK * half, BANK * (half + 1))
+            nc.vector.tensor_tensor(result[:, cols], acc[:], weights[:, cols], ALU.mult)
 
-            def weights(f):
-                group, u = divmod(f, PACKED)
-                return bw[:, f, P * j : P * (j + 1)].bitcast(FP8X4), b_s[4 * u :, group, P * j : P * (j + 1)]
+        def experts(j, half):
+            acc = mm.tile([P, BANK], F32, name="acc")
+            for u in range(BANK // C):
+                e = half * BANK // C + u
+                nc.tensor.matmul_mx(
+                    out=acc[:, C * u : C * (u + 1)],
+                    lhsT=ww[:, e, 2 * P * j : 2 * P * (j + 1)].bitcast(FP4X4),
+                    lhsT_scale=ws[:, e, P * j : P * (j + 1)],
+                    rhs=e_words[:, C * e : C * (e + 1)].bitcast(FP8X4),
+                    rhs_scale=e_scales[:, C * e : C * (e + 1)],
+                    start=True,
+                    stop=True,
+                )
+            gated(ys[j], acc, g1, half)
 
-            gated_tile(zs, hw, hs, weights, BLOCKS)
-            return zs
+        def second_layer(j, half):
+            acc = mm.tile([P, BANK], F32, name="acc")
+            for u in range(PACKED):
+                nc.tensor.matmul_mx(
+                    out=acc[:, D * u : D * (u + 1)],
+                    lhsT=bw[:, PACKED * half + u, P * j : P * (j + 1)].bitcast(FP8X4),
+                    lhsT_scale=b_s[half][4 * u :, P * j : P * (j + 1)],
+                    rhs=hw[half][:, D * u : D * (u + 1)].bitcast(FP8X4),
+                    rhs_scale=hs[half][:, D * u : D * (u + 1)],
+                    start=True,
+                    stop=True,
+                )
+            gated(zs[j], acc, g2, half)
 
-        def scatter(name, offsets, values):
-            window = keep.tile([P, WINDOW], F32, name=name, align_bytes=ALIGN)
-            nc.vector.tensor_copy(window[:].indirect(offsets[:]), values[:])
-            return window
+        def vector_scatter(window, offsets, values, first, end):
+            nc.vector.tensor_copy(window[:].indirect(entries(offsets, first, end)), values[:, first:end])
 
-        oy = [scatter("oy%d" % j, list1, ys[j]) for j in range(LAST)]
-        nc.vector.quantize_mx(out=hw[:].bitcast(FP8X4), scales=hs[:], in_=hb[:].rearrange("p s t -> p (s t)"))
-        oy.append(scatter("oy%d" % LAST, list1, ys[LAST]))
-        zs = [second_layer(j) for j in range(TILES)]
-        for j in range(LAST):
-            oz = scatter("oz%d" % j, list2, zs[j])
-            res = keep.tile([P, T], F32, name="res%d" % j, align_bytes=ALIGN)
-            nc.gpsimd.tensor_tensor(res[:], oy[j][:, :T], oz[:, :T], ALU.add)
+        def scalar_scatter(window, offsets, values, first, end):
+            nc.scalar.activation(
+                out=window[:].indirect(entries(offsets, first, end)), in_=values[:, first:end], func=ACT.Copy
+            )
+
+        def scalar_pair(windows, offsets, values):
+            for first in range(0, T, ACT_PIECE):
+                for j in range(2):
+                    scalar_scatter(windows[j], offsets, values[j], first, min(first + ACT_PIECE, T))
+
+        def add_and_store(j):
+            res = kept("res%d" % j, [P, T], F32)
+            nc.gpsimd.tensor_tensor(res[:], oy[j][:, :T], oz[j][:, :T], ALU.add)
             nc.sync.dma_start(out=out[P * j : P * (j + 1), :], in_=res[:])
 
-        oz_last = scatter("oz%d" % LAST, list2, zs[LAST])
+        for f in range(F):
+            first_layer(f)
+        for pair in range(2):
+            for half in range(2):
+                for j in (2 * pair, 2 * pair + 1):
+                    experts(j, half)
+            quantize(pair)
+        oy = [kept("oy%d" % j, [P, WINDOW], F32) for j in range(2)]
+        oz = [kept("oz%d" % j, [P, WINDOW], F32) for j in range(TILES)]
+        scalar_pair(oy, list1, ys)
+        for half in range(2):
+            for j in range(TILES):
+                second_layer(j, half)
+        scalar_pair(oz, list2, zs)
+
+        vector_scatter(oz[2], list2, zs[2], 0, T)
+        oy.append(kept("oy2", [P, WINDOW], F32, tag="hw1"))
+        vector_scatter(oy[2], list1, ys[2], 0, T)
+        oy.append(kept("oy3", [P, WINDOW], F32, tag="zs2"))
+        vector_scatter(oy[LAST], list1, ys[LAST], 0, ACT_PIECE)
+        middle = (ACT_PIECE + T) // 2
+        scalar_scatter(oy[LAST], list1, ys[LAST], ACT_PIECE, middle)
+        scalar_scatter(oy[LAST], list1, ys[LAST], middle, T)
+        vector_scatter(oz[LAST], list2, zs[LAST], 0, T)
+        for j in (2, 0, 1):
+            add_and_store(j)
+
         for c in range(0, T, PIECE):
             cols = slice(c, c + PIECE)
-            piece = keep.tile([P, PIECE], F32, name="piece%d" % c, align_bytes=ALIGN)
-            nc.vector.tensor_tensor(piece[:], oy[LAST][:, cols], oz_last[:, cols], ALU.add)
+            piece = kept("piece%d" % c, [P, PIECE], F32)
+            nc.vector.tensor_tensor(piece[:], oy[LAST][:, cols], oz[LAST][:, cols], ALU.add)
             nc.sync.dma_start(out=out[P * LAST : P * TILES, cols], in_=piece[:])

@@ -20,10 +20,9 @@ ALU = mybir.AluOpType
 P = 128
 BANK = 512
 TILES = N // P
-LAST = TILES - 1
 QUADS = 4
 PACKED = 4
-STACK = P - 4 * QUADS
+A_ROW, B_ROW = 4, 8
 LIST_COLS = T // 16
 WINDOW = 1408
 EARLY = 2 * D
@@ -38,9 +37,9 @@ def tile_moe_mlr_relu2_kernel(
     nc = tc.nc
     with ExitStack() as ctx:
         keep = ctx.enter_context(tc.tile_pool(name="keep", bufs=1))
-        ring = ctx.enter_context(tc.tile_pool(name="ring", bufs=3))
-        mm = ctx.enter_context(tc.psum_pool(name="mm", bufs=4))
-        tr = ctx.enter_context(tc.psum_pool(name="tr", bufs=4))
+        ring = ctx.enter_context(tc.tile_pool(name="ring", bufs=F))
+        sums = ctx.enter_context(tc.tile_pool(name="sums", bufs=2))
+        mm = ctx.enter_context(tc.psum_pool(name="mm", bufs=6))
 
         def kept(name, shape, dtype, tag=None):
             return keep.tile(shape, dtype, name=name, tag=tag or name, align_bytes=ALIGN)
@@ -48,51 +47,39 @@ def tile_moe_mlr_relu2_kernel(
         list1 = kept("list1", [P, LIST_COLS], U16)
         list2 = kept("list2", [P, LIST_COLS], U16)
         xw = kept("xw", [P, WINDOW], I32)
-        xs_stacked = kept("xs_stacked", [P, WINDOW], U8)
+        xs = kept("xs", [P, WINDOW], U8)
         a_parts = ((0, EARLY), (EARLY, T))
-        a_scales = [kept("a_scales%d" % i, [P, b - a], U8) for i, (a, b) in enumerate(a_parts)]
-        e_scales = kept("e_scales", [P, T], U8)
         ww = kept("ww", [P, E, 2 * N], U8)
-        ws = kept("ws", [P, E, N], U8)
+        ws = kept("ws", [P, E * N + 4], U8)
         aw = [kept("aw%d" % i, [P, 2, H], I32) for i in range(F // 2)]
-        bw = kept("bw", [P, F, N], I32)
-        a_s = [kept("a_s%d" % g, [P, H], U8) for g in range(F // PACKED)]
-        b_s = [kept("b_s%d" % g, [P, N], U8) for g in range(F // PACKED)]
+        bw = [kept("bw%d" % half, [P, PACKED, N], I32) for half in range(2)]
+        a_s = kept("a_s", [P, F * H], U8)
+        b_s = kept("b_s", [P, F * N], U8)
         g1 = kept("g1", [P, T], F32)
         g2 = kept("g2", [P, T], F32)
         ident = kept("ident", [P, P], F32)
 
-        nc.gpsimd.memset(xs_stacked[:STACK, :T].bitcast(I32), 0)
-        nc.gpsimd.memset(a_s[0][:].bitcast(I32), 0)
-        nc.gpsimd.memset(a_scales[0][:].bitcast(I32), 0)
+        nc.gpsimd.memset(xs[:, :T].bitcast(I32), 0)
+        nc.gpsimd.memset(a_s[:].bitcast(I32), 0)
         make_identity(nc, ident[:])
-        nc.gpsimd.memset(a_scales[1][:].bitcast(I32), 0)
-        nc.gpsimd.memset(a_s[1][:].bitcast(I32), 0)
-        nc.gpsimd.memset(e_scales[:].bitcast(I32), 0)
-        nc.gpsimd.memset(ws[:].rearrange("p e n -> p (e n)").bitcast(I32), 0)
-        for scale_tile in b_s:
-            nc.gpsimd.memset(scale_tile[:].bitcast(I32), 0)
+        nc.vector.memset(ws[:].bitcast(I32), 0)
+        nc.gpsimd.memset(b_s[:].bitcast(I32), 0)
 
         def entries(offsets, first, end):
             return offsets[:, first // 16 : end // 16]
 
-        def gather(name, window, dtype, offsets):
-            picked = kept(name, [P, 16 * offsets.shape[1]], dtype)
+        def gather(name, window, dtype, offsets, tag=None):
+            picked = kept(name, [P, 16 * offsets.shape[1]], dtype, tag)
             nc.vector.tensor_copy(picked[:], window.indirect(offsets))
             return picked
 
-        def unstack(scale_tile, stacked):
+        def load_scales(scale_tile, row, scales):
+            matrices, width = scales.shape[0], scales.shape[3]
             for q in range(QUADS):
+                rows = scale_tile[32 * q + row : 32 * q + row + 4, : matrices * width]
                 nc.sync.dma_start(
-                    out=scale_tile[32 * q : 32 * q + 4, :].bitcast(I32),
-                    in_=stacked[STACK + 4 * q : STACK + 4 * (q + 1), :].bitcast(I32),
-                )
-
-        def load_packed_scales(scale_tile, scales, group):
-            for q in range(QUADS):
-                nc.sync.dma_start(
-                    out=scale_tile[32 * q : 32 * q + 4 * PACKED, :].bitcast(I32),
-                    in_=scales[PACKED * group : PACKED * (group + 1), 0, 4 * q : 4 * q + 4, :].bitcast(I32),
+                    out=rows.rearrange("r (f n) -> r f n", n=width).bitcast(I32),
+                    in_=scales[:, 0, 4 * q : 4 * q + 4, :].rearrange("f r n -> r f n").bitcast(I32),
                 )
 
         def load_words(word_tile, words, first):
@@ -100,39 +87,38 @@ def tile_moe_mlr_relu2_kernel(
             nc.sync.dma_start(out=word_tile[:], in_=matrices.rearrange("f p n d -> p f (n d)").bitcast(I32))
 
         x_word_window = xw[:].bitcast(U32)
-        nc.sync.dma_start(out=xs_stacked[STACK:, :T].bitcast(I32), in_=x_scales[0].bitcast(I32))
-        nc.sync.dma_start(list2[:], offs2)
         nc.sync.dma_start(out=xw[:, :T], in_=x_words[0].rearrange("p t d -> p (t d)").bitcast(I32))
-        load_words(aw[0], wa_words, 0)
-        load_packed_scales(a_s[0], wa_scales, 0)
-        nc.sync.dma_start(list1[:], offs)
-        a_words = []
-        for i, (a, b) in enumerate(a_parts):
-            unstack(a_scales[i], gather("a_stacked%d" % i, xs_stacked[:], U8, entries(list2, a, b)))
-            a_words.append(gather("a_words%d" % i, x_word_window, U32, entries(list2, a, b)))
-            load_words(aw[i + 1], wa_words, 2 * (i + 1))
-        load_packed_scales(a_s[1], wa_scales, 1)
-        load_words(aw[3], wa_words, 6)
-        unstack(e_scales, gather("e_stacked", xs_stacked[:], U8, list1[:]))
-        e_words = gather("e_words", x_word_window, U32, list1[:])
-        nc.sync.dma_start(out=ww[:].bitcast(I32), in_=w_words[:, 0].rearrange("e p b -> p e b").bitcast(I32))
         for q in range(QUADS):
             nc.sync.dma_start(
-                out=ws[32 * q : 32 * q + 4, :, :].bitcast(I32),
-                in_=w_scales[:, 0, 4 * q : 4 * q + 4, :].rearrange("e r n -> r e n").bitcast(I32),
+                out=xs[32 * q : 32 * q + 4, :T].bitcast(I32), in_=x_scales[0, 4 * q : 4 * q + 4, :].bitcast(I32)
             )
+        nc.sync.dma_start(list2[:], offs2)
+        load_words(aw[0], wa_words, 0)
+        load_scales(a_s, A_ROW, wa_scales)
+        for i in range(1, F // 2):
+            load_words(aw[i], wa_words, 2 * i)
+        nc.sync.dma_start(list1[:], offs)
+        nc.sync.dma_start(out=ww[:].bitcast(I32), in_=w_words[:, 0].rearrange("e p b -> p e b").bitcast(I32))
+        load_scales(ws, 0, w_scales)
         nc.sync.dma_start(out=g1[:], in_=gate)
-        for group in range(F // PACKED):
-            load_packed_scales(b_s[group], wb_scales, group)
-        load_words(bw, wb_words, 0)
+        load_scales(b_s, B_ROW, wb_scales)
+        load_words(bw[0], wb_words, 0)
+        load_words(bw[1], wb_words, PACKED)
         nc.sync.dma_start(out=g2[:], in_=gate2)
 
-        hb = [kept("hb%d" % half, [P, BANK, 4], BF16) for half in range(2)]
-        hw = [kept("hw%d" % half, [P, BANK], U32) for half in range(2)]
-        hs = [kept("hs%d" % half, [P, BANK], U8) for half in range(2)]
+        a_words, a_scales = [], []
+        for i, (a, b) in enumerate(a_parts):
+            a_words.append(gather("a_words%d" % i, x_word_window, U32, entries(list2, a, b)))
+            a_scales.append(gather("a_scales%d" % i, xs[:], U8, entries(list2, a, b)))
+        e_words = [gather("e_words0", x_word_window, U32, entries(list1, 0, BANK))]
+        e_scales = [gather("e_scales0", xs[:], U8, entries(list1, 0, BANK))]
+        e_words.append(gather("e_words1", x_word_window, U32, entries(list1, BANK, T)))
+
+        hb = kept("hb", [P, T, 4], BF16)
+        hw = kept("hw", [P, T], U32)
+        hs = kept("hs", [P, T], U8)
 
         def first_layer(f):
-            group, u = divmod(f, PACKED)
             part = 0 if f * D < EARLY else 1
             first = f * D - a_parts[part][0]
             acc = mm.tile([P, BANK], F32, name="acc")
@@ -141,23 +127,24 @@ def tile_moe_mlr_relu2_kernel(
                 lhsT=a_words[part][:, first : first + D].bitcast(FP8X4),
                 lhsT_scale=a_scales[part][:, first : first + D],
                 rhs=aw[f // 2][:, f % 2, :].bitcast(FP8X4),
-                rhs_scale=a_s[group][4 * u :, :],
+                rhs_scale=a_s[A_ROW:, H * f : H * (f + 1)],
                 start=True,
                 stop=True,
             )
-            pos = ring.tile([P, 4, P], F32, name="pos", align_bytes=ALIGN)
-            nc.scalar.activation(out=pos[:], in_=acc[:].rearrange("p (m t) -> p t m", t=4), func=ACT.Relu)
-            turned = tr.tile([P, 4, P], F32, name="turned")
-            for t in range(4):
-                nc.tensor.transpose(turned[:, t, :], pos[:, t, :], ident[:])
-            nc.scalar.activation(
-                out=hb[group][:, u * D : (u + 1) * D, :], in_=turned[:].rearrange("p t s -> p s t"), func=ACT.Square
-            )
+            pos = ring.tile([P, H], F32, name="pos", align_bytes=ALIGN)
+            nc.scalar.activation(out=pos[:], in_=acc[:], func=ACT.Relu)
+            squared = ring.tile([P, H], BF16, name="squared", align_bytes=ALIGN)
+            nc.gpsimd.tensor_tensor(squared[:], pos[:], pos[:], ALU.mult)
+            return squared
 
-        def quantize(half):
-            nc.vector.quantize_mx(
-                out=hw[half][:].bitcast(FP8X4), scales=hs[half][:], in_=hb[half][:].rearrange("p s t -> p (s t)")
-            )
+        def turn(pair, squares):
+            turned = mm.tile([P, 2, 2, D], F32, name="acc")
+            for a, squared in enumerate(squares):
+                for u in range(2):
+                    nc.tensor.transpose(turned[:, a, u, :], squared[:].bitcast(F32)[:, u::2], ident[:])
+            slots = hb[:, 2 * D * pair : 2 * D * (pair + 1), :].bitcast(F32).rearrange("p (a s) u -> p a s u", a=2)
+            copy = nc.scalar.copy if pair == 0 else nc.vector.tensor_copy
+            copy(slots, turned[:].rearrange("p a u s -> p a s u"))
 
         ys = [kept("ys%d" % j, [P, T], F32) for j in range(TILES)]
         zs = [kept("zs%d" % j, [P, T], F32) for j in range(TILES)]
@@ -173,23 +160,23 @@ def tile_moe_mlr_relu2_kernel(
                 nc.tensor.matmul_mx(
                     out=acc[:, C * u : C * (u + 1)],
                     lhsT=ww[:, e, 2 * P * j : 2 * P * (j + 1)].bitcast(FP4X4),
-                    lhsT_scale=ws[:, e, P * j : P * (j + 1)],
-                    rhs=e_words[:, C * e : C * (e + 1)].bitcast(FP8X4),
-                    rhs_scale=e_scales[:, C * e : C * (e + 1)],
+                    lhsT_scale=ws[:, N * e + P * j : N * e + P * (j + 1)],
+                    rhs=e_words[half][:, C * u : C * (u + 1)].bitcast(FP8X4),
+                    rhs_scale=e_scales[half][:, C * u : C * (u + 1)],
                     start=True,
                     stop=True,
                 )
-            gated(ys[j], acc, g1, half)
+            return acc
 
         def second_layer(j, half):
             acc = mm.tile([P, BANK], F32, name="acc")
             for u in range(PACKED):
                 nc.tensor.matmul_mx(
                     out=acc[:, D * u : D * (u + 1)],
-                    lhsT=bw[:, PACKED * half + u, P * j : P * (j + 1)].bitcast(FP8X4),
-                    lhsT_scale=b_s[half][4 * u :, P * j : P * (j + 1)],
-                    rhs=hw[half][:, D * u : D * (u + 1)].bitcast(FP8X4),
-                    rhs_scale=hs[half][:, D * u : D * (u + 1)],
+                    lhsT=bw[half][:, u, P * j : P * (j + 1)].bitcast(FP8X4),
+                    lhsT_scale=b_s[B_ROW:, N * (PACKED * half + u) + P * j : N * (PACKED * half + u) + P * (j + 1)],
+                    rhs=hw[:, BANK * half + D * u : BANK * half + D * (u + 1)].bitcast(FP8X4),
+                    rhs_scale=hs[:, BANK * half + D * u : BANK * half + D * (u + 1)],
                     start=True,
                     stop=True,
                 )
@@ -203,45 +190,50 @@ def tile_moe_mlr_relu2_kernel(
                 out=window[:].indirect(entries(offsets, first, end)), in_=values[:, first:end], func=ACT.Copy
             )
 
-        def scalar_pair(windows, offsets, values):
+        def scalar_pair(*jobs):
             for first in range(0, T, ACT_PIECE):
-                for j in range(2):
-                    scalar_scatter(windows[j], offsets, values[j], first, min(first + ACT_PIECE, T))
+                for window, offsets, values in jobs:
+                    scalar_scatter(window, offsets, values, first, min(first + ACT_PIECE, T))
 
         def add_and_store(j):
-            res = kept("res%d" % j, [P, T], F32)
+            res = sums.tile([P, T], F32, name="res", align_bytes=ALIGN)
             nc.gpsimd.tensor_tensor(res[:], oy[j][:, :T], oz[j][:, :T], ALU.add)
             nc.sync.dma_start(out=out[P * j : P * (j + 1), :], in_=res[:])
 
-        for f in range(F):
-            first_layer(f)
-        for pair in range(2):
+        squares = [first_layer(f) for f in range(F)]
+        turn(0, squares[:2])
+        first_half = {j: experts(j, 0) for j in (1, 2, 3, 0)}
+        for j in (1, 2):
+            gated(ys[j], first_half[j], g1, 0)
+        e_scales.append(gather("e_scales1", xs[:], U8, entries(list1, BANK, T), tag="e_scales0"))
+        for j in (3, 0):
+            gated(ys[j], first_half[j], g1, 0)
+        for j in (1, 2, 3):
+            gated(ys[j], experts(j, 1), g1, 1)
+        for pair in range(1, F // 2):
+            turn(pair, squares[2 * pair : 2 * pair + 2])
+        nc.vector.quantize_mx(out=hw[:].bitcast(FP8X4), scales=hs[:], in_=hb[:].rearrange("p s t -> p (s t)"))
+        gated(ys[0], experts(0, 1), g1, 1)
+        oy = [None] + [kept("oy%d" % j, [P, WINDOW], F32) for j in (1, 2)]
+        oz = [None] + [kept("oz%d" % j, [P, WINDOW], F32) for j in (1, 2, 3)]
+        scalar_pair((oy[1], list1, ys[1]), (oy[2], list1, ys[2]))
+        for j in (3, 1, 2, 0):
             for half in range(2):
-                for j in (2 * pair, 2 * pair + 1):
-                    experts(j, half)
-            quantize(pair)
-        oy = [kept("oy%d" % j, [P, WINDOW], F32) for j in range(2)]
-        oz = [kept("oz%d" % j, [P, WINDOW], F32) for j in range(TILES)]
-        scalar_pair(oy, list1, ys)
-        for half in range(2):
-            for j in range(TILES):
                 second_layer(j, half)
-        scalar_pair(oz, list2, zs)
+        oy.append(kept("oy3", [P, WINDOW], F32, tag="hw"))
+        scalar_pair((oy[3], list1, ys[3]), (oz[3], list2, zs[3]))
+        oz[0] = kept("oz0", [P, WINDOW], F32, tag="zs3")
+        scalar_pair((oz[0], list2, zs[0]))
 
+        vector_scatter(oz[1], list2, zs[1], 0, T)
         vector_scatter(oz[2], list2, zs[2], 0, T)
-        oy.append(kept("oy2", [P, WINDOW], F32, tag="hw1"))
-        vector_scatter(oy[2], list1, ys[2], 0, T)
-        oy.append(kept("oy3", [P, WINDOW], F32, tag="zs2"))
-        vector_scatter(oy[LAST], list1, ys[LAST], 0, ACT_PIECE)
-        middle = (ACT_PIECE + T) // 2
-        scalar_scatter(oy[LAST], list1, ys[LAST], ACT_PIECE, middle)
-        scalar_scatter(oy[LAST], list1, ys[LAST], middle, T)
-        vector_scatter(oz[LAST], list2, zs[LAST], 0, T)
-        for j in (2, 0, 1):
+        oy[0] = kept("oy0", [P, WINDOW], F32, tag="zs1")
+        vector_scatter(oy[0], list1, ys[0], 0, T)
+        for j in (1, 2, 3):
             add_and_store(j)
 
+        last = kept("last", [P, T], F32, tag="oz3")
         for c in range(0, T, PIECE):
             cols = slice(c, c + PIECE)
-            piece = kept("piece%d" % c, [P, PIECE], F32)
-            nc.vector.tensor_tensor(piece[:], oy[LAST][:, cols], oz[LAST][:, cols], ALU.add)
-            nc.sync.dma_start(out=out[P * LAST : P * TILES, cols], in_=piece[:])
+            nc.vector.tensor_tensor(last[:, cols], oy[0][:, cols], oz[0][:, cols], ALU.add)
+            nc.sync.dma_start(out=out[0:P, cols], in_=last[:, cols])

@@ -22,7 +22,7 @@ BANK = 512
 TILES = N // P
 QUADS = 4
 PACKED = 4
-A_ROW, B_ROW = 4, 8
+B_ROW = 8
 LIST_COLS = T // 16
 WINDOW = 1408
 EARLY = 2 * D
@@ -40,6 +40,7 @@ def tile_moe_mlr_relu2_kernel(
         ring = ctx.enter_context(tc.tile_pool(name="ring", bufs=F))
         sums = ctx.enter_context(tc.tile_pool(name="sums", bufs=2))
         mm = ctx.enter_context(tc.psum_pool(name="mm", bufs=6))
+        held = ctx.enter_context(tc.psum_pool(name="held", bufs=2))
 
         def kept(name, shape, dtype, tag=None):
             return keep.tile(shape, dtype, name=name, tag=tag or name, align_bytes=ALIGN)
@@ -53,14 +54,15 @@ def tile_moe_mlr_relu2_kernel(
         ws = kept("ws", [P, E * N + 4], U8)
         aw = [kept("aw%d" % i, [P, 2, H], I32) for i in range(F // 2)]
         bw = [kept("bw%d" % half, [P, PACKED, N], I32) for half in range(2)]
-        a_s = kept("a_s", [P, F * H], U8)
+        a_s = [kept("a_s%d" % g, [P, H], U8) for g in range(F // PACKED)]
         b_s = kept("b_s", [P, F * N], U8)
         g1 = kept("g1", [P, T], F32)
         g2 = kept("g2", [P, T], F32)
         ident = kept("ident", [P, P], F32)
 
         nc.gpsimd.memset(xs[:, :T].bitcast(I32), 0)
-        nc.gpsimd.memset(a_s[:].bitcast(I32), 0)
+        for scale_tile in a_s:
+            nc.gpsimd.memset(scale_tile[:].bitcast(I32), 0)
         make_identity(nc, ident[:])
         nc.vector.memset(ws[:].bitcast(I32), 0)
         nc.gpsimd.memset(b_s[:].bitcast(I32), 0)
@@ -82,6 +84,13 @@ def tile_moe_mlr_relu2_kernel(
                     in_=scales[:, 0, 4 * q : 4 * q + 4, :].rearrange("f r n -> r f n").bitcast(I32),
                 )
 
+        def load_packed_scales(scale_tile, scales, group):
+            for q in range(QUADS):
+                nc.sync.dma_start(
+                    out=scale_tile[32 * q : 32 * q + 4 * PACKED, :].bitcast(I32),
+                    in_=scales[PACKED * group : PACKED * (group + 1), 0, 4 * q : 4 * q + 4, :].bitcast(I32),
+                )
+
         def load_words(word_tile, words, first):
             matrices = words[first : first + word_tile.shape[1], 0]
             nc.sync.dma_start(out=word_tile[:], in_=matrices.rearrange("f p n d -> p f (n d)").bitcast(I32))
@@ -94,10 +103,12 @@ def tile_moe_mlr_relu2_kernel(
             )
         nc.sync.dma_start(list2[:], offs2)
         load_words(aw[0], wa_words, 0)
-        load_scales(a_s, A_ROW, wa_scales)
-        for i in range(1, F // 2):
-            load_words(aw[i], wa_words, 2 * i)
+        load_packed_scales(a_s[0], wa_scales, 0)
+        load_words(aw[1], wa_words, 2)
         nc.sync.dma_start(list1[:], offs)
+        load_packed_scales(a_s[1], wa_scales, 1)
+        for i in range(2, F // 2):
+            load_words(aw[i], wa_words, 2 * i)
         nc.sync.dma_start(out=ww[:].bitcast(I32), in_=w_words[:, 0].rearrange("e p b -> p e b").bitcast(I32))
         load_scales(ws, 0, w_scales)
         nc.sync.dma_start(out=g1[:], in_=gate)
@@ -127,7 +138,7 @@ def tile_moe_mlr_relu2_kernel(
                 lhsT=a_words[part][:, first : first + D].bitcast(FP8X4),
                 lhsT_scale=a_scales[part][:, first : first + D],
                 rhs=aw[f // 2][:, f % 2, :].bitcast(FP8X4),
-                rhs_scale=a_s[A_ROW:, H * f : H * (f + 1)],
+                rhs_scale=a_s[f // PACKED][4 * (f % PACKED) :, :],
                 start=True,
                 stop=True,
             )
@@ -146,7 +157,7 @@ def tile_moe_mlr_relu2_kernel(
             copy = nc.scalar.copy if pair == 0 else nc.vector.tensor_copy
             copy(slots, turned[:].rearrange("p a u s -> p a s u"))
 
-        ys = [kept("ys%d" % j, [P, T], F32) for j in range(TILES)]
+        ys = [None] + [kept("ys%d" % j, [P, T], F32) for j in range(1, TILES)]
         zs = [kept("zs%d" % j, [P, T], F32) for j in range(TILES)]
 
         def gated(result, acc, weights, half):
@@ -154,7 +165,7 @@ def tile_moe_mlr_relu2_kernel(
             nc.vector.tensor_tensor(result[:, cols], acc[:], weights[:, cols], ALU.mult)
 
         def experts(j, half):
-            acc = mm.tile([P, BANK], F32, name="acc")
+            acc = (held if j == 0 else mm).tile([P, BANK], F32, name="acc")
             for u in range(BANK // C):
                 e = half * BANK // C + u
                 nc.tensor.matmul_mx(
@@ -202,37 +213,39 @@ def tile_moe_mlr_relu2_kernel(
 
         squares = [first_layer(f) for f in range(F)]
         turn(0, squares[:2])
-        first_half = {j: experts(j, 0) for j in (1, 2, 3, 0)}
-        for j in (1, 2):
+        first_half = {j: experts(j, 0) for j in (1, 3, 2, 0)}
+        for j in (1, 3):
             gated(ys[j], first_half[j], g1, 0)
         e_scales.append(gather("e_scales1", xs[:], U8, entries(list1, BANK, T), tag="e_scales0"))
-        for j in (3, 0):
-            gated(ys[j], first_half[j], g1, 0)
-        for j in (1, 2, 3):
+        gated(ys[2], first_half[2], g1, 0)
+        for j in (1, 3):
             gated(ys[j], experts(j, 1), g1, 1)
+        second_half = experts(0, 1)
+        oy = [None] + [kept("oy%d" % j, [P, WINDOW], F32, tag="xs" if j == 2 else None) for j in (1, 2, 3)]
+        oz = [None] + [kept("oz%d" % j, [P, WINDOW], F32) for j in (1, 2, 3)]
+        vector_scatter(oy[2], list1, ys[2], 0, BANK)
         for pair in range(1, F // 2):
             turn(pair, squares[2 * pair : 2 * pair + 2])
         nc.vector.quantize_mx(out=hw[:].bitcast(FP8X4), scales=hs[:], in_=hb[:].rearrange("p s t -> p (s t)"))
-        gated(ys[0], experts(0, 1), g1, 1)
-        oy = [None] + [kept("oy%d" % j, [P, WINDOW], F32) for j in (1, 2)]
-        oz = [None] + [kept("oz%d" % j, [P, WINDOW], F32) for j in (1, 2, 3)]
-        scalar_pair((oy[1], list1, ys[1]), (oy[2], list1, ys[2]))
-        for j in (3, 1, 2, 0):
-            for half in range(2):
-                second_layer(j, half)
-        oy.append(kept("oy3", [P, WINDOW], F32, tag="hw"))
-        scalar_pair((oy[3], list1, ys[3]), (oz[3], list2, zs[3]))
+        ys[0] = kept("ys0", [P, T], F32, tag="hb")
+        gated(ys[0], first_half[0], g1, 0)
+        gated(ys[0], second_half, g1, 1)
+        scalar_pair((oy[1], list1, ys[1]), (oy[3], list1, ys[3]))
+        for j, half in ((3, 0), (2, 0), (3, 1), (2, 1), (1, 0), (1, 1), (0, 0), (0, 1)):
+            second_layer(j, half)
+        gated(ys[2], experts(2, 1), g1, 1)
+        scalar_pair((oz[3], list2, zs[3]), (oz[2], list2, zs[2]))
         oz[0] = kept("oz0", [P, WINDOW], F32, tag="zs3")
         scalar_pair((oz[0], list2, zs[0]))
 
         vector_scatter(oz[1], list2, zs[1], 0, T)
-        vector_scatter(oz[2], list2, zs[2], 0, T)
+        vector_scatter(oy[2], list1, ys[2], BANK, T)
         oy[0] = kept("oy0", [P, WINDOW], F32, tag="zs1")
         vector_scatter(oy[0], list1, ys[0], 0, T)
-        for j in (1, 2, 3):
+        for j in (1, 3, 2):
             add_and_store(j)
 
-        last = kept("last", [P, T], F32, tag="oz3")
+        last = kept("last", [P, T], F32, tag="oz2")
         for c in range(0, T, PIECE):
             cols = slice(c, c + PIECE)
             nc.vector.tensor_tensor(last[:, cols], oy[0][:, cols], oz[0][:, cols], ALU.add)

@@ -28,6 +28,7 @@ WINDOW = 1408
 EARLY = 2 * D
 ACT_PIECE = 384
 PIECE = 256
+MOVED = 128
 ALIGN = 256
 
 
@@ -38,7 +39,6 @@ def tile_moe_mlr_relu2_kernel(
     with ExitStack() as ctx:
         keep = ctx.enter_context(tc.tile_pool(name="keep", bufs=1))
         ring = ctx.enter_context(tc.tile_pool(name="ring", bufs=F))
-        sums = ctx.enter_context(tc.tile_pool(name="sums", bufs=2))
         mm = ctx.enter_context(tc.psum_pool(name="mm", bufs=6))
         held = ctx.enter_context(tc.psum_pool(name="held", bufs=2))
 
@@ -144,7 +144,7 @@ def tile_moe_mlr_relu2_kernel(
             )
             pos = ring.tile([P, H], F32, name="pos", align_bytes=ALIGN)
             nc.scalar.activation(out=pos[:], in_=acc[:], func=ACT.Relu)
-            squared = ring.tile([P, H], BF16, name="squared", align_bytes=ALIGN)
+            squared = kept("squared%d" % f, [P, H], BF16)
             nc.gpsimd.tensor_tensor(squared[:], pos[:], pos[:], ALU.mult)
             return squared
 
@@ -206,8 +206,8 @@ def tile_moe_mlr_relu2_kernel(
                 for window, offsets, values in jobs:
                     scalar_scatter(window, offsets, values, first, min(first + ACT_PIECE, T))
 
-        def add_and_store(j):
-            res = sums.tile([P, T], F32, name="res", align_bytes=ALIGN)
+        def add_and_store(j, buffer):
+            res = kept("res%d" % j, [P, T], F32, tag=buffer)
             nc.gpsimd.tensor_tensor(res[:], oy[j][:, :T], oz[j][:, :T], ALU.add)
             nc.sync.dma_start(out=out[P * j : P * (j + 1), :], in_=res[:])
 
@@ -216,34 +216,41 @@ def tile_moe_mlr_relu2_kernel(
         first_half = {j: experts(j, 0) for j in (1, 3, 2, 0)}
         for j in (1, 3):
             gated(ys[j], first_half[j], g1, 0)
+        oy3 = kept("oy3", [P, T], F32)
         e_scales.append(gather("e_scales1", xs[:], U8, entries(list1, BANK, T), tag="e_scales0"))
+        vector_scatter(oy3, list1, ys[3], 0, MOVED)
         gated(ys[2], first_half[2], g1, 0)
         for j in (1, 3):
             gated(ys[j], experts(j, 1), g1, 1)
         second_half = experts(0, 1)
-        oy = [None] + [kept("oy%d" % j, [P, WINDOW], F32, tag="xs" if j == 2 else None) for j in (1, 2, 3)]
+        oy = [None, kept("oy1", [P, WINDOW], F32), kept("oy2", [P, WINDOW], F32, tag="xs"), oy3]
         oz = [None] + [kept("oz%d" % j, [P, WINDOW], F32) for j in (1, 2, 3)]
         vector_scatter(oy[2], list1, ys[2], 0, BANK)
         for pair in range(1, F // 2):
             turn(pair, squares[2 * pair : 2 * pair + 2])
         nc.vector.quantize_mx(out=hw[:].bitcast(FP8X4), scales=hs[:], in_=hb[:].rearrange("p s t -> p (s t)"))
-        ys[0] = kept("ys0", [P, T], F32, tag="hb")
+        ys[0] = kept("ys0", [P, T], F32, tag="squared%d" % (F - 1))
         gated(ys[0], first_half[0], g1, 0)
         gated(ys[0], second_half, g1, 1)
-        scalar_pair((oy[1], list1, ys[1]), (oy[3], list1, ys[3]))
-        for j, half in ((3, 0), (2, 0), (3, 1), (2, 1), (1, 0), (1, 1), (0, 0), (0, 1)):
+        cuts1, cuts3 = (0, ACT_PIECE, 2 * ACT_PIECE, T), (MOVED, BANK, BANK + C, T)
+        for i in range(3):
+            scalar_scatter(oy[1], list1, ys[1], cuts1[i], cuts1[i + 1])
+            scalar_scatter(oy[3], list1, ys[3], cuts3[i], cuts3[i + 1])
+        for j, half in ((3, 0), (2, 0), (3, 1), (2, 1), (1, 0), (1, 1)):
             second_layer(j, half)
+        vector_scatter(oz[1], list2, zs[1], 0, T)
         gated(ys[2], experts(2, 1), g1, 1)
+        for half in range(2):
+            second_layer(0, half)
         scalar_pair((oz[3], list2, zs[3]), (oz[2], list2, zs[2]))
         oz[0] = kept("oz0", [P, WINDOW], F32, tag="zs3")
         scalar_pair((oz[0], list2, zs[0]))
 
-        vector_scatter(oz[1], list2, zs[1], 0, T)
         vector_scatter(oy[2], list1, ys[2], BANK, T)
         oy[0] = kept("oy0", [P, WINDOW], F32, tag="zs1")
         vector_scatter(oy[0], list1, ys[0], 0, T)
-        for j in (1, 3, 2):
-            add_and_store(j)
+        for j, buffer in ((1, None), (3, "oz1"), (2, "oz3")):
+            add_and_store(j, buffer)
 
         last = kept("last", [P, T], F32, tag="oz2")
         for c in range(0, T, PIECE):

@@ -50,14 +50,16 @@ def tile_moe_mlr_relu2_kernel(
         xw = kept("xw", [P, WINDOW], I32)
         xs = kept("xs", [P, WINDOW], U8)
         a_parts = ((0, EARLY), (EARLY, T))
+        middle = (EARLY + T) // 2
+        scale_parts = (((0, EARLY),), ((EARLY, middle), (middle, T)))
         ww = kept("ww", [P, E, 2 * N], U8)
         ws = kept("ws", [P, E * N + 4], U8)
-        aw = [kept("aw%d" % i, [P, 2, H], I32) for i in range(F // 2)]
+        aw = [kept("aw%d" % half, [P, PACKED, H], I32) for half in range(2)]
         bw = [kept("bw%d" % half, [P, PACKED, N], I32) for half in range(2)]
         a_s = [kept("a_s%d" % g, [P, H], U8) for g in range(F // PACKED)]
         b_s = kept("b_s", [P, F * N], U8)
-        g1 = kept("g1", [P, T], F32)
-        g2 = kept("g2", [P, T], F32)
+        g1 = [kept("g1%d" % half, [P, BANK], F32) for half in range(2)]
+        g2 = [kept("g2%d" % half, [P, BANK], F32) for half in range(2)]
         ident = kept("ident", [P, P], F32)
 
         nc.gpsimd.memset(xs[:, :T].bitcast(I32), 0)
@@ -104,23 +106,24 @@ def tile_moe_mlr_relu2_kernel(
         nc.sync.dma_start(list2[:], offs2)
         load_words(aw[0], wa_words, 0)
         load_packed_scales(a_s[0], wa_scales, 0)
-        load_words(aw[1], wa_words, 2)
         nc.sync.dma_start(list1[:], offs)
+        load_words(aw[1], wa_words, PACKED)
         load_packed_scales(a_s[1], wa_scales, 1)
-        for i in range(2, F // 2):
-            load_words(aw[i], wa_words, 2 * i)
         nc.sync.dma_start(out=ww[:].bitcast(I32), in_=w_words[:, 0].rearrange("e p b -> p e b").bitcast(I32))
         load_scales(ws, 0, w_scales)
-        nc.sync.dma_start(out=g1[:], in_=gate)
+        for half in range(2):
+            nc.sync.dma_start(out=g1[half][:], in_=gate[:, BANK * half : BANK * (half + 1)])
         load_scales(b_s, B_ROW, wb_scales)
-        load_words(bw[0], wb_words, 0)
-        load_words(bw[1], wb_words, PACKED)
-        nc.sync.dma_start(out=g2[:], in_=gate2)
+        for half in range(2):
+            load_words(bw[half], wb_words, PACKED * half)
+            nc.sync.dma_start(out=g2[half][:], in_=gate2[:, BANK * half : BANK * (half + 1)])
 
         a_words, a_scales = [], []
         for i, (a, b) in enumerate(a_parts):
             a_words.append(gather("a_words%d" % i, x_word_window, U32, entries(list2, a, b)))
-            a_scales.append(gather("a_scales%d" % i, xs[:], U8, entries(list2, a, b)))
+            for first, end in scale_parts[i]:
+                picked = gather("a_scales%d" % first, xs[:], U8, entries(list2, first, end))
+                a_scales.extend(picked[:, u : u + D] for u in range(0, end - first, D))
         e_words = [gather("e_words0", x_word_window, U32, entries(list1, 0, BANK))]
         e_scales = [gather("e_scales0", xs[:], U8, entries(list1, 0, BANK))]
         e_words.append(gather("e_words1", x_word_window, U32, entries(list1, BANK, T)))
@@ -136,8 +139,8 @@ def tile_moe_mlr_relu2_kernel(
             nc.tensor.matmul_mx(
                 out=acc[:],
                 lhsT=a_words[part][:, first : first + D].bitcast(FP8X4),
-                lhsT_scale=a_scales[part][:, first : first + D],
-                rhs=aw[f // 2][:, f % 2, :].bitcast(FP8X4),
+                lhsT_scale=a_scales[f],
+                rhs=aw[f // PACKED][:, f % PACKED, :].bitcast(FP8X4),
                 rhs_scale=a_s[f // PACKED][4 * (f % PACKED) :, :],
                 start=True,
                 stop=True,
@@ -162,7 +165,7 @@ def tile_moe_mlr_relu2_kernel(
 
         def gated(result, acc, weights, half):
             cols = slice(BANK * half, BANK * (half + 1))
-            nc.vector.tensor_tensor(result[:, cols], acc[:], weights[:, cols], ALU.mult)
+            nc.vector.tensor_tensor(result[:, cols], acc[:], weights[half][:], ALU.mult)
 
         def experts(j, half):
             acc = (held if j == 0 else mm).tile([P, BANK], F32, name="acc")

@@ -28,7 +28,7 @@ WINDOW = 1408
 EARLY = 2 * D
 ACT_PIECE = 384
 PIECE = 256
-MOVED = 128
+MOVED = 224
 ALIGN = 256
 
 
@@ -38,7 +38,6 @@ def tile_moe_mlr_relu2_kernel(
     nc = tc.nc
     with ExitStack() as ctx:
         keep = ctx.enter_context(tc.tile_pool(name="keep", bufs=1))
-        ring = ctx.enter_context(tc.tile_pool(name="ring", bufs=F))
         mm = ctx.enter_context(tc.psum_pool(name="mm", bufs=6))
         held = ctx.enter_context(tc.psum_pool(name="held", bufs=2))
 
@@ -52,14 +51,15 @@ def tile_moe_mlr_relu2_kernel(
         a_parts = ((0, EARLY), (EARLY, T))
         middle = (EARLY + T) // 2
         scale_parts = (((0, EARLY),), ((EARLY, middle), (middle, T)))
-        ww = kept("ww", [P, E, 2 * N], U8)
+        ww = [kept("ww%d" % half, [P, E // 2, 2 * N], U8) for half in range(2)]
         ws = kept("ws", [P, E * N + 4], U8)
         aw = [kept("aw%d" % half, [P, PACKED, H], I32) for half in range(2)]
         bw = [kept("bw%d" % half, [P, PACKED, N], I32) for half in range(2)]
         a_s = [kept("a_s%d" % g, [P, H], U8) for g in range(F // PACKED)]
         b_s = kept("b_s", [P, F * N], U8)
         g1 = [kept("g1%d" % half, [P, BANK], F32) for half in range(2)]
-        g2 = [kept("g2%d" % half, [P, BANK], F32) for half in range(2)]
+        g2_whole = kept("g2", [P, T], F32)
+        g2 = [g2_whole[:, :BANK], g2_whole[:, BANK:]]
         ident = kept("ident", [P, P], F32)
 
         nc.gpsimd.memset(xs[:, :T].bitcast(I32), 0)
@@ -109,14 +109,16 @@ def tile_moe_mlr_relu2_kernel(
         nc.sync.dma_start(list1[:], offs)
         load_words(aw[1], wa_words, PACKED)
         load_packed_scales(a_s[1], wa_scales, 1)
-        nc.sync.dma_start(out=ww[:].bitcast(I32), in_=w_words[:, 0].rearrange("e p b -> p e b").bitcast(I32))
-        load_scales(ws, 0, w_scales)
         for half in range(2):
+            matrices = w_words[2 * half : 2 * half + 2, 0]
+            nc.sync.dma_start(out=ww[half][:].bitcast(I32), in_=matrices.rearrange("e p b -> p e b").bitcast(I32))
+            if half == 0:
+                load_scales(ws, 0, w_scales)
             nc.sync.dma_start(out=g1[half][:], in_=gate[:, BANK * half : BANK * (half + 1)])
         load_scales(b_s, B_ROW, wb_scales)
         for half in range(2):
             load_words(bw[half], wb_words, PACKED * half)
-            nc.sync.dma_start(out=g2[half][:], in_=gate2[:, BANK * half : BANK * (half + 1)])
+        nc.sync.dma_start(out=g2_whole[:], in_=gate2)
 
         a_words, a_scales = [], []
         for i, (a, b) in enumerate(a_parts):
@@ -129,8 +131,7 @@ def tile_moe_mlr_relu2_kernel(
         e_words.append(gather("e_words1", x_word_window, U32, entries(list1, BANK, T)))
 
         hb = kept("hb", [P, T, 4], BF16)
-        hw = kept("hw", [P, T], U32)
-        hs = kept("hs", [P, T], U8)
+        hw, hs = [], []
 
         def first_layer(f):
             part = 0 if f * D < EARLY else 1
@@ -145,11 +146,23 @@ def tile_moe_mlr_relu2_kernel(
                 start=True,
                 stop=True,
             )
-            pos = ring.tile([P, H], F32, name="pos", align_bytes=ALIGN)
+            pos = kept("pos%d" % f, [P, H], F32)
+            if f < 2:
+                by_byte = pos[:].rearrange("p (t m) -> p t m", t=4)
+                nc.scalar.activation(out=by_byte, in_=acc[:].rearrange("p (m t) -> p t m", t=4), func=ACT.Relu)
+                return pos
             nc.scalar.activation(out=pos[:], in_=acc[:], func=ACT.Relu)
             squared = kept("squared%d" % f, [P, H], BF16)
             nc.gpsimd.tensor_tensor(squared[:], pos[:], pos[:], ALU.mult)
             return squared
+
+        def turn_then_square(f, pos):
+            turned = mm.tile([P, 4, D], F32, name="acc")
+            for t in range(4):
+                nc.tensor.transpose(turned[:, t, :], pos[:, P * t : P * (t + 1)], ident[:])
+            nc.scalar.activation(
+                out=hb[:, D * f : D * (f + 1), :], in_=turned[:].rearrange("p t s -> p s t"), func=ACT.Square
+            )
 
         def turn(pair, squares):
             turned = mm.tile([P, 2, 2, D], F32, name="acc")
@@ -157,8 +170,14 @@ def tile_moe_mlr_relu2_kernel(
                 for u in range(2):
                     nc.tensor.transpose(turned[:, a, u, :], squared[:].bitcast(F32)[:, u::2], ident[:])
             slots = hb[:, 2 * D * pair : 2 * D * (pair + 1), :].bitcast(F32).rearrange("p (a s) u -> p a s u", a=2)
-            copy = nc.scalar.copy if pair == 0 else nc.vector.tensor_copy
+            copy = nc.scalar.copy if pair == 1 else nc.vector.tensor_copy
             copy(slots, turned[:].rearrange("p a u s -> p a s u"))
+
+        def quantize(half, buffer):
+            hw.append(kept("hw%d" % half, [P, BANK], U32, tag=buffer))
+            hs.append(kept("hs%d" % half, [P, BANK], U8))
+            values = hb[:, BANK * half : BANK * (half + 1), :].rearrange("p s t -> p (s t)")
+            nc.vector.quantize_mx(out=hw[half][:].bitcast(FP8X4), scales=hs[half][:], in_=values)
 
         ys = [None] + [kept("ys%d" % j, [P, T], F32) for j in range(1, TILES)]
         zs = [kept("zs%d" % j, [P, T], F32) for j in range(TILES)]
@@ -173,7 +192,7 @@ def tile_moe_mlr_relu2_kernel(
                 e = half * BANK // C + u
                 nc.tensor.matmul_mx(
                     out=acc[:, C * u : C * (u + 1)],
-                    lhsT=ww[:, e, 2 * P * j : 2 * P * (j + 1)].bitcast(FP4X4),
+                    lhsT=ww[half][:, u, 2 * P * j : 2 * P * (j + 1)].bitcast(FP4X4),
                     lhsT_scale=ws[:, N * e + P * j : N * e + P * (j + 1)],
                     rhs=e_words[half][:, C * u : C * (u + 1)].bitcast(FP8X4),
                     rhs_scale=e_scales[half][:, C * u : C * (u + 1)],
@@ -189,8 +208,8 @@ def tile_moe_mlr_relu2_kernel(
                     out=acc[:, D * u : D * (u + 1)],
                     lhsT=bw[half][:, u, P * j : P * (j + 1)].bitcast(FP8X4),
                     lhsT_scale=b_s[B_ROW:, N * (PACKED * half + u) + P * j : N * (PACKED * half + u) + P * (j + 1)],
-                    rhs=hw[:, BANK * half + D * u : BANK * half + D * (u + 1)].bitcast(FP8X4),
-                    rhs_scale=hs[:, BANK * half + D * u : BANK * half + D * (u + 1)],
+                    rhs=hw[half][:, D * u : D * (u + 1)].bitcast(FP8X4),
+                    rhs_scale=hs[half][:, D * u : D * (u + 1)],
                     start=True,
                     stop=True,
                 )
@@ -214,9 +233,12 @@ def tile_moe_mlr_relu2_kernel(
             nc.gpsimd.tensor_tensor(res[:], oy[j][:, :T], oz[j][:, :T], ALU.add)
             nc.sync.dma_start(out=out[P * j : P * (j + 1), :], in_=res[:])
 
-        squares = [first_layer(f) for f in range(F)]
-        turn(0, squares[:2])
+        squares = [first_layer(f) for f in range(2)]
+        for f in range(2):
+            turn_then_square(f, squares[f])
+        squares.extend(first_layer(f) for f in range(2, F))
         first_half = {j: experts(j, 0) for j in (1, 3, 2, 0)}
+        turn(1, squares[2:4])
         for j in (1, 3):
             gated(ys[j], first_half[j], g1, 0)
         oy3 = kept("oy3", [P, T], F32)
@@ -229,9 +251,10 @@ def tile_moe_mlr_relu2_kernel(
         oy = [None, kept("oy1", [P, WINDOW], F32), kept("oy2", [P, WINDOW], F32, tag="xs"), oy3]
         oz = [None] + [kept("oz%d" % j, [P, WINDOW], F32) for j in (1, 2, 3)]
         vector_scatter(oy[2], list1, ys[2], 0, BANK)
-        for pair in range(1, F // 2):
+        quantize(0, "pos%d" % (F - 1))
+        for pair in range(2, F // 2):
             turn(pair, squares[2 * pair : 2 * pair + 2])
-        nc.vector.quantize_mx(out=hw[:].bitcast(FP8X4), scales=hs[:], in_=hb[:].rearrange("p s t -> p (s t)"))
+        quantize(1, None)
         ys[0] = kept("ys0", [P, T], F32, tag="squared%d" % (F - 1))
         gated(ys[0], first_half[0], g1, 0)
         gated(ys[0], second_half, g1, 1)
@@ -245,9 +268,9 @@ def tile_moe_mlr_relu2_kernel(
         gated(ys[2], experts(2, 1), g1, 1)
         for half in range(2):
             second_layer(0, half)
-        scalar_pair((oz[3], list2, zs[3]), (oz[2], list2, zs[2]))
-        oz[0] = kept("oz0", [P, WINDOW], F32, tag="zs3")
-        scalar_pair((oz[0], list2, zs[0]))
+        oz[0] = kept("oz0", [P, WINDOW], F32)
+        for j, i in ((3, 0), (2, 0), (3, 1), (2, 1), (3, 2), (0, 0), (2, 2), (0, 1), (0, 2)):
+            scalar_scatter(oz[j], list2, zs[j], cuts1[i], cuts1[i + 1])
 
         vector_scatter(oy[2], list1, ys[2], BANK, T)
         oy[0] = kept("oy0", [P, WINDOW], F32, tag="zs1")

@@ -19,17 +19,18 @@ ALU = mybir.AluOpType
 
 P = 128
 BANK = 512
-TILES = N // P
 QUADS = 4
 PACKED = 4
 B_ROW = 8
 LIST_COLS = T // 16
 WINDOW = 1408
-EARLY = 2 * D
-ACT_PIECE = 384
+WIDE = 2048
+SHARE = 256
+CUT = 416
+FILL = 3
 PIECE = 256
-MOVED = 224
 ALIGN = 256
+SPLIT = 768
 
 
 def tile_moe_mlr_relu2_kernel(
@@ -38,35 +39,40 @@ def tile_moe_mlr_relu2_kernel(
     nc = tc.nc
     with ExitStack() as ctx:
         keep = ctx.enter_context(tc.tile_pool(name="keep", bufs=1))
-        mm = ctx.enter_context(tc.psum_pool(name="mm", bufs=6))
-        held = ctx.enter_context(tc.psum_pool(name="held", bufs=2))
+        banks = ctx.enter_context(tc.psum_pool(name="banks", bufs=1))
 
         def kept(name, shape, dtype, tag=None):
             return keep.tile(shape, dtype, name=name, tag=tag or name, align_bytes=ALIGN)
+
+        def bank(name, shape, number):
+            return banks.tile(shape, F32, name=name, tag="bank%d" % number)
 
         list1 = kept("list1", [P, LIST_COLS], U16)
         list2 = kept("list2", [P, LIST_COLS], U16)
         xw = kept("xw", [P, WINDOW], I32)
         xs = kept("xs", [P, WINDOW], U8)
-        a_parts = ((0, EARLY), (EARLY, T))
-        middle = (EARLY + T) // 2
-        scale_parts = (((0, EARLY),), ((EARLY, middle), (middle, T)))
-        ww = [kept("ww%d" % half, [P, E // 2, 2 * N], U8) for half in range(2)]
+        folded = kept("folded", [P, 2, T], U8)
+        ww = [kept("ww0", [P, 1, 2 * N], U8), kept("ww1", [P, E - 1, 2 * N], U8)]
         ws = kept("ws", [P, E * N + 4], U8)
-        aw = [kept("aw%d" % half, [P, PACKED, H], I32) for half in range(2)]
+        aw = [kept("aw%d" % pair, [P, 2, H], I32) for pair in range(F // 2)]
         bw = [kept("bw%d" % half, [P, PACKED, N], I32) for half in range(2)]
         a_s = [kept("a_s%d" % g, [P, H], U8) for g in range(F // PACKED)]
         b_s = kept("b_s", [P, F * N], U8)
-        g1 = [kept("g1%d" % half, [P, BANK], F32) for half in range(2)]
-        g2_whole = kept("g2", [P, T], F32)
-        g2 = [g2_whole[:, :BANK], g2_whole[:, BANK:]]
-        ident = kept("ident", [P, P], F32)
+        g1 = [kept("g10", [P, C], F32), kept("g11", [P, T - C], F32)]
+        g2 = kept("g2", [P, T], F32)
+        one = kept("one", [P, 1], F32)
 
+        zero = kept("zero", [P, 1], F32)
+
+        nc.gpsimd.memset(ws[:, :SPLIT].bitcast(I32), 0)
+        nc.vector.memset(ws[:, SPLIT:].bitcast(I32), 0)
         nc.gpsimd.memset(xs[:, :T].bitcast(I32), 0)
+        nc.vector.memset(zero[:], 0.0)
+        nc.scalar.activation(out=one[:], in_=zero[:], func=ACT.Relu, bias=1.0)
         for scale_tile in a_s:
             nc.gpsimd.memset(scale_tile[:].bitcast(I32), 0)
+        ident = kept("ident", [P, P], F32)
         make_identity(nc, ident[:])
-        nc.vector.memset(ws[:].bitcast(I32), 0)
         nc.gpsimd.memset(b_s[:].bitcast(I32), 0)
 
         def entries(offsets, first, end):
@@ -98,188 +104,233 @@ def tile_moe_mlr_relu2_kernel(
             nc.sync.dma_start(out=word_tile[:], in_=matrices.rearrange("f p n d -> p f (n d)").bitcast(I32))
 
         x_word_window = xw[:].bitcast(U32)
-        nc.sync.dma_start(out=xw[:, :T], in_=x_words[0].rearrange("p t d -> p (t d)").bitcast(I32))
-        for q in range(QUADS):
+        for h in range(2):
             nc.sync.dma_start(
-                out=xs[32 * q : 32 * q + 4, :T].bitcast(I32), in_=x_scales[0, 4 * q : 4 * q + 4, :].bitcast(I32)
+                out=folded[64 * h : 64 * h + 4].bitcast(I32),
+                in_=x_scales[0, 8 * h : 8 * h + 8, :].rearrange("(q r) n -> r q n", q=2).bitcast(I32),
             )
+        for h in range(2):
+            for q in range(2):
+                first = 64 * h + 32 * q
+                nc.vector.tensor_copy(
+                    xs[first : first + 4, :T].bitcast(I32), folded[64 * h : 64 * h + 4, q, :].bitcast(I32)
+                )
+        nc.sync.dma_start(list1[:], offs)
         nc.sync.dma_start(list2[:], offs2)
+        nc.sync.dma_start(out=xw[:, :T], in_=x_words[0].rearrange("p t d -> p (t d)").bitcast(I32))
+        nc.sync.dma_start(out=ww[0][:, 0, :].bitcast(I32), in_=w_words[0, 0].bitcast(I32))
+        nc.sync.dma_start(out=g1[0][:], in_=gate[:, :C])
+        load_scales(ws, 0, w_scales)
+        load_words(aw[1], wa_words, 2)
         load_words(aw[0], wa_words, 0)
         load_packed_scales(a_s[0], wa_scales, 0)
-        nc.sync.dma_start(list1[:], offs)
-        load_words(aw[1], wa_words, PACKED)
+        for pair in (2, 3):
+            load_words(aw[pair], wa_words, 2 * pair)
         load_packed_scales(a_s[1], wa_scales, 1)
-        for half in range(2):
-            matrices = w_words[2 * half : 2 * half + 2, 0]
-            nc.sync.dma_start(out=ww[half][:].bitcast(I32), in_=matrices.rearrange("e p b -> p e b").bitcast(I32))
-            if half == 0:
-                load_scales(ws, 0, w_scales)
-            nc.sync.dma_start(out=g1[half][:], in_=gate[:, BANK * half : BANK * (half + 1)])
+        nc.sync.dma_start(out=ww[1][:].bitcast(I32), in_=w_words[1:, 0].rearrange("e p b -> p e b").bitcast(I32))
+        nc.sync.dma_start(out=g1[1][:], in_=gate[:, C:])
         load_scales(b_s, B_ROW, wb_scales)
         for half in range(2):
             load_words(bw[half], wb_words, PACKED * half)
-        nc.sync.dma_start(out=g2_whole[:], in_=gate2)
-
-        a_words, a_scales = [], []
-        for i, (a, b) in enumerate(a_parts):
-            a_words.append(gather("a_words%d" % i, x_word_window, U32, entries(list2, a, b)))
-            for first, end in scale_parts[i]:
-                picked = gather("a_scales%d" % first, xs[:], U8, entries(list2, first, end))
-                a_scales.extend(picked[:, u : u + D] for u in range(0, end - first, D))
-        e_words = [gather("e_words0", x_word_window, U32, entries(list1, 0, BANK))]
-        e_scales = [gather("e_scales0", xs[:], U8, entries(list1, 0, BANK))]
-        e_words.append(gather("e_words1", x_word_window, U32, entries(list1, BANK, T)))
-
-        hb = kept("hb", [P, T, 4], BF16)
-        hw, hs = [], []
-
-        def first_layer(f):
-            part = 0 if f * D < EARLY else 1
-            first = f * D - a_parts[part][0]
-            acc = mm.tile([P, BANK], F32, name="acc")
-            nc.tensor.matmul_mx(
-                out=acc[:],
-                lhsT=a_words[part][:, first : first + D].bitcast(FP8X4),
-                lhsT_scale=a_scales[f],
-                rhs=aw[f // PACKED][:, f % PACKED, :].bitcast(FP8X4),
-                rhs_scale=a_s[f // PACKED][4 * (f % PACKED) :, :],
-                start=True,
-                stop=True,
-            )
-            pos = kept("pos%d" % f, [P, H], F32)
-            if f < 2:
-                by_byte = pos[:].rearrange("p (t m) -> p t m", t=4)
-                nc.scalar.activation(out=by_byte, in_=acc[:].rearrange("p (m t) -> p t m", t=4), func=ACT.Relu)
-                return pos
-            nc.scalar.activation(out=pos[:], in_=acc[:], func=ACT.Relu)
-            squared = kept("squared%d" % f, [P, H], BF16)
-            nc.gpsimd.tensor_tensor(squared[:], pos[:], pos[:], ALU.mult)
-            return squared
-
-        def turn_then_square(f, pos):
-            turned = mm.tile([P, 4, D], F32, name="acc")
-            for t in range(4):
-                nc.tensor.transpose(turned[:, t, :], pos[:, P * t : P * (t + 1)], ident[:])
-            nc.scalar.activation(
-                out=hb[:, D * f : D * (f + 1), :], in_=turned[:].rearrange("p t s -> p s t"), func=ACT.Square
-            )
-
-        def turn(pair, squares):
-            turned = mm.tile([P, 2, 2, D], F32, name="acc")
-            for a, squared in enumerate(squares):
-                for u in range(2):
-                    nc.tensor.transpose(turned[:, a, u, :], squared[:].bitcast(F32)[:, u::2], ident[:])
-            slots = hb[:, 2 * D * pair : 2 * D * (pair + 1), :].bitcast(F32).rearrange("p (a s) u -> p a s u", a=2)
-            copy = nc.scalar.copy if pair == 1 else nc.vector.tensor_copy
-            copy(slots, turned[:].rearrange("p a u s -> p a s u"))
-
-        def quantize(half, buffer):
-            hw.append(kept("hw%d" % half, [P, BANK], U32, tag=buffer))
-            hs.append(kept("hs%d" % half, [P, BANK], U8))
-            values = hb[:, BANK * half : BANK * (half + 1), :].rearrange("p s t -> p (s t)")
-            nc.vector.quantize_mx(out=hw[half][:].bitcast(FP8X4), scales=hs[half][:], in_=values)
-
-        ys = [None] + [kept("ys%d" % j, [P, T], F32) for j in range(1, TILES)]
-        zs = [kept("zs%d" % j, [P, T], F32) for j in range(TILES)]
-
-        def gated(result, acc, weights, half):
+        for half in range(2):
             cols = slice(BANK * half, BANK * (half + 1))
-            nc.vector.tensor_tensor(result[:, cols], acc[:], weights[half][:], ALU.mult)
+            nc.sync.dma_start(out=g2[:, cols], in_=gate2[:, cols])
 
-        def experts(j, half):
-            acc = (held if j == 0 else mm).tile([P, BANK], F32, name="acc")
-            for u in range(BANK // C):
-                e = half * BANK // C + u
+        ys = kept("ys", [P, 4, T], F32)
+        zs = [kept("zs%d" % j, [P, T], F32) for j in range(4)]
+
+        def expert(e, tiles, words, scales, number):
+            acc = bank("y%d%d" % (e, tiles[0]), [P, len(tiles), C], number)
+            part = min(e, 1)
+            for u, j in enumerate(tiles):
                 nc.tensor.matmul_mx(
-                    out=acc[:, C * u : C * (u + 1)],
-                    lhsT=ww[half][:, u, 2 * P * j : 2 * P * (j + 1)].bitcast(FP4X4),
+                    out=acc[:, u, :],
+                    lhsT=ww[part][:, e - part, 2 * P * j : 2 * P * (j + 1)].bitcast(FP4X4),
                     lhsT_scale=ws[:, N * e + P * j : N * e + P * (j + 1)],
-                    rhs=e_words[half][:, C * u : C * (u + 1)].bitcast(FP8X4),
-                    rhs_scale=e_scales[half][:, C * u : C * (u + 1)],
+                    rhs=words.bitcast(FP8X4),
+                    rhs_scale=scales,
                     start=True,
                     stop=True,
                 )
             return acc
 
-        def second_layer(j, half):
-            acc = mm.tile([P, BANK], F32, name="acc")
-            for u in range(PACKED):
-                nc.tensor.matmul_mx(
-                    out=acc[:, D * u : D * (u + 1)],
-                    lhsT=bw[half][:, u, P * j : P * (j + 1)].bitcast(FP8X4),
-                    lhsT_scale=b_s[B_ROW:, N * (PACKED * half + u) + P * j : N * (PACKED * half + u) + P * (j + 1)],
-                    rhs=hw[half][:, D * u : D * (u + 1)].bitcast(FP8X4),
-                    rhs_scale=hs[half][:, D * u : D * (u + 1)],
-                    start=True,
-                    stop=True,
-                )
-            gated(zs[j], acc, g2, half)
+        def gate_expert(e, tiles, acc):
+            part = min(e, 1)
+            weights = g1[part][:, C * (e - part) : C * (e - part + 1)].unsqueeze(1).to_broadcast([P, len(tiles), C])
+            result = ys[:, tiles[0] : tiles[-1] + 1, C * e : C * (e + 1)]
+            nc.vector.tensor_tensor(result, acc[:], weights, ALU.mult)
 
         def vector_scatter(window, offsets, values, first, end):
             nc.vector.tensor_copy(window[:].indirect(entries(offsets, first, end)), values[:, first:end])
 
         def scalar_scatter(window, offsets, values, first, end):
             nc.scalar.activation(
-                out=window[:].indirect(entries(offsets, first, end)), in_=values[:, first:end], func=ACT.Copy
+                out=window[:].indirect(entries(offsets, first, end)),
+                in_=values[:, first:end],
+                func=ACT.Copy,
+                scale=one[:],
             )
 
-        def scalar_pair(*jobs):
-            for first in range(0, T, ACT_PIECE):
-                for window, offsets, values in jobs:
-                    scalar_scatter(window, offsets, values, first, min(first + ACT_PIECE, T))
+        oy = [kept("oy%d" % j, [P, WIDE], F32) for j in range(2)]
 
-        def add_and_store(j, buffer):
+        scales0 = gather("e_scales0", xs[:], U8, entries(list1, 0, C))
+        words0 = gather("e_words0", x_word_window, U32, entries(list1, 0, C))
+        a_words = [gather("a_words0", x_word_window, U32, entries(list2, 0, FILL * D))]
+        for number, tiles in enumerate(((0,), (1, 2))):
+            gate_expert(0, tiles, expert(0, tiles, words0[:], scales0[:], number))
+        last_of_first = expert(0, (3,), words0[:], scales0[:], 2)
+        for j in range(2):
+            scalar_scatter(oy[j], list1, ys[:, j, :], 0, C)
+
+        a_scales = kept("a_scales", [P, T], U8, tag="e_scales0")
+        nc.vector.tensor_copy(a_scales[:, : 2 * D], xs[:].indirect(entries(list2, 0, 2 * D)))
+        gate_expert(0, (3,), last_of_first)
+        a_words.append(gather("a_words1", x_word_window, U32, entries(list2, FILL * D, T), tag="e_words0"))
+        nc.vector.tensor_copy(a_scales[:, 2 * D :], xs[:].indirect(entries(list2, 2 * D, T)))
+        scales1 = gather("e_scales1", xs[:], U8, entries(list1, C, 2 * C), tag="g10")
+        words1 = gather("e_words1", x_word_window, U32, entries(list1, C, T), tag="ww0")
+
+        def tokens(f):
+            part = 0 if f < FILL else 1
+            first = D * (f - part * FILL)
+            return a_words[part][:, first : first + D].bitcast(FP8X4)
+
+        squares = {}
+        hb = [kept("hb%d" % half, [P, BANK, 4], BF16) for half in range(2)]
+        reordered = [kept("reordered%d" % u, [P, 4, P], I32) for u in range(2)]
+        for u in range(2):
+            nc.gpsimd.tensor_copy(reordered[u][:], aw[1][:, u, :].rearrange("p (m t) -> p t m", t=4))
+        reordered_scales = kept("reordered_scales", [P, 4, P], U8)
+        nc.gpsimd.tensor_copy(reordered_scales[:], a_s[0][:].rearrange("p (m t) -> p t m", t=4))
+
+        def first_layer(f, number):
+            acc = bank("h%d" % f, [P, H], number)
+            nc.tensor.matmul_mx(
+                out=acc[:],
+                lhsT=tokens(f),
+                lhsT_scale=a_scales[:, D * f : D * (f + 1)],
+                rhs=aw[f // 2][:, f % 2, :].bitcast(FP8X4),
+                rhs_scale=a_s[f // PACKED][4 * (f % PACKED) :, :],
+                start=True,
+                stop=True,
+            )
+            pos = kept("pos%d" % f, [P, H], F32)
+            nc.scalar.activation(out=pos[:], in_=acc[:], func=ACT.Relu)
+            squares.setdefault(f, kept("squared%d" % f, [P, H], BF16))
+            nc.gpsimd.tensor_tensor(squares[f][:], pos[:], pos[:], ALU.mult)
+
+        def first_layer_reordered(f, number):
+            acc = bank("h%d" % f, [P, 4, D], number)
+            for t in range(4):
+                nc.tensor.matmul_mx(
+                    out=acc[:, t, :],
+                    lhsT=reordered[f % 2][:, t, :].bitcast(FP8X4),
+                    lhsT_scale=reordered_scales[4 * f :, t, :],
+                    rhs=tokens(f),
+                    rhs_scale=a_scales[:, D * f : D * (f + 1)],
+                    start=True,
+                    stop=True,
+                )
+            pos = kept("pos%d" % f, [P, D, 4], F32)
+            nc.scalar.activation(out=pos[:], in_=acc[:].rearrange("p t s -> p s t"), func=ACT.Relu)
+            nc.gpsimd.tensor_tensor(hb[0][:, D * f : D * (f + 1), :], pos[:], pos[:], ALU.mult)
+
+        for f, number in zip((0, 1, 4, 5, 6, 7), (4, 5, 6, 7, 0, 1)):
+            first_layer(f, number)
+        for f, number in zip((2, 3), (4, 5)):
+            first_layer_reordered(f, number)
+        oy.append(kept("oy2", [P, T], F32, tag="aw0"))
+        scalar_scatter(oy[2], list1, ys[:, 2, :], 0, C)
+        pairs = ((0, 1), (2, 3))
+        second = [expert(1, tiles, words1[:, :C], scales1[:], number) for tiles, number in zip(pairs, (3, 2))]
+        scales2 = gather("e_scales2", xs[:], U8, entries(list1, BANK, T), tag="aw2")
+        gate_expert(1, pairs[0], second[0])
+        gate_expert(1, pairs[1], second[1])
+        for j in range(2):
+            scalar_scatter(oy[j], list1, ys[:, j, :], C, 2 * C)
+
+        def last_two_experts(j, number):
+            acc = bank("y_late%d" % j, [P, BANK], number)
+            for u in range(2):
+                e = 2 + u
+                nc.tensor.matmul_mx(
+                    out=acc[:, C * u : C * (u + 1)],
+                    lhsT=ww[1][:, e - 1, 2 * P * j : 2 * P * (j + 1)].bitcast(FP4X4),
+                    lhsT_scale=ws[:, N * e + P * j : N * e + P * (j + 1)],
+                    rhs=words1[:, C * (e - 1) : C * e].bitcast(FP8X4),
+                    rhs_scale=scales2[:, C * u : C * (u + 1)],
+                    start=True,
+                    stop=True,
+                )
+            nc.vector.tensor_tensor(ys[:, j, BANK:], acc[:], g1[1][:, C:], ALU.mult)
+
+        for j, number in ((2, 6), (0, 7), (1, 3)):
+            last_two_experts(j, number)
+        for j in range(2):
+            scalar_scatter(oy[j], list1, ys[:, j, :], BANK, T)
+        vector_scatter(oy[2], list1, ys[:, 2, :], CUT, T)
+        scalar_scatter(oy[2], list1, ys[:, 2, :], C, CUT)
+
+        def turn(pair, number):
+            turned = bank("turned%d" % pair, [P, 2, 2, D], number)
+            for a in range(2):
+                for u in range(2):
+                    nc.tensor.transpose(turned[:, a, u, :], squares[2 * pair + a][:].bitcast(F32)[:, u::2], ident[:])
+            slots = hb[pair // 2][:, 2 * D * (pair % 2) : 2 * D * (pair % 2 + 1), :].bitcast(F32).rearrange("p (a s) u -> p a s u", a=2)
+            nc.vector.tensor_copy(slots, turned[:].rearrange("p a u s -> p a s u"))
+
+        hw, hs = [], []
+
+        def quantize(half, buffer):
+            hw.append(kept("hw%d" % half, [P, BANK], U32, tag=buffer))
+            hs.append(kept("hs%d" % half, [P, BANK], U8))
+            values = hb[half][:].rearrange("p s t -> p (s t)")
+            nc.vector.quantize_mx(out=hw[half][:].bitcast(FP8X4), scales=hs[half][:], in_=values)
+
+        for pair, number in ((0, 2), (2, 6)):
+            turn(pair, number)
+        quantize(0, None)
+        turn(3, 3)
+        last_two_experts(3, 7)
+        quantize(1, None)
+
+        def second_layer(j, half):
+            acc = bank("z%d%d" % (j, half), [P, BANK], ((0, 1, 4, 5), (6, 7, 3, 2))[half][j])
+            for u in range(PACKED):
+                first = N * (PACKED * half + u) + P * j
+                nc.tensor.matmul_mx(
+                    out=acc[:, D * u : D * (u + 1)],
+                    lhsT=bw[half][:, u, P * j : P * (j + 1)].bitcast(FP8X4),
+                    lhsT_scale=b_s[B_ROW:, first : first + P],
+                    rhs=hw[half][:, D * u : D * (u + 1)].bitcast(FP8X4),
+                    rhs_scale=hs[half][:, D * u : D * (u + 1)],
+                    start=True,
+                    stop=True,
+                )
+            cols = slice(BANK * half, BANK * (half + 1))
+            nc.vector.tensor_tensor(zs[j][:, cols], acc[:], g2[:, cols], ALU.mult)
+
+        oz = [kept("oz%d" % j, [P, WINDOW if j == 2 else WIDE], F32) for j in range(4)]
+        for j in range(4):
+            for half in range(2):
+                second_layer(j, half)
+            if j == 1:
+                vector_scatter(oz[1], list2, zs[1], 0, SHARE)
+        for half in range(2):
+            scalar_scatter(oz[0], list2, zs[0], BANK * half, BANK * (half + 1))
+        scalar_scatter(oz[1], list2, zs[1], SHARE, T)
+        vector_scatter(oz[2], list2, zs[2], 0, T)
+        scalar_scatter(oz[3], list2, zs[3], 0, T)
+        oy.append(kept("oy3", [P, WINDOW], F32, tag="hw1"))
+        vector_scatter(oy[3], list1, ys[:, 3, :], 0, T)
+
+        for j, buffer in ((0, None), (2, "oz0"), (1, "oz2")):
             res = kept("res%d" % j, [P, T], F32, tag=buffer)
             nc.gpsimd.tensor_tensor(res[:], oy[j][:, :T], oz[j][:, :T], ALU.add)
             nc.sync.dma_start(out=out[P * j : P * (j + 1), :], in_=res[:])
 
-        squares = [first_layer(f) for f in range(2)]
-        for f in range(2):
-            turn_then_square(f, squares[f])
-        squares.extend(first_layer(f) for f in range(2, F))
-        first_half = {j: experts(j, 0) for j in (1, 3, 2, 0)}
-        turn(1, squares[2:4])
-        for j in (1, 3):
-            gated(ys[j], first_half[j], g1, 0)
-        oy3 = kept("oy3", [P, T], F32)
-        e_scales.append(gather("e_scales1", xs[:], U8, entries(list1, BANK, T), tag="e_scales0"))
-        vector_scatter(oy3, list1, ys[3], 0, MOVED)
-        gated(ys[2], first_half[2], g1, 0)
-        for j in (1, 3):
-            gated(ys[j], experts(j, 1), g1, 1)
-        second_half = experts(0, 1)
-        oy = [None, kept("oy1", [P, WINDOW], F32), kept("oy2", [P, WINDOW], F32, tag="xs"), oy3]
-        oz = [None] + [kept("oz%d" % j, [P, WINDOW], F32) for j in (1, 2, 3)]
-        vector_scatter(oy[2], list1, ys[2], 0, BANK)
-        quantize(0, "pos%d" % (F - 1))
-        for pair in range(2, F // 2):
-            turn(pair, squares[2 * pair : 2 * pair + 2])
-        quantize(1, None)
-        ys[0] = kept("ys0", [P, T], F32, tag="squared%d" % (F - 1))
-        gated(ys[0], first_half[0], g1, 0)
-        gated(ys[0], second_half, g1, 1)
-        cuts1, cuts3 = (0, ACT_PIECE, 2 * ACT_PIECE, T), (MOVED, BANK, BANK + C, T)
-        for i in range(3):
-            scalar_scatter(oy[1], list1, ys[1], cuts1[i], cuts1[i + 1])
-            scalar_scatter(oy[3], list1, ys[3], cuts3[i], cuts3[i + 1])
-        for j, half in ((3, 0), (2, 0), (3, 1), (2, 1), (1, 0), (1, 1)):
-            second_layer(j, half)
-        vector_scatter(oz[1], list2, zs[1], 0, T)
-        gated(ys[2], experts(2, 1), g1, 1)
-        for half in range(2):
-            second_layer(0, half)
-        oz[0] = kept("oz0", [P, WINDOW], F32)
-        for j, i in ((3, 0), (2, 0), (3, 1), (2, 1), (3, 2), (0, 0), (2, 2), (0, 1), (0, 2)):
-            scalar_scatter(oz[j], list2, zs[j], cuts1[i], cuts1[i + 1])
-
-        vector_scatter(oy[2], list1, ys[2], BANK, T)
-        oy[0] = kept("oy0", [P, WINDOW], F32, tag="zs1")
-        vector_scatter(oy[0], list1, ys[0], 0, T)
-        for j, buffer in ((1, None), (3, "oz1"), (2, "oz3")):
-            add_and_store(j, buffer)
-
-        last = kept("last", [P, T], F32, tag="oz2")
+        last = kept("last", [P, T], F32, tag="oz1")
         for c in range(0, T, PIECE):
             cols = slice(c, c + PIECE)
-            nc.vector.tensor_tensor(last[:, cols], oy[0][:, cols], oz[0][:, cols], ALU.add)
-            nc.sync.dma_start(out=out[0:P, cols], in_=last[:, cols])
+            nc.vector.tensor_tensor(last[:, cols], oy[3][:, cols], oz[3][:, cols], ALU.add)
+            nc.sync.dma_start(out=out[3 * P : 4 * P, cols], in_=last[:, cols])

@@ -25,7 +25,7 @@ B_ROW = 8
 LIST_COLS = T // 16
 WINDOW = 1408
 WIDE = 2048
-SHARE = 256
+SHARE = 288
 CUT = 416
 FILL = 3
 PIECE = 256
@@ -57,7 +57,7 @@ def tile_moe_mlr_relu2_kernel(
         aw = [kept("aw%d" % pair, [P, 2, H], I32) for pair in range(F // 2)]
         bw = [kept("bw%d" % half, [P, PACKED, N], I32) for half in range(2)]
         a_s = [kept("a_s%d" % g, [P, H], U8) for g in range(F // PACKED)]
-        b_s = kept("b_s", [P, F * N], U8)
+        b_s = kept("b_s", [P, F * N + 4], U8)
         g1 = [kept("g10", [P, C], F32), kept("g11", [P, T - C], F32)]
         g2 = kept("g2", [P, T], F32)
         one = kept("one", [P, 1], F32)
@@ -73,7 +73,7 @@ def tile_moe_mlr_relu2_kernel(
             nc.gpsimd.memset(scale_tile[:].bitcast(I32), 0)
         ident = kept("ident", [P, P], F32)
         make_identity(nc, ident[:])
-        nc.gpsimd.memset(b_s[:].bitcast(I32), 0)
+        nc.vector.memset(b_s[:].bitcast(I32), 0)
 
         def entries(offsets, first, end):
             return offsets[:, first // 16 : end // 16]
@@ -187,7 +187,9 @@ def tile_moe_mlr_relu2_kernel(
         gate_expert(0, (3,), last_of_first)
         a_words.append(gather("a_words1", x_word_window, U32, entries(list2, FILL * D, T), tag="e_words0"))
         nc.vector.tensor_copy(a_scales[:, 2 * D :], xs[:].indirect(entries(list2, 2 * D, T)))
-        scales1 = gather("e_scales1", xs[:], U8, entries(list1, C, 2 * C), tag="g10")
+        late_scales = kept("late_scales", [P, T - C], U8, tag="g10")
+        scales1, scales2 = late_scales[:, :C], late_scales[:, C:]
+        nc.vector.tensor_copy(scales1, xs[:].indirect(entries(list1, C, BANK)))
         words1 = gather("e_words1", x_word_window, U32, entries(list1, C, T), tag="ww0")
 
         def tokens(f):
@@ -197,9 +199,13 @@ def tile_moe_mlr_relu2_kernel(
 
         squares = {}
         hb = [kept("hb%d" % half, [P, BANK, 4], BF16) for half in range(2)]
-        reordered = [kept("reordered%d" % u, [P, 4, P], I32) for u in range(2)]
-        for u in range(2):
+        reordered = []
+
+        def reorder(u, buffer):
+            reordered.append(kept("reordered%d" % u, [P, 4, P], I32, tag=buffer))
             nc.gpsimd.tensor_copy(reordered[u][:], aw[1][:, u, :].rearrange("p (m t) -> p t m", t=4))
+
+        reorder(0, None)
         reordered_scales = kept("reordered_scales", [P, 4, P], U8)
         nc.gpsimd.tensor_copy(reordered_scales[:], a_s[0][:].rearrange("p (m t) -> p t m", t=4))
 
@@ -237,13 +243,15 @@ def tile_moe_mlr_relu2_kernel(
 
         for f, number in zip((0, 1, 4, 5, 6, 7), (4, 5, 6, 7, 0, 1)):
             first_layer(f, number)
+            if f == 1:
+                reorder(1, "a_s0")
         for f, number in zip((2, 3), (4, 5)):
             first_layer_reordered(f, number)
         oy.append(kept("oy2", [P, T], F32, tag="aw0"))
         scalar_scatter(oy[2], list1, ys[:, 2, :], 0, C)
         pairs = ((0, 1), (2, 3))
-        second = [expert(1, tiles, words1[:, :C], scales1[:], number) for tiles, number in zip(pairs, (3, 2))]
-        scales2 = gather("e_scales2", xs[:], U8, entries(list1, BANK, T), tag="aw2")
+        second = [expert(1, tiles, words1[:, :C], scales1, number) for tiles, number in zip(pairs, (3, 2))]
+        nc.vector.tensor_copy(scales2, xs[:].indirect(entries(list1, BANK, T)))
         gate_expert(1, pairs[0], second[0])
         gate_expert(1, pairs[1], second[1])
         for j in range(2):

from contextlib import ExitStack

import concourse.mybir as mybir
from concourse.masks import make_identity

K, T, E, C, F, D, H, N = 512, 1024, 4, 256, 8, 128, 512, 512
FLOPS = 2 * K * N * E * C + 2 * K * H * F * D + 2 * H * N * F * D

F32 = mybir.dt.float32
BF16 = mybir.dt.bfloat16
I32 = mybir.dt.int32
U32 = mybir.dt.uint32
U16 = mybir.dt.uint16
U8 = mybir.dt.uint8
FP8X4 = mybir.dt.float8_e4m3fn_x4
FP4X4 = mybir.dt.float4_e2m1fn_x4
ACT = mybir.ActivationFunctionType
ALU = mybir.AluOpType

P = 128
BANK = 512
QUADS = 4
PACKED = 4
B_ROW = 8
LIST_COLS = T // 16
WINDOW = 1408
WIDE = 2048
SHARE = 288
CUT = 416
FILL = 3
PIECE = 256
ALIGN = 256
SPLIT = 768


def tile_moe_mlr_relu2_kernel(
    tc, x_words, x_scales, w_words, w_scales, wa_words, wa_scales, wb_words, wb_scales, gate, gate2, offs, offs2, out
):
    nc = tc.nc
    with ExitStack() as ctx:
        keep = ctx.enter_context(tc.tile_pool(name="keep", bufs=1))
        banks = ctx.enter_context(tc.psum_pool(name="banks", bufs=1))

        def kept(name, shape, dtype, tag=None):
            return keep.tile(shape, dtype, name=name, tag=tag or name, align_bytes=ALIGN)

        def bank(name, shape, number):
            return banks.tile(shape, F32, name=name, tag="bank%d" % number)

        list1 = kept("list1", [P, LIST_COLS], U16)
        list2 = kept("list2", [P, LIST_COLS], U16)
        xw = kept("xw", [P, WINDOW], I32)
        xs = kept("xs", [P, WINDOW], U8)
        folded = kept("folded", [P, 2, T], U8)
        ww = [kept("ww0", [P, 1, 2 * N], U8), kept("ww1", [P, E - 1, 2 * N], U8)]
        ws = kept("ws", [P, E * N + 4], U8)
        aw = [kept("aw%d" % pair, [P, 2, H], I32) for pair in range(F // 2)]
        bw = [kept("bw%d" % half, [P, PACKED, N], I32) for half in range(2)]
        a_s = [kept("a_s%d" % g, [P, H], U8) for g in range(F // PACKED)]
        b_s = kept("b_s", [P, F * N + 4], U8)
        g1 = [kept("g10", [P, C], F32), kept("g11", [P, T - C], F32)]
        g2 = kept("g2", [P, T], F32)
        one = kept("one", [P, 1], F32)

        zero = kept("zero", [P, 1], F32)

        nc.gpsimd.memset(ws[:, :SPLIT].bitcast(I32), 0)
        nc.vector.memset(ws[:, SPLIT:].bitcast(I32), 0)
        nc.gpsimd.memset(xs[:, :T].bitcast(I32), 0)
        nc.vector.memset(zero[:], 0.0)
        nc.scalar.activation(out=one[:], in_=zero[:], func=ACT.Relu, bias=1.0)
        for scale_tile in a_s:
            nc.gpsimd.memset(scale_tile[:].bitcast(I32), 0)
        ident = kept("ident", [P, P], F32)
        make_identity(nc, ident[:])
        nc.vector.memset(b_s[:].bitcast(I32), 0)

        def entries(offsets, first, end):
            return offsets[:, first // 16 : end // 16]

        def gather(name, window, dtype, offsets, tag=None):
            picked = kept(name, [P, 16 * offsets.shape[1]], dtype, tag)
            nc.vector.tensor_copy(picked[:], window.indirect(offsets))
            return picked

        def load_scales(scale_tile, row, scales):
            matrices, width = scales.shape[0], scales.shape[3]
            for q in range(QUADS):
                rows = scale_tile[32 * q + row : 32 * q + row + 4, : matrices * width]
                nc.sync.dma_start(
                    out=rows.rearrange("r (f n) -> r f n", n=width).bitcast(I32),
                    in_=scales[:, 0, 4 * q : 4 * q + 4, :].rearrange("f r n -> r f n").bitcast(I32),
                )

        def load_packed_scales(scale_tile, scales, group):
            for q in range(QUADS):
                nc.sync.dma_start(
                    out=scale_tile[32 * q : 32 * q + 4 * PACKED, :].bitcast(I32),
                    in_=scales[PACKED * group : PACKED * (group + 1), 0, 4 * q : 4 * q + 4, :].bitcast(I32),
                )

        def load_words(word_tile, words, first):
            matrices = words[first : first + word_tile.shape[1], 0]
            nc.sync.dma_start(out=word_tile[:], in_=matrices.rearrange("f p n d -> p f (n d)").bitcast(I32))

        x_word_window = xw[:].bitcast(U32)
        for h in range(2):
            nc.sync.dma_start(
                out=folded[64 * h : 64 * h + 4].bitcast(I32),
                in_=x_scales[0, 8 * h : 8 * h + 8, :].rearrange("(q r) n -> r q n", q=2).bitcast(I32),
            )
        for h in range(2):
            for q in range(2):
                first = 64 * h + 32 * q
                nc.vector.tensor_copy(
                    xs[first : first + 4, :T].bitcast(I32), folded[64 * h : 64 * h + 4, q, :].bitcast(I32)
                )
        nc.sync.dma_start(list1[:], offs)
        nc.sync.dma_start(list2[:], offs2)
        nc.sync.dma_start(out=xw[:, :T], in_=x_words[0].rearrange("p t d -> p (t d)").bitcast(I32))
        nc.sync.dma_start(out=ww[0][:, 0, :].bitcast(I32), in_=w_words[0, 0].bitcast(I32))
        nc.sync.dma_start(out=g1[0][:], in_=gate[:, :C])
        load_scales(ws, 0, w_scales)
        load_words(aw[1], wa_words, 2)
        load_words(aw[0], wa_words, 0)
        load_packed_scales(a_s[0], wa_scales, 0)
        for pair in (2, 3):
            load_words(aw[pair], wa_words, 2 * pair)
        load_packed_scales(a_s[1], wa_scales, 1)
        nc.sync.dma_start(out=ww[1][:].bitcast(I32), in_=w_words[1:, 0].rearrange("e p b -> p e b").bitcast(I32))
        nc.sync.dma_start(out=g1[1][:], in_=gate[:, C:])
        load_scales(b_s, B_ROW, wb_scales)
        for half in range(2):
            load_words(bw[half], wb_words, PACKED * half)
        for half in range(2):
            cols = slice(BANK * half, BANK * (half + 1))
            nc.sync.dma_start(out=g2[:, cols], in_=gate2[:, cols])

        ys = kept("ys", [P, 4, T], F32)
        zs = [kept("zs%d" % j, [P, T], F32) for j in range(4)]

        def expert(e, tiles, words, scales, number):
            acc = bank("y%d%d" % (e, tiles[0]), [P, len(tiles), C], number)
            part = min(e, 1)
            for u, j in enumerate(tiles):
                nc.tensor.matmul_mx(
                    out=acc[:, u, :],
                    lhsT=ww[part][:, e - part, 2 * P * j : 2 * P * (j + 1)].bitcast(FP4X4),
                    lhsT_scale=ws[:, N * e + P * j : N * e + P * (j + 1)],
                    rhs=words.bitcast(FP8X4),
                    rhs_scale=scales,
                    start=True,
                    stop=True,
                )
            return acc

        def gate_expert(e, tiles, acc):
            part = min(e, 1)
            weights = g1[part][:, C * (e - part) : C * (e - part + 1)].unsqueeze(1).to_broadcast([P, len(tiles), C])
            result = ys[:, tiles[0] : tiles[-1] + 1, C * e : C * (e + 1)]
            nc.vector.tensor_tensor(result, acc[:], weights, ALU.mult)

        def vector_scatter(window, offsets, values, first, end):
            nc.vector.tensor_copy(window[:].indirect(entries(offsets, first, end)), values[:, first:end])

        def scalar_scatter(window, offsets, values, first, end):
            nc.scalar.activation(
                out=window[:].indirect(entries(offsets, first, end)),
                in_=values[:, first:end],
                func=ACT.Copy,
                scale=one[:],
            )

        oy = [kept("oy%d" % j, [P, WIDE], F32) for j in range(2)]

        scales0 = gather("e_scales0", xs[:], U8, entries(list1, 0, C))
        words0 = gather("e_words0", x_word_window, U32, entries(list1, 0, C))
        a_words = [gather("a_words0", x_word_window, U32, entries(list2, 0, FILL * D))]
        for number, tiles in enumerate(((0,), (1, 2))):
            gate_expert(0, tiles, expert(0, tiles, words0[:], scales0[:], number))
        last_of_first = expert(0, (3,), words0[:], scales0[:], 2)
        for j in range(2):
            scalar_scatter(oy[j], list1, ys[:, j, :], 0, C)

        a_scales = kept("a_scales", [P, T], U8, tag="e_scales0")
        nc.vector.tensor_copy(a_scales[:, : 2 * D], xs[:].indirect(entries(list2, 0, 2 * D)))
        gate_expert(0, (3,), last_of_first)
        a_words.append(gather("a_words1", x_word_window, U32, entries(list2, FILL * D, T), tag="e_words0"))
        nc.vector.tensor_copy(a_scales[:, 2 * D :], xs[:].indirect(entries(list2, 2 * D, T)))
        late_scales = kept("late_scales", [P, T - C], U8, tag="g10")
        scales1, scales2 = late_scales[:, :C], late_scales[:, C:]
        nc.vector.tensor_copy(scales1, xs[:].indirect(entries(list1, C, BANK)))
        words1 = gather("e_words1", x_word_window, U32, entries(list1, C, T), tag="ww0")

        def tokens(f):
            part = 0 if f < FILL else 1
            first = D * (f - part * FILL)
            return a_words[part][:, first : first + D].bitcast(FP8X4)

        squares = {}
        hb = [kept("hb%d" % half, [P, BANK, 4], BF16) for half in range(2)]
        reordered = []

        def reorder(u, buffer):
            reordered.append(kept("reordered%d" % u, [P, 4, P], I32, tag=buffer))
            nc.gpsimd.tensor_copy(reordered[u][:], aw[1][:, u, :].rearrange("p (m t) -> p t m", t=4))

        reorder(0, None)
        reordered_scales = kept("reordered_scales", [P, 4, P], U8)
        nc.gpsimd.tensor_copy(reordered_scales[:], a_s[0][:].rearrange("p (m t) -> p t m", t=4))

        def first_layer(f, number):
            acc = bank("h%d" % f, [P, H], number)
            nc.tensor.matmul_mx(
                out=acc[:],
                lhsT=tokens(f),
                lhsT_scale=a_scales[:, D * f : D * (f + 1)],
                rhs=aw[f // 2][:, f % 2, :].bitcast(FP8X4),
                rhs_scale=a_s[f // PACKED][4 * (f % PACKED) :, :],
                start=True,
                stop=True,
            )
            pos = kept("pos%d" % f, [P, H], F32)
            nc.scalar.activation(out=pos[:], in_=acc[:], func=ACT.Relu)
            squares.setdefault(f, kept("squared%d" % f, [P, H], BF16))
            nc.gpsimd.tensor_tensor(squares[f][:], pos[:], pos[:], ALU.mult)

        def first_layer_reordered(f, number):
            acc = bank("h%d" % f, [P, 4, D], number)
            for t in range(4):
                nc.tensor.matmul_mx(
                    out=acc[:, t, :],
                    lhsT=reordered[f % 2][:, t, :].bitcast(FP8X4),
                    lhsT_scale=reordered_scales[4 * f :, t, :],
                    rhs=tokens(f),
                    rhs_scale=a_scales[:, D * f : D * (f + 1)],
                    start=True,
                    stop=True,
                )
            pos = kept("pos%d" % f, [P, D, 4], F32)
            nc.scalar.activation(out=pos[:], in_=acc[:].rearrange("p t s -> p s t"), func=ACT.Relu)
            nc.gpsimd.tensor_tensor(hb[0][:, D * f : D * (f + 1), :], pos[:], pos[:], ALU.mult)

        for f, number in zip((0, 1, 4, 5, 6, 7), (4, 5, 6, 7, 0, 1)):
            first_layer(f, number)
            if f == 1:
                reorder(1, "a_s0")
        for f, number in zip((2, 3), (4, 5)):
            first_layer_reordered(f, number)
        oy.append(kept("oy2", [P, T], F32, tag="aw0"))
        scalar_scatter(oy[2], list1, ys[:, 2, :], 0, C)
        pairs = ((0, 1), (2, 3))
        second = [expert(1, tiles, words1[:, :C], scales1, number) for tiles, number in zip(pairs, (3, 2))]
        nc.vector.tensor_copy(scales2, xs[:].indirect(entries(list1, BANK, T)))
        gate_expert(1, pairs[0], second[0])
        gate_expert(1, pairs[1], second[1])
        for j in range(2):
            scalar_scatter(oy[j], list1, ys[:, j, :], C, 2 * C)

        def last_two_experts(j, number):
            acc = bank("y_late%d" % j, [P, BANK], number)
            for u in range(2):
                e = 2 + u
                nc.tensor.matmul_mx(
                    out=acc[:, C * u : C * (u + 1)],
                    lhsT=ww[1][:, e - 1, 2 * P * j : 2 * P * (j + 1)].bitcast(FP4X4),
                    lhsT_scale=ws[:, N * e + P * j : N * e + P * (j + 1)],
                    rhs=words1[:, C * (e - 1) : C * e].bitcast(FP8X4),
                    rhs_scale=scales2[:, C * u : C * (u + 1)],
                    start=True,
                    stop=True,
                )
            nc.vector.tensor_tensor(ys[:, j, BANK:], acc[:], g1[1][:, C:], ALU.mult)

        for j, number in ((2, 6), (0, 7), (1, 3)):
            last_two_experts(j, number)
        for j in range(2):
            scalar_scatter(oy[j], list1, ys[:, j, :], BANK, T)
        vector_scatter(oy[2], list1, ys[:, 2, :], CUT, T)
        scalar_scatter(oy[2], list1, ys[:, 2, :], C, CUT)

        def turn(pair, number):
            turned = bank("turned%d" % pair, [P, 2, 2, D], number)
            for a in range(2):
                for u in range(2):
                    nc.tensor.transpose(turned[:, a, u, :], squares[2 * pair + a][:].bitcast(F32)[:, u::2], ident[:])
            slots = hb[pair // 2][:, 2 * D * (pair % 2) : 2 * D * (pair % 2 + 1), :].bitcast(F32).rearrange("p (a s) u -> p a s u", a=2)
            nc.vector.tensor_copy(slots, turned[:].rearrange("p a u s -> p a s u"))

        hw, hs = [], []

        def quantize(half, buffer):
            hw.append(kept("hw%d" % half, [P, BANK], U32, tag=buffer))
            hs.append(kept("hs%d" % half, [P, BANK], U8))
            values = hb[half][:].rearrange("p s t -> p (s t)")
            nc.vector.quantize_mx(out=hw[half][:].bitcast(FP8X4), scales=hs[half][:], in_=values)

        for pair, number in ((0, 2), (2, 6)):
            turn(pair, number)
        quantize(0, None)
        turn(3, 3)
        last_two_experts(3, 7)
        quantize(1, None)

        def second_layer(j, half):
            acc = bank("z%d%d" % (j, half), [P, BANK], ((0, 1, 4, 5), (6, 7, 3, 2))[half][j])
            for u in range(PACKED):
                first = N * (PACKED * half + u) + P * j
                nc.tensor.matmul_mx(
                    out=acc[:, D * u : D * (u + 1)],
                    lhsT=bw[half][:, u, P * j : P * (j + 1)].bitcast(FP8X4),
                    lhsT_scale=b_s[B_ROW:, first : first + P],
                    rhs=hw[half][:, D * u : D * (u + 1)].bitcast(FP8X4),
                    rhs_scale=hs[half][:, D * u : D * (u + 1)],
                    start=True,
                    stop=True,
                )
            cols = slice(BANK * half, BANK * (half + 1))
            nc.vector.tensor_tensor(zs[j][:, cols], acc[:], g2[:, cols], ALU.mult)

        oz = [kept("oz%d" % j, [P, WINDOW if j == 2 else WIDE], F32) for j in range(4)]
        for j in range(4):
            for half in range(2):
                second_layer(j, half)
            if j == 1:
                vector_scatter(oz[1], list2, zs[1], 0, SHARE)
        for half in range(2):
            scalar_scatter(oz[0], list2, zs[0], BANK * half, BANK * (half + 1))
        scalar_scatter(oz[1], list2, zs[1], SHARE, T)
        vector_scatter(oz[2], list2, zs[2], 0, T)
        scalar_scatter(oz[3], list2, zs[3], 0, T)
        oy.append(kept("oy3", [P, WINDOW], F32, tag="hw1"))
        vector_scatter(oy[3], list1, ys[:, 3, :], 0, T)

        for j, buffer in ((0, None), (2, "oz0"), (1, "oz2")):
            res = kept("res%d" % j, [P, T], F32, tag=buffer)
            nc.gpsimd.tensor_tensor(res[:], oy[j][:, :T], oz[j][:, :T], ALU.add)
            nc.sync.dma_start(out=out[P * j : P * (j + 1), :], in_=res[:])

        last = kept("last", [P, T], F32, tag="oz1")
        for c in range(0, T, PIECE):
            cols = slice(c, c + PIECE)
            nc.vector.tensor_tensor(last[:, cols], oy[3][:, cols], oz[3][:, cols], ALU.add)
            nc.sync.dma_start(out=out[3 * P : 4 * P, cols], in_=last[:, cols])
